import numpy as np, ml_dtypes
CORES = [13,21,141,149]
N = 4
BF = ml_dtypes.bfloat16
def gentries(a):
    return np.ascontiguousarray(a.reshape(8, 16, -1).transpose(0, 2, 1)).reshape(8, -1)
def gtable(e):
    e = np.asarray(e); return np.ascontiguousarray(e.reshape(8, -1, 16).transpose(0, 2, 1)).reshape(128, -1).astype(np.int32)
V, G, P, E, O, RO, ST = 1024, 512, 1024, 112, 48, 4, 2
W = V + (N - 1) * G; L = E + (N - 1) * O
def power(rng, *shape):
    lead = rng.integers(0, 16, shape[:-2] + (1,) + shape[-1:])
    return np.where(np.arange(16)[:, None] == lead, rng.integers(128, 256, shape), rng.integers(0, 40, shape))
def parts(rng):
    x = power(rng, N, 8, 16, V); plans = power(rng, 8, 16, P)
    share = 0.3 + 0.3 * rng.random((N, 8, 1, 1))
    nb = np.where(rng.random((N, 8, 16, V)) < share, rng.integers(V, W, (N, 8, 16, V)), rng.integers(0, V, (N, 8, 16, V)))
    pt = 2048 * rng.integers(0, 1024, (N, 8, 16, V)) + rng.integers(0, P, (N, 8, 16, V))
    req = np.ascontiguousarray(np.argsort(rng.random((N, 8, RO, V)), axis=-1)[..., :E])
    th = rng.integers(180, 281, (N, 8, 16, 1))
    return x, nb, pt, plans, req, th
def pack(x, nb, pt, plans, req, th):
    return {"x": np.ascontiguousarray(x.reshape(N, 128, V)).astype(np.float32).astype(BF), "nb": np.ascontiguousarray(nb.reshape(N, 128, V)).astype(np.int32),
            "pt": np.ascontiguousarray(pt.reshape(N, 128, V)).astype(np.int32), "plans": np.repeat(plans.reshape(1, 128, P), N, axis=0).astype(np.float32).astype(BF),
            "req": np.stack([gtable(a.reshape(8, RO * E)) for a in req]), "th": np.ascontiguousarray(th.reshape(N, 128, 1)).astype(np.int32)}
def setup_inputs(rng):
    return pack(*parts(rng))
def setup_inputs_room(rng):
    x, nb, pt, plans, req, th = parts(rng); x = np.maximum(x, 1); plans = np.maximum(plans, 1); th = th * 0
    for q in range(N):
        for g in range(8):
            o = rng.permutation(V)[:E]; req[q, g, 0] = o
            n = [int(a) for a in rng.choice(np.array([0, 1, O - 1, O, O + 1]), N - 1)]
            if q == 0: n[0] = (O, O + 1, O - 1, 0, 1, O, O + 1, E)[g]
            left = E; goals = []
            for d in range(N - 1):
                m = min(n[d], left); left -= m
                goals.append(V + d * G + rng.integers(0, G, m))
            goals.append(o[rng.integers(0, E, left)])
            nb[q, g][:, o] = rng.permutation(np.concatenate(goals))[None, :]
    return pack(x, nb, pt, plans, req, th)
def setup_inputs_ties(rng):
    x, nb, pt, plans, req, th = parts(rng)
    x = rng.integers(0, 4, x.shape); plans = rng.integers(0, 4, plans.shape); th = rng.integers(12, 19, th.shape)
    pt = 2048 * rng.integers(0, 4, pt.shape) + rng.integers(0, P, pt.shape)
    x[:, 0] = 5; x[:, 1] = 5; th[:, 0] = 80; th[:, 1] = 79; pt[:, :2] = pt[:, :2] & 2047
    x[:, 2, ::2] = 0; th[:, 2, ::2] = 0
    return pack(x, nb, pt, plans, req, th)
def setup_inputs_alike(rng):
    x, nb, pt, plans, req, th = parts(rng); s = np.arange(V)
    req[:, 0] = req[:, 0, :1]
    req[:, 3] = rng.integers(0, 40, (N, RO, E))
    req[:, 5] = rng.choice(np.array([0, V - 1, 1, V >> 1]), (N, RO, E))
    req[:, 7] = np.where(rng.random((N, RO, E)) < 0.5, req[:, 7, :, :1], req[:, 7])
    nb[:, 2] = np.where(rng.random((N, 16, V)) < 0.5, s, nb[:, 2])
    nb[:, 4] = rng.choice(np.array([0, V - 1, V, V + G - 1, W - 1]), (N, 16, V))
    nb[:, 6] = nb[:, 6, :1]
    nb[:, 1, 8:] = nb[:, 1, :8]
    return pack(x, nb, pt, plans, req, th)
def wire(rng, x, nb, plans, th, g, nxt):
    strong = np.zeros((N, V), bool)
    for q in range(N):
        t = nxt[q][nxt[q] >= 0]; strong[q, t[t < V]] = True
        e = t[t >= V] - V; strong[(q - 1 - e // G) % N, e % G] = True
    x[:, g] = np.where(strong[:, None, :], rng.integers(200, 256, (N, 16, V)), rng.integers(0, 8, (N, 16, V)))
    plans[g] = rng.integers(0, 8, (16, P)); th[:, g] = rng.integers(112, 200, (N, 16, 1))
    for q in range(N):
        seen = np.concatenate([strong[q]] + [strong[(q - d) % N, :G] for d in range(1, N)]); calm = np.nonzero(~seen)[0]
        nb[q, g] = calm[rng.integers(0, len(calm), (16, V))]
        s = np.nonzero(nxt[q] >= 0)[0]; nb[q, g][rng.integers(0, 16, len(s)), s] = nxt[q, s]
def ordered(rng, nxt, pt, req, g, a, goals, ban):
    for d in range(1, N):
        q = (a + d) % N; o = rng.permutation(V); s = o[:O]
        nxt[q, s] = V + (d - 1) * G + goals[d - 1]
        cost = np.where(np.arange(16)[:, None] == ban[d - 1][None, :], 0, rng.integers(500, 1024, (16, O)))
        pt[q, g][:, s] = 2048 * cost + (pt[q, g][:, s] & 2047)
        req[q, g, 0] = rng.permutation(o[:E]); req[q, g, 1:] = rng.choice(o[O:], (RO - 1, E))
def setup_inputs_hubs(rng):
    x, nb, pt, plans, req, th = parts(rng)
    for q in range(N):
        for g in range(8):
            own = np.concatenate([rng.permutation(G)[:3], rng.permutation(V)[:3]])
            x[q, g][:, own] = 255 - rng.integers(0, 3, (16, 6))
            goals = np.concatenate([own, V + rng.integers(0, (N - 1) * G, 2)])
            nb[q, g] = np.where(rng.random((16, V)) < 0.08, rng.choice(goals, (16, V)), nb[q, g])
    n = (N - 1) * O
    for g in (4, 5, 6):
        a = int(rng.integers(0, N)); nxt = np.full((N, V), -1, np.int64)
        goals = np.concatenate([np.zeros(1, np.int64), 1 + rng.permutation(G - 1)[:n - 1]]); ban = rng.integers(0, 16, n); ban[0] = 0
        o = rng.permutation(np.setdiff1d(np.arange(V), goals))
        ordered(rng, nxt, pt, req, g, a, goals.reshape(N - 1, O), ban.reshape(N - 1, O))
        if g == 4:
            m = 2 * E * ST; c = o[:m].reshape(2 * E, ST); nxt[a, c[:, :-1]] = c[:, 1:]
            e = np.concatenate([goals[:, None], o[m:m + n * (ST - 1)].reshape(n, ST - 1)], axis=1); nxt[a, e[:, :-1]] = e[:, 1:]
            req[a, g] = rng.choice(o[m + n * (ST - 1):], (RO, E)); req[a, g, 0] = c[:E, 0]; req[a, g, 1] = c[E:, 0]
        elif g == 5:
            hub = o[:RO]; block = o[RO:RO + (RO - 1) * E].reshape(RO - 1, E)
            nxt[a, block] = hub[:RO - 1, None]; nxt[a, goals] = hub[1]
            req[a, g, :RO - 1] = block; req[a, g, RO - 1] = rng.permutation(np.concatenate([goals, block[-1]]))[:E]
        else:
            b = o[:n]; nxt[a, goals] = b; nxt[a, b] = goals
            c = o[n:n + E]; e = o[n + E:n + 2 * E]; nxt[a, c] = e; nxt[a, e] = c
            req[a, g] = rng.choice(o[n + 2 * E:], (RO, E)); req[a, g, 0] = c
        wire(rng, x, nb, plans, th, g, nxt)
        if g == 6:
            x[a, g][ban, b] = rng.integers(0, 8, n)
            cost = np.where(np.arange(16)[:, None] == ban[None, :], 1023, rng.integers(0, 301, (16, n)))
            pt[a, g][:, b] = 2048 * cost + (pt[a, g][:, b] & 2047)
    return pack(x, nb, pt, plans, req, th)
def setup_inputs_spread(rng):
    x, nb, pt, plans, req, th = parts(rng)
    x = np.minimum((np.exp2(8 * rng.random((N, 8, 1, V))) * rng.random((N, 8, 16, V))).astype(np.int64), 255)
    plans = np.minimum((np.exp2(8 * rng.random((8, 1, P))) * rng.random((8, 16, P))).astype(np.int64), 255)
    x[..., 0] = 255; x[..., V - 1] = 255
    cost = np.minimum(np.exp2(10 * rng.random(pt.shape)).astype(np.int64) - 1, 1023)
    pt = 2048 * cost + rng.integers(0, P, pt.shape); pt[..., 0] = 2048 * 1023 + P - 1
    th = (np.exp2(5 + 5 * rng.random((N, 8, 1, 1))) * (0.5 + rng.random((N, 8, 16, 1)))).astype(np.int64)
    th[:, 0] = rng.integers(0, 4081, (N, 16, 1))
    for g, n, lo, t0, t1, u0, u1, k0, k1 in ((5, 8, 200, 3900, 4080, 0, 12, 500, 200), (6, 15, 240, 3000, 3700, 22, 26, 900, 300), (7, 16, 240, 3930, 3990, 0, 0, 500, 0)):
        heavy = rng.permutation(16)[:, None] < n
        x[:, g] = np.where(heavy, rng.integers(lo, 256, (N, 16, V)), rng.integers(0, 4, (N, 16, V)))
        plans[g] = np.where(heavy, rng.integers(lo, 256, (16, P)), rng.integers(0, 4, (16, P)))
        th[:, g] = np.where(heavy, rng.integers(t0, t1 + 1, (N, 16, 1)), rng.integers(u0, u1 + 1, (N, 16, 1)))
        cost = np.where(heavy, rng.integers(k0, 1024, (N, 16, V)), rng.integers(0, k1 + 1, (N, 16, V)))
        pt[:, g] = 2048 * cost + (pt[:, g] & 2047)
    return pack(x, nb, pt, plans, req, th)
def check_inputs(d):
    bad = []
    for k in ("x", "plans"):
        v = np.asarray(d[k]).astype(np.float32)
        if not (np.min(v) >= 0 and np.max(v) <= 255 and np.all(v == np.floor(v))): bad.append("range of " + k)
    for k, hi in (("nb", W - 1), ("pt", 2048 * 1023 + 2047), ("req", V - 1), ("th", 4080)):
        if not (np.min(d[k]) >= 0 and np.max(d[k]) <= hi): bad.append("range of " + k)
    if np.max(np.asarray(d["pt"]).astype(np.int64) & 2047) >= P: bad.append("plan numbers in pt")
    v = np.asarray(d["plans"]).astype(np.float32)
    if not np.all(v == v[:1]): bad.append("plans alike on all ranks")
    return bad
def chains(w, nbg, ptg, tg, frozen, first, ban):
    lanes = np.arange(L); ch = np.arange(16)[:, None]; mark = np.array(frozen)
    got = np.zeros((ST, L), bool); where = np.zeros((ST, L), np.int64); plan = np.zeros((ST, L), np.int64)
    good = np.zeros(L, bool); order = np.full(L, -1, np.int64); live = first >= 0; s = first
    for k in range(ST):
        at = np.where(live, s, 0)
        idx = np.nonzero(live & ~mark[at])[0]
        u, j = np.unique(at[idx], return_index=True)
        reach = np.zeros(L, bool); reach[idx[j]] = True; mark[u] = True
        q = nbg[:, at]
        p = w[:, q]
        total = np.add.reduce(p, axis=1); over = total > tg
        price = total + (ptg[:, at] >> 11) + 4096 * over + 16384 * (ch == ban[None, :])
        c = np.argmin(price, axis=0)
        got[k] = reach; where[k] = at; plan[k] = ptg[c, at] & 2047
        stuck = over[c, lanes]
        b = q[np.argmax(p[c, :, lanes], axis=1), lanes]
        good = good | (reach & ~stuck)
        order = np.where(reach & stuck & (b >= V), (b - V) * 16 + c, order)
        live = reach & stuck & (b < V); s = b; ban = c
    return got, where, plan, good, order
def reference(x, nb, pt, plans, req, th):
    now = x.astype(np.float32).astype(np.int64).reshape(N, 8, 16, V); nbl = nb.astype(np.int64).reshape(N, 8, 16, V); ptl = pt.astype(np.int64).reshape(N, 8, 16, V)
    pl = plans.astype(np.float32).astype(np.int64).reshape(N, 8, 16, P); t = th.astype(np.int64).reshape(N, 8, 16, 1)
    rq = np.stack([gentries(a) for a in req]).astype(np.int64).reshape(N, 8, RO, E)
    frozen = np.zeros((N, 8, V), bool); inbox = np.full((N, 8, N - 1, O), -1, np.int64)
    for rnd in range(RO):
        new = np.array(now); nextbox = np.full((N, 8, N - 1, O), -1, np.int64)
        for r in range(N):
            w = np.concatenate([now[r]] + [now[(r - d) % N][:, :, :G] for d in range(1, N)], axis=2)
            for g in range(8):
                box = inbox[r, g].reshape(-1)
                first = np.concatenate([rq[r, g, rnd], np.where(box >= 0, box >> 4, -1)])
                ban = np.concatenate([np.full(E, -1, np.int64), np.where(box >= 0, box & 15, -1)])
                got, where, plan, good, order = chains(w[g], nbl[r, g], ptl[r, g], t[r, g], frozen[r, g], first, ban)
                for d in range(1, N):
                    i = np.nonzero((order >= (d - 1) * 16 * G) & (order < d * 16 * G))[0][:O]
                    good[i] = True; nextbox[(r - d) % N, g, d - 1, :len(i)] = order[i] - (d - 1) * 16 * G
                for k in range(ST):
                    m = got[k] & good
                    new[r, g][:, where[k][m]] = pl[r, g][:, plan[k][m]]
                frozen[r, g][where[0][got[0] & ~good]] = True
        now = new; inbox = nextbox
    return {"y": now.reshape(N, 128, V).astype(np.float32).astype(BF)}

@@ -1,0 +1,634 @@
+import math
+from concourse.bass import DstId, RemoteDMATransfer
+from concourse.mybir import AluOpType as A, ActivationFunctionType as F
+
+V, GH, RO = 1024, 512, 4
+BIG = 2.0 ** 94
+LNB = math.log(1.75)
+LN0 = 90 * math.log(2.0)
+ONV = {(4, 0): (0,), (4, 1): (3,), (8, 0): (0, 3, 6), (8, 1): (2, 5)}
+CUT = 24
+
+
+def _sb(n, d="float32"):
+    return ("sbuf", [128] + (n if isinstance(n, list) else [n]), d)
+
+
+H, I32, U16, F16 = "bfloat16", "int32", "uint16", "float16"
+SCRATCH = {
+    "W": _sb(2560, H), "S0": _sb(2064, H), "S1": _sb(1552, H), "S2": _sb(1552, H), "S3": _sb(1552, H),
+    "nbi": _sb(V + 16, I32), "pti": _sb(V, I32), "pli": _sb(V + 16, I32), "cst": _sb(V + 16),
+    "rq": _sb(28, I32), "rqb": _sb(28, I32), "thi": _sb(4, I32), "col": _sb(16), "coli": _sb(4, I32),
+    "row": _sb(144), "rowg": _sb(128), "rowj": _sb(128), "Rc": _sb(512, H),
+    "idb": _sb(128, H), "id12": _sb(128, H), "id8": _sb(128, H), "idB": _sb(128, H), "idm": _sb(128, H), "id32": _sb(128),
+    "BOc": _sb(128, H), "Cm": _sb(128, F16), "BN": _sb(256, H), "tn": _sb(32, H), "cb": _sb(16, U16),
+    "BO": _sb(128, H), "nBO": _sb(128, H), "tri": _sb(128, H), "EE": _sb(144, H), "SWs": _sb([4, 128], H), "SWb": _sb([4, 128], H),
+    "ta": _sb(1040, H), "tb": _sb(160, H), "tba": _sb(64), "tbb": _sb(64), "tcf": _sb(320), "tc": _sb(320, H), "bci": _sb(32, I32), "bc": _sb(32, U16),
+    "rep": _sb(4, U16), "dc": _sb(48), "r3": _sb(48),
+    "rmin": _sb(256), "rmax": _sb(256), "rrk": _sb(48, H), "offc": _sb(16, I32), "wi": _sb(32), "wcol": _sb(2), "thr": _sb(16),
+    "mp": _sb(64), "mpa": _sb(64), "kp": _sb(64), "mp16": _sb(64, U16), "FZ": _sb(64, H), "fz1": _sb(64, H), "MK": _sb(64, H), "Ms": _sb(160, H),
+    "AW": _sb([128, 16], H), "AF": _sb([256, 16], F16),
+    "L0": _sb(48, U16), "s1": _sb(16, U16), "b1": _sb(16, U16), "c0": _sb(16, U16), "c1": _sb(16, U16), "oi": _sb(16, I32),
+    "Q": _sb(256, U16), "Qf": _sb(256, F16), "CK": _sb(256), "TH": _sb(256), "BAN": _sb(256, H),
+    "OH0": _sb(256, H), "OH1": _sb(256, H), "G": _sb(4096, H), "GT": _sb(4096, H),
+    "ov": _sb(256), "kR": _sb([8, 2, 16]), "kT": _sb(256), "km": _sb(256), "ki": _sb(16, I32), "ci": _sb(16, I32), "off": _sb(16, U16),
+    "hh": _sb(16, I32), "ht": _sb(16), "CS": _sb(32, H), "K1": _sb(256, H), "K1T": _sb(256), "bm": _sb(256), "bi": _sb(16, I32), "si": _sb(16, I32),
+    "AR0": _sb(256, H), "AR1": _sb(256, H), "FB": _sb(256, H), "B0": _sb(1024, H), "B1": _sb(1024, H), "LK": _sb(256, H), "PL": _sb(256, F16),
+    "z": _sb([32, 16]), "zi": _sb([5, 16], I32), "dI": _sb(16, I32), "ff": _sb(48, H), "inc": _sb(48, H), "fr": _sb(48), "WW": _sb(32), "XI": _sb(16, I32), "SL": _sb(16, U16),
+    "D": _sb(512, F16), "DX": _sb(256, F16), "AO": _sb(512, H), "X": _sb(512, F16),
+    "MSG": _sb([3, 64], U16), "IN": _sb([9, 72], U16), "HB": _sb(128, H), "HM": _sb([3, 64], U16),
+}
+for _p in ("pX", "pA", "pB0", "pB1", "pM", "pT"):
+    SCRATCH[_p] = ("psum", [128, 512], "float32")
+for _p in ("pQ", "pS"):
+    SCRATCH[_p] = ("psum", [128, 16, 2, 16], "float32")
+SEMAPHORES = (["cV", "cS", "cP", "cG", "l0", "ls", "hx", "hm0", "hm1", "hm2", "xg1", "xg2", "xg3"] + ["m%d" % k for k in range(9)] + ["d%d" % k for k in range(24)])
+
+
+def bits(es):
+    m = 0
+    for e in es:
+        m |= 1 << e
+    return m
+
+
+def ways(T, topo, r):
+    me = T.cores[r]
+    n = len(T.cores)
+    near = [q for q in range(n) if q != r and topo.may_write(me, T.cores[q])]
+    far = [q for q in range(n) if q != r and q not in near]
+    hands = [c for c in topo.cores_of(me) if T.rank_of(c) is None and all(topo.may_write(c, T.cores[q]) for q in far)]
+    close = sorted(hands, key=lambda c: topo.die(c) != topo.die(me))[:len(far)]
+    return near, far, hands, close
+
+
+def send(g, T, topo, me, items, sem_here):
+    trs = []
+    for dst, es, sem, src, out in items:
+        rid, pid = topo.addr(dst, me)
+        trs.append(RemoteDMATransfer(dst_ids=[DstId(rid=rid, pnc=pid)], dma_engine_mask=bits(es), remote_sem=T.sem[sem], srcs=[src], dsts=[out]))
+    g.remote_dma_fused(trs, local_sem=T.sem[sem_here])
+    return sum(len(it[1]) for it in items)
+
+
+def helper(g, core, T, topo):
+    own = [c for c in topo.cores_of(core) if T.rank_of(c) is not None]
+    if not own:
+        return
+    r = T.rank_of(own[0])
+    n = len(T.cores)
+    near, far, hands, close = ways(T, topo, r)
+    if core not in hands:
+        return
+    k = hands.index(core)
+    wd = GH // len(hands)
+    es = topo.engines(core, T.cores[far[0]])
+    per = len(es) // len(far)
+    g.wait_ge(T.sem.hx, len(topo.engines(own[0], core)) // len(hands))
+    items = []
+    for i, q in enumerate(far):
+        d = (q - r) % n
+        a = V + (d - 1) * GH + k * wd
+        items.append((T.cores[q], es[i * per:(i + 1) * per], "xg%d" % d, T.HB[:, 0:wd], T.W[:, a:a + wd]))
+    ls = send(g, T, topo, core, items, "ls")
+    if core in close:
+        q = far[close.index(core)]
+        d = (r - q) % n
+        left = len(topo.engines(own[0], core)) - len(topo.engines(own[0], T.cores[near[0]]))
+        for t in range(RO - 1):
+            g.wait_ge(T.sem["hm%d" % t], left // len(far))
+            j = 3 * t + d - 1
+            ls += send(g, T, topo, core, [(T.cores[q], es, "m%d" % j, T.HM[:, t, :], T.IN[:, j, 12 - 4 * d:76 - 4 * d])], "ls")
+    g.wait_ge(T.sem.ls, ls)
+
+
+def rank_program(g, core, T, topo):
+    rank = T.rank_of(core)
+    if rank is None:
+        helper(g, core, T, topo)
+        return
+    N = len(T.cores)
+    near, far, hands, close = ways(T, topo, rank)
+    eng = {"V": g.vector, "S": g.scalar, "P": g.tensor, "G": g, "Y": g.sync}
+    cnt, seen, lastw, reads, nd, ls = {}, {}, {}, {}, [0], [0]
+
+    def deps(e, R, Wr):
+        need = {}
+
+        def want(x):
+            if x[1] > need.get(x[0], 0):
+                need[x[0]] = x[1]
+        for k in R:
+            if k in lastw:
+                want(lastw[k])
+            if k[0] == "p" and k[1].isupper():
+                for x in reads.get(k, {}).values():
+                    if x[2] != e:
+                        want(x)
+        for k in Wr:
+            if k in lastw and not (e == "P" and lastw[k][2] == "P"):
+                want(lastw[k])
+            for x in reads.get(k, {}).values():
+                want(x)
+        for s, v in need.items():
+            if seen.get((e, s), 0) < v:
+                eng[e].wait_ge(T.sem[s], v)
+                seen[(e, s)] = v
+
+    def note(e, s, R, Wr):
+        x = (s, cnt[s], e)
+        for k in R:
+            reads.setdefault(k, {})[s] = x
+        for k in Wr:
+            lastw[k] = x
+            reads[k] = {}
+
+    def op(e, fn, R, Wr):
+        R, Wr = R.split(), Wr.split()
+        deps(e, R, Wr)
+        s = "c" + e
+        out = fn(eng[e])
+        for ins in (out if isinstance(out, list) else [out]):
+            ins.then_inc(T.sem[s], 1)
+            cnt[s] = cnt.get(s, 0) + 1
+        note(e, s, R, Wr)
+
+    def dma(e, out, in_, R, Wr):
+        R, Wr = R.split(), Wr.split()
+        deps(e, R, Wr)
+        s = "d%d" % nd[0]
+        nd[0] += 1
+        eng[e].dma_start(out, in_).then_inc(T.sem[s], 16)
+        cnt[s] = 16
+        note(e, s, R, Wr)
+
+    def lands(s, n, key):
+        cnt[s] = n
+        lastw[key] = (s, n, "far")
+
+    def ts(out, in0, s1, s2, o0, o1, R, Wr):
+        if o1 is None:
+            op("V", lambda q: q.tensor_scalar(out, in0, s1, None, o0), R, Wr)
+        else:
+            op("V", lambda q: q.tensor_scalar(out, in0, s1, s2, o0, o1), R, Wr)
+
+    def tt(out, a, b, o, R, Wr):
+        op("V", lambda q: q.tensor_tensor(out, a, b, o), R, Wr)
+
+    def cp(out, a, R, Wr, e="V"):
+        if e == "V":
+            op("V", lambda q: q.tensor_copy(out, a), R, Wr)
+        else:
+            op("S", lambda q: q.activation(out, a, F.Copy), R, Wr)
+
+    def act(out, a, f, R, Wr, bias=0.0, scale=1.0):
+        op("S", lambda q: q.activation(out, a, f, bias=bias, scale=scale), R, Wr)
+
+    def mm(items, R, Wr, start=True, stop=True):
+        n = len(items)
+        op("P", lambda q: [q.matmul(o, l, r, start and i == 0, stop and i == n - 1) for i, (o, l, r) in enumerate(items)], R, Wr)
+
+    def scan(out, a, b, o0, o1, R, Wr):
+        op("V", lambda q: q.tensor_tensor_scan(out, a, b, 0.0, o0, o1), R, Wr)
+
+    def fill(ap, c, Wr):
+        op("V", lambda q: q.memset(ap, c), "", Wr)
+
+    def iota(ap, pat, base, cm, Wr, flt=True):
+        if flt:
+            op("G", lambda q: q.iota(ap, pat, base, cm, allow_small_or_imprecise_dtypes=True), "", Wr)
+        else:
+            op("G", lambda q: q.iota(ap, pat, base, cm), "", Wr)
+
+    C = lambda k: T.col[:, k:k + 1]
+    Z = lambda k, n: T.z[:, k, 0:n]
+    SR = [T.S0, T.S1, T.S2, T.S3]
+    SHR, AND = A.logical_shift_right, A.bitwise_and
+
+    dma("Y", T.W[:, 0:GH], T.x[:, 0:GH], "", "Wa")
+    dma("S", T.rq[:], T.req[:], "", "rq")
+    dma("S", T.thi[:, 0:1], T.th[:], "", "thi")
+    dma("Y", T.nbi[:, 0:V], T.nb[:], "", "nbi")
+    dma("Y", T.pti[:], T.pt[:], "", "pti")
+    dma("Y", T.W[:, GH:V], T.x[:, GH:V], "", "Wb")
+    iota(T.coli[:, 0:1], [[0, 1]], 0, 1, "coli", False)
+    iota(T.row[:], [[1, 144]], 0, 0, "row")
+    iota(T.rowj[:], [[0, 8], [1, 16]], 0, 0, "rowj")
+    iota(T.rowg[:], [[1, 8], [0, 16]], 0, 0, "rowg")
+    iota(T.wi[:, 0:2], [[128, 2]], 0, 1, "wi0")
+    iota(T.wi[:, 16:32], [[16, 16]], 0, 0, "wi1")
+    iota(T.offc[:], [[512, 8], [16, 2]], 0, 0, "offc", False)
+    deps("G", ["Wa"], [])
+    chip = topo.engines(core, hands[0])
+    per = len(chip) // len(hands)
+    wd = GH // len(hands)
+    l0 = send(g, T, topo, core, [(h, chip[i * per:(i + 1) * per], "hx", T.W[:, i * wd:(i + 1) * wd], T.HB[:, 0:wd]) for i, h in enumerate(hands)], "l0")
+    out_e = topo.engines(core, T.cores[near[0]])
+    for q in near:
+        d = (q - rank) % N
+        a = V + (d - 1) * GH
+        l0 += send(g, T, topo, core, [(T.cores[q], out_e, "xg%d" % d, T.W[:, 0:GH], T.W[:, a:a + GH])], "l0")
+    for d in range(1, N):
+        q = (rank - d) % N
+        nq, fq, hq, _c = ways(T, topo, q)
+        lands("xg%d" % d, len(out_e) if rank in nq else len(hq) * (len(topo.engines(hq[0], core)) // len(fq)), "W%d" % d)
+    lands("l0", l0, "sent")
+    fill(T.Rc[:], 0.0, "Rc")
+    iota(T.tba[:], [[1, 8], [0, 8]], 0, 0, "tba")
+    iota(T.tbb[:], [[0, 8], [1, 8]], 8, 0, "tbb")
+    op("G", lambda q: q.affine_select(T.Rc[:], T.Rc[:], [[16, 8], [1, 8], [0, 8]], A.not_equal, 1.0, 0, -1), "Rc", "Rc")
+    op("G", lambda q: q.affine_select(T.Rc[:], T.Rc[:], [[16, 8], [0, 8], [1, 8]], A.not_equal, 1.0, 8, -1), "Rc", "Rc")
+    iota(T.AW[:], [[0, 2048]], 0, 0, "AW0 AW1")
+    iota(T.bci[:], [[1, 32]], 0, 0, "bci", False)
+    iota(T.mpa[:], [[16, 64]], 1040, 0, "mpa")
+    iota(T.dc[:], [[1, 3], [0, 16]], 2, 0, "dc")
+    iota(T.tcf[:], [[4, 5], [1, 4], [0, 16]], -8, 0, "tcf")
+
+    ts(T.coli[:, 1:2], T.coli[:, 0:1], 15, None, AND, None, "coli", "coli1")
+    ts(T.coli[:, 2:3], T.coli[:, 0:1], 4, None, SHR, None, "coli", "coli2")
+    ts(T.coli[:, 3:4], T.coli[:, 0:1], 4, 1, SHR, AND, "coli", "coli3")
+    cp(T.col[:, 0:4], T.coli[:, 0:4], "coli coli1 coli2 coli3", "col")
+    ts(T.id32[:], T.row[:, 0:128], C(0), None, A.is_equal, None, "row col", "id32")
+    ts(T.ta[:, 0:128], T.rowj[:], C(1), None, A.is_equal, None, "rowj col", "ta")
+    for nm, sc in (("id12", 2.0 ** -12), ("idb", 1.0), ("id8", 8.0), ("idB", 32768.0), ("idm", -255.0)):
+        act(T[nm][:], T.id32[:], F.Identity, "id32", nm, scale=sc)
+    for w in (128, 256, 512):
+        cp(T.ta[:, w:2 * w], T.ta[:, 0:w], "ta", "ta", "S")
+    ts(C(4), C(3), -1.0, 1.0, A.mult, A.add, "col", "col4")
+    ts(C(5), C(0), 16.0, None, A.add, None, "col", "col5")
+    ts(C(6), C(0), -16.0, None, A.add, None, "col", "col6")
+    ts(C(7), C(2), 16.0, 15.0, A.mult, A.add, "col", "col7")
+    ts(T.BOc[:], T.rowj[:], -1.0 / 16, 61.0 / 64, A.mult, A.add, "rowj", "BOc")
+    ts(C(9), C(1), 32.0, None, A.mult, None, "col", "col9")
+    ts(T.wi[:, 16:32], T.wi[:, 16:32], C(1), -LNB, A.add, A.mult, "wi1 col", "wi1")
+    ts(T.wi[:, 0:2], T.wi[:, 0:2], -LNB, LN0, A.mult, A.add, "wi0", "wi0")
+    ts(T.wi[:, 16:32], T.wi[:, 16:32], LN0 + math.log(2.53), None, A.add, None, "wi1", "wi1")
+    for k, (a, b) in enumerate(((0, 4), (5, 4), (6, 3), (0, 3))):
+        ts(T.SWb[:, k, :], T.row[:, 0:128], C(a), C(b), A.is_equal, A.mult, "row col col4 col5 col6", "SW%d" % k)
+    act(T.thr[:], T.wi[:, 16:32], F.Exp, "wi1", "thr")
+    act(T.wcol[:], T.wi[:, 0:2], F.Exp, "wi0", "wcol")
+    act(T.SWs[:], T.SWb[:], F.Identity, "SW0 SW1 SW2 SW3", "SWs", scale=2.0 ** -16)
+    fill(T.rmin[:], 0.0, "rmin")
+    fill(T.ta[:, V:V + 16], 0.0, "taz")
+    fill(T.rmin[:, 0:256:16], 1024.0, "rmin")
+    ts(T.BO[:], T.rowg[:], C(2), None, A.is_equal, None, "rowg col", "BO")
+    act(T.rmax[:], T.rmin[:], F.Identity, "rmin", "rmax", scale=-1.0)
+    ts(C(15), C(1), -1024.0, None, A.add, None, "col", "col15")
+    cp(T.tn[:, 0:16], T.ta[:, 0:16], "ta", "tn0", "S")
+    act(T.tn[:, 16:32], T.ta[:, 0:16], F.Identity, "ta", "tn1", scale=-1.0)
+    tt(T.BOc[:], T.BOc[:], T.BO[:], A.mult, "BOc BO", "BOc")
+    ts(T.Cm[:], T.BO[:], C(15), None, A.mult, None, "BO col15", "Cm")
+    act(T.nBO[:], T.BO[:], F.Identity, "BO", "nBO", scale=-1.0)
+    ts(T.tri[:], T.rowj[:], C(1), -1.0, A.is_le, A.mult, "rowj col", "tri")
+    ts(T.EE[:], T.row[:], C(7), None, A.is_equal, None, "row col7", "EE")
+    tt(T.tri[:], T.tri[:], T.BO[:], A.mult, "tri BO", "tri")
+    fill(T.L0[:], 0, "L0")
+    fill(T.nbi[:, V:V + 16], 0, "pad0")
+    fill(T.pli[:, V:V + 16], 0, "pad1")
+    fill(T.cst[:, V:V + 16], 0.0, "pad2")
+    tt(T.tri[:], T.tri[:], T.idm[:], A.add, "tri idm", "tri")
+    fill(T.L0[:, 23:24], 64, "L0")
+    ts(T.offc[:], T.offc[:], C(9), None, A.add, None, "offc col9", "offc")
+    fill(T.L0[:, 32:48], V + 8, "L0")
+    fill(T.ta[:, V:V + 1], 1.0, "taz")
+    fill(T.FZ[:], 0.0, "FZ")
+    fill(T.Ms[:], BIG, "Ms")
+    fill(T.tb[:], 0.0, "tb")
+    fill(T.BAN[:], 0.0, "BAN0 BAN1")
+    fill(T.rrk[:], 1.0, "rrk")
+    fill(T.r3[:], 0.0, "r3")
+    fill(T.rrk[:, 0:48:8], 0.0, "rrk")
+    fill(T.r3[:, 0:48:3], 1024.0, "r3")
+    for s in range(4):
+        fill(SR[s][:, 0:16], 0.0, "Sz%d" % s)
+    ts(T.rqb[:], T.rq[:], 4, None, SHR, None, "rq", "rqb")
+    cp(C(10), T.thi[:, 0:1], "thi", "col10")
+
+    def requests(t):
+        cp(T.L0[:, 0:7], T.rq[:, 7 * t:7 * t + 7], "rq L0", "Ls0")
+        cp(T.L0[:, 16:23], T.rqb[:, 7 * t:7 * t + 7], "rqb L0", "Lb0")
+    requests(0)
+    ts(C(13), C(10), 2048.0, 2.0 ** -17, A.is_ge, A.mult, "col10", "col13")
+    ts(C(12), C(10), 2.0 ** -12, 2.0 ** -13, A.mult, A.add, "col10", "col12")
+    ts(C(14), C(1), 2.0 ** -16, 8.0, A.mult, A.add, "col", "col14")
+    ts(T.tba[:], T.tba[:], C(1), None, A.is_equal, None, "tba col", "tba")
+    tt(C(11), C(14), C(13), A.add, "col14 col13", "col11")
+    ts(T.tbb[:], T.tbb[:], C(1), None, A.is_equal, None, "tbb col", "tbb")
+    tt(T.tb[:, 0:64], T.tba[:], T.tbb[:], A.add, "tba tbb", "tb")
+    ts(T.cst[:, 0:V], T.pti[:], 1.5 * 2.0 ** 34, 1.5 * 2.0 ** 34, A.add, A.subtract, "pti", "cst")
+    ts(T.pli[:, 0:V], T.pti[:], 2047, None, AND, None, "pti", "pli")
+
+    def later():
+        cp(T.AF[:, 0:64, :], T.AW[:, 64:128, :], "AW1", "AF0")
+        cp(T.bc[:], T.bci[:], "bci", "bc")
+        ts(T.mp[:], T.mpa[:], C(1), None, A.add, None, "mpa col", "mp")
+        ts(T.rep[:], T.rowg[:, 0:4], C(1), None, A.add, None, "rowg col", "rep")
+        ts(T.tc[:], T.tcf[:], C(1), None, A.is_equal, None, "tcf col", "tc")
+        for u in range(1, 4):
+            dma("Y", T.AF[:, 64 * u:64 * u + 64, :], T.AF[:, 0:64, :], "AF0", "AF%d" % u)
+        for d in range(1, N):
+            dma("Y", SR[d][:, 1040:1552], T.W[:, V + (d - 1) * GH:V + d * GH], "W%d" % d, "Sx%d" % d)
+        dma("Y", T.S0[:, 1040:2064], T.x[:], "", "Sx0")
+        for d in range(N):
+            dma("Y", SR[d][:, 16:1040], T.plans[:], "", "Sp%d" % d)
+
+    WALL = "Wa Wb W1 W1b W2 W3"
+    LS, LB, LC = "Ls0 Ls1 pad0 pad1 pad2", "Lb0 Lb1", "L0 Lc1"
+
+    def to_list(out, bank, src, L, key):
+        mm([(out, T.EE[:, 15 - j:143 - j], src[:, j:L:16]) for j in range(16)], "EE " + key, bank)
+
+    def marks_1(t, NB, sl, bl, sk, bk):
+        L = 32 * NB
+        AR = T["AR%d" % t]
+        cp(T.FB[:, 0:L], T.tb[:].indirect(bl), "tb " + bk, "FB", "S")
+        cp(AR[:, 0:L], T.ta[:].indirect(sl), "ta taz " + sk, "AR%d" % t, "S")
+        for h in range(L // 128):
+            mm([(T["pB%d" % h][:], T.FB[:, 128 * h:128 * h + 128], T.Rc[:])], "FB Rc", "pB%d" % h)
+        for h in range(L // 128):
+            mm([(T.pA[:, 128 * h:128 * h + 128], AR[:, 128 * h:128 * h + 128], T.idb[:])], "idb AR%d" % t, "pA")
+        one_b(t, 0)
+        for h in range(L // 128):
+            act(T.AW[:, 64 * h:64 * h + 64:8, :], T.pA[:, 128 * h:128 * h + 128], F.Identity, "pA wcol", "AW%d" % h, scale=T.wcol[:, h:h + 1])
+
+    def one_b(t, h):
+        act(T["B%d" % t][:, 512 * h:512 * h + 512], T["pB%d" % h][:], F.Relu, "pB%d" % h, "B%d%d" % (t, h), bias=-1.0)
+
+    def marks_2(t, NB):
+        L = 32 * NB
+        B = T["B%d" % t]
+        for h in range(L // 128):
+            mm([(T.pM[:, 0:64], T.AW[:, 64 * h + 7 * k:64 * h + 7 * k + 8, :], B[:, 512 * h + 64 * k:512 * h + 64 * k + 64]) for k in range(8)],
+               "AW%d B%d%d" % (h, t, h), "pM", h == 0, h == L // 128 - 1)
+
+    def marks_3(t, NB, bl, bk):
+        L, n = 32 * NB, 2 * NB
+        tt(T.Ms[:, 0:64], T.pM[:, 0:64], (T.FZ if t == 0 else T.MK)[:], A.add, "pM FZ MK", "Ms")
+        tt(T.LK[:, 0:L], T.Ms[:].indirect(bl), T["AR%d" % t][:, 0:L], A.mult, "Ms AR%d " % t + bk, "LK")
+        to_list(T.pS[:, 0, 0, 0:n], "pS", T.LK, L, "LK")
+
+    def reached(t, n):
+        tt(Z(1 + t, n), T.pS[:, 0, 0, 0:n], T.thr[:, 0:n], A.is_lt, "pS thr", "got%d" % t)
+        tt(Z(9 + t, n), Z(1 + t, n), Z(7 + t, n), A.mult, "got%d st%d" % (t, t), "gs%d" % t)
+
+    def plan(t, NB, S16, sk):
+        L, n = 32 * NB, 2 * NB
+        tt(T.PL[:, 0:L], T.pli[:].indirect(S16[:, 0:n]), T["OH%d" % t][:, 0:L], A.mult, "pli OH%d " % t + sk, "PL")
+        if t == 1:
+            to_list(T.pT[:, 64:64 + n], "pT", T.PL, L, "PL")
+            act(Z(4, n), T.pT[:, 64:64 + n], F.Identity, "pT", "pl1", bias=16.0)
+
+    def near_of(S16, sk, NB, v, a, b):
+        cp(T.Q[:, 32 * a + v:32 * b:2], T.nbi[:].indirect(S16[:, NB * v + a:NB * v + b]), "nbi " + sk, "Q%d" % v)
+
+    def cost_of(S16, sk, NB, v, a, b):
+        act(T.CK[:, 32 * a + v:32 * b:2], T.cst[:].indirect(S16[:, NB * v + a:NB * v + b]), F.Identity, "cst col11 " + sk, "CK%d" % v, bias=C(11), scale=2.0 ** -23)
+
+    def step(t, NB, S16, sk, ban, hook):
+        L, n = 32 * NB, 2 * NB
+        run = lambda k: hook.get(k, lambda: None)()
+        a0 = 6 if "head" in hook else 0
+        near_of(S16, sk, NB, 0, a0, NB)
+        near_of(S16, sk, NB, 1, 0, NB)
+        run("head")
+        cost_of(S16, sk, NB, 0, a0, NB)
+        cost_of(S16, sk, NB, 1, 0, NB)
+        run("early")
+        onv = ONV[(NB, t)]
+        done = []
+        kq = T.pQ[:, 0:NB, :, :]
+
+        def turn(a, b):
+            keys = range(a, b)
+            op("V", lambda q: q.transpose(T.GT[:, 512 * a:512 * b], T.G[:, 512 * a:512 * b]), " ".join("G%d" % k for k in keys), " ".join("GT%d" % k for k in keys))
+            done.extend(keys)
+        for b in range(NB):
+            cp(T.G[:, 512 * b:512 * b + 512], T.W[:].indirect(T.Q[:, 32 * b:32 * b + 32]), WALL + " Q0 Q1", "G%d" % b, "V" if b in onv else "S")
+            if b == 0:
+                ts(T.Qf[:, 0:L], T.Q[:, 0:L], -1024.0, None, A.add, None, "Q0 Q1", "Qf")
+            run(b)
+            if b % 2 == 1:
+                k = b // 2
+                if k == 0:
+                    mm([(T.pX[:, 0:L], T.id32[:], T.CK[:, 0:L])], "id32 CK0 CK1", "pX", True, False)
+                if b == NB - 1 and ban is not None:
+                    mm([(T.pX[:, 0:L], T.id8[:], T[ban][:, 0:L])], "id8 %s0 %s1" % (ban, ban), "pX", False, False)
+                mm([(T.pX[:, 64 * k:64 * k + 64], T.id12[:], T.G[:, 1024 * k + i:1024 * k + 1024:16]) for i in range(16)], "id12 G%d G%d" % (b - 1, b), "pX", False, b == NB - 1)
+            if b in onv and b - len(done) >= 2:
+                turn(len(done), b - 1 if b < NB - 1 else b)
+        act(T.TH[:, 0:L], T.CK[:, 0:L], F.Identity, "CK0 CK1 col12", "TH", bias=C(12))
+        run("gathered")
+        if len(done) < NB - 1:
+            turn(len(done), NB - 1)
+        turn(len(done), NB)
+        run("mid")
+        mm([(kq, T.BOc[:], T.ta[:, 0:L])] + [(T.pQ[:, 0:NB, e, :], T.SWs[:, 2 * e + v, :], T.Qf[:, v:L:2]) for e in range(2) for v in range(2)],
+           "BOc ta SWs Qf", "pQ", True, False)
+        tt(T.ov[:, 0:L], T.pX[:, 0:L], T.TH[:, 0:L], A.is_gt, "pX TH", "ov")
+        for v in range(2):
+            tt(T.kR[:, 0:NB, v, :], T.pX[:, v:L:2], T.ov[:, v:L:2], A.add, "pX ov", "kR%d" % v)
+        op("V", lambda q: q.transpose(T.kT[:, 0:L], T.kR[:, 0:NB, :, :]), "kR0 kR1", "kT")
+        scan(T.km[:, 0:L], T.rmin[:, 0:L], T.kT[:, 0:L], A.add, A.min, "rmin kT", "km")
+        ts(T.ki[:, 0:n], T.km[:, 15:L:16], 2.0 ** 17, None, A.mult, None, "km", "ki")
+        ts(T.ci[:, 0:n], T.ki[:, 0:n], 1, 15, SHR, AND, "ki", "ci")
+        ts(T.hh[:, 0:n], T.ki[:, 0:n], 1, None, AND, None, "ki", "hh")
+        tt(T.off[:, 0:n], T.ci[:, 0:n], T.offc[:, 0:n], A.add, "ci offc", "off")
+        cp(T.K1[:, 0:L], T.GT[:, 0:16 * L].indirect(T.off[:, 0:n]), " ".join("GT%d" % a for a in range(NB)) + " off", "K1", "S")
+        cp(T.CS[:, 0:n], T.ci[:, 0:n], "ci", "CS0")
+        ts(T.ht[:, 0:n], T.hh[:, 0:n], 65536.0, 131103.0 + 2.0 ** 20, A.mult, A.add, "hh", "ht")
+        tt(T.CS[:, 16:16 + n], T.ki[:, 0:n], T.ht[:, 0:n], A.is_gt, "ki ht", "CS1")
+        for f in range(2):
+            bank = ("pT", "pA")[f]
+            for v in range(2):
+                mm([(T[bank][:, 384 + NB * v:384 + NB * (v + 1)], T.SWb[:, 2 * v + e, :], T.CS[:, 16 * f + e:16 * f + n:2]) for e in range(2)], "SWs CS%d" % f, bank)
+        mm([(kq, T.idb[:], T.K1[:, 0:L])], "idb K1", "pQ", False, True)
+        cl = T["c%d" % t]
+        cp(cl[:, 0:n], T.pT[:, 384:384 + n], "pT", "cl%d" % t)
+        run("chosen")
+        if NB == 8:
+            one_b(t, 1)
+        marks_2(t, NB)
+        op("V", lambda q: q.transpose(T.K1T[:, 0:L], kq), "pQ", "K1T")
+        cp(Z(7 + t, n), T.pA[:, 384:384 + n], "pA", "st%d" % t, "S")
+        cp(T["OH%d" % t][:, 0:L], T.ta[:].indirect(cl[:, 0:n]), "ta taz cl%d" % t, "OH%d" % t, "S")
+        scan(T.bm[:, 0:L], T.rmax[:, 0:L], T.K1T[:, 0:L], A.add, A.max, "rmax K1T", "bm")
+        run("late")
+        for v in range(2):
+            ts(T.bi[:, NB * v:NB * (v + 1)], T.bm[:, 16 * v + 15:L:32], 65536.0, None, A.mult, None, "bm", "bi%d" % v)
+        if t == 0:
+            ts(T.si[:, 0:n], T.bi[:, 0:n], 1023, None, AND, None, "bi0 bi1", "si")
+            cp(T.s1[:, 0:n], T.si[:, 0:n], "si", "s1")
+        else:
+            ts(T.zi[:, 1, 0:n], T.bi[:, 0:n], 4095, None, AND, None, "bi0 bi1", "b1")
+
+    def refresh(d, j, a, b, e, key):
+        at, m = V + (d - 1) * GH, 12 - 4 * (N - d)
+        cp(T.W[:, at + 16 * a:at + 16 * b], SR[d][:].indirect(T.IN[:, j, m + a:m + b]), "Sz%d Sp%d Sx%d IN%d" % (d, d, d, j), key, e)
+
+    for rnd in range(RO):
+        NB = 4 if rnd == 0 else 8
+        L, n, NH = 32 * NB, 2 * NB, NB // 4
+        last = rnd == RO - 1
+        sl0, bl0 = T.L0[:, 0:n], T.L0[:, 16:16 + n]
+        j0 = 3 * (rnd - 1)
+        INS = "IN%d IN%d IN%d" % (j0, j0 + 1, j0 + 2)
+        YB = [T.pX[:, 0:128], T.pQ[:, 0:4, :, :], T.pB0[:, 0:128], T.pB1[:, 0:128]]
+        YK = ("pX", "pQ", "pB0", "pB1")
+
+        def head0():
+            refresh(1, j0 + 2, 0, CUT, "V", "W1")
+            cp(T.L0[:, 39:48], T.IN[:, j0:j0 + 3, 56:59], "L0 " + INS, "Lc1")
+
+        def ban0():
+            cp(T.BAN[:, 192:256:2], T.ta[:].indirect(T.L0[:, 38:40]), "ta taz " + LC, "BAN0", "S")
+            cp(T.BAN[:, 1:256:2], T.ta[:].indirect(T.L0[:, 40:48]), "ta taz " + LC, "BAN1", "S")
+
+        def lists0():
+            cp(T.oi[:, 0:9], T.L0[:, 7:16], LS, "oi")
+            ts(T.oi[:, 0:9], T.oi[:, 0:9], 4, None, SHR, None, "oi", "oi")
+            cp(T.L0[:, 23:32], T.oi[:, 0:9], "L0 oi", "Lb1")
+
+        hook = {"mid": lambda: marks_1(0, NB, sl0, bl0, LS, LB)}
+        if rnd > 0:
+            hook.update({"head": head0, "early": ban0, 0: lists0})
+        else:
+            hook["gathered"] = later
+        step(0, NB, T.L0, LS, "BAN" if rnd > 0 else None, hook)
+
+        def after0a():
+            marks_3(0, NB, bl0, LB)
+            ts(T.zi[:, 0, 0:n], T.bi[:, 0:n], 4095, None, AND, None, "bi0 bi1", "b0")
+            ts(T.zi[:, 2, 0:n], T.bi[:, 0:n], 4, 255, SHR, AND, "bi0 bi1", "sb")
+            ts(T.MK[:], T.Ms[:, 0:64], 0.0, BIG, A.is_gt, A.mult, "Ms", "MK")
+
+        def after0b():
+            reached(0, n)
+            ts(Z(19, n), Z(9, n), -64.0, 64.0, A.mult, A.add, "gs0", "z19")
+            tt(Z(13, n), Z(9, n), T.zi[:, 0, 0:n], A.mult, "gs0 b0", "bg0")
+            tt(T.b1[:, 0:n], Z(19, n), T.zi[:, 2, 0:n], A.max, "z19 sb", "bl1")
+            ts(Z(15, n), Z(13, n), 1024.0, 16.0, A.is_ge, A.mult, "bg0", "ask0")
+            cp(Z(5, n), T.c0[:, 0:n], "cl0", "ch0")
+            tt(T.cb[:, 0:n], Z(15, n), Z(5, n), A.add, "ask0 ch0", "cb")
+            plan(0, NB, T.L0, LS)
+            tt(Z(11, n), Z(1, n), Z(9, n), A.subtract, "got0 gs0", "gd0")
+
+        def ban1():
+            for v in range(2):
+                cp(T.BN[:, v:L:2], T.tn[:].indirect(T.cb[:, NB * v:NB * (v + 1)]), "tn0 tn1 cb", "BN%d" % v, "S")
+
+        def after0c():
+            to_list(T.pT[:, 64:64 + n], "pT", T.PL, L, "PL")
+            act(Z(22, n), Z(1, n), F.Identity, "got0", "q0", scale=0.25)
+
+        def late1():
+            tt(Z(21, n), Z(1, n), Z(3, n), A.mult, "got0 pl0", "a0")
+            marks_3(1, NB, T.b1[:, 0:n], "bl1")
+
+        hook = {"early": after0a, 1: after0b, NB // 2: ban1, "gathered": after0c, "mid": lambda: marks_1(1, NB, T.s1[:, 0:n], T.b1[:, 0:n], "s1", "bl1"),
+                "chosen": lambda: act(Z(3, n), T.pT[:, 64:64 + n], F.Identity, "pT", "pl0", bias=15.75), "late": late1}
+        step(1, NB, T.s1, "s1", "BN", hook)
+        for t in range(2):
+            for h in range(NH):
+                mm([(YB[2 * t + h], T["AR%d" % t][:, 128 * h:128 * h + 128], T.idB[:])], "idB AR%d" % t, YK[2 * t + h], True, False)
+        plan(1, NB, T.s1, "s1")
+        reached(1, n)
+        bI, dI = T.zi[:, 3, 0:n], T.dI[:, 0:n]
+        tt(Z(14, n), Z(10, n), T.zi[:, 1, 0:n], A.mult, "gs1 b1", "bg1")
+        tt(bI, Z(13, n), Z(14, n), A.max, "bg0 bg1", "bI")
+        ts(dI, bI, 9, None, SHR, None, "bI", "dI")
+        if n == 16:
+            tt(T.ff[:], T.dI[:].indirect(T.rep[:, 0:3]), T.dc[:], A.is_equal, "dI rep dc", "ff0 ff1 ff2")
+        else:
+            for d in range(3):
+                ts(T.ff[:, n * d:n * d + n], dI, float(d + 2), None, A.is_equal, None, "dI", "ff%d" % d)
+        scan(T.inc[:, 0:3 * n], T.rrk[:, 0:3 * n], T.ff[:, 0:3 * n], A.mult, A.add, "rrk ff0 ff1 ff2", "inc")
+        for d in range(3):
+            o = T.pM[:, 64 + d:64 + 3 * n:3]
+            mm([(o, T.tri[:], T.ff[:, n * d:n * d + n]), (o, T.BO[:], T.inc[:, n * d:n * d + n])], "tri BO ff0 ff1 ff2 inc", "pM")
+        tt(Z(12, n), Z(2, n), Z(10, n), A.subtract, "got1 gs1", "gd1")
+        if not last:
+            ts(Z(26, n), dI, 64.0, None, A.mult, None, "dI", "z26")
+            ts(T.XI[:, 0:n], bI, 511, None, AND, None, "bI", "XI")
+        tt(Z(25, n), Z(11, n), Z(12, n), A.add, "gd0 gd1", "gd")
+        scan(T.fr[:, 0:3 * n], T.r3[:, 0:3 * n], T.pM[:, 64:64 + 3 * n], A.add, A.min, "r3 pM", "fr")
+        rk = T.fr[:, 2:3 * n:3]
+        tt(Z(31, n), Z(2, n), Z(4, n), A.mult, "got1 pl1", "a1")
+        if not last:
+            ts(Z(27, n), rk, 255.0, 48.0, A.add, A.min, "fr", "z27")
+        ts(Z(28, n), rk, -207.5, None, A.is_lt, None, "fr", "sent1")
+        if not last:
+            tt(T.SL[:, 0:n], Z(26, n), Z(27, n), A.add, "z26 z27", "SL")
+            cp(T.AO[:, L:2 * L], T.tc[:].indirect(T.SL[:, 0:n]), "tc SL", "AO1", "S")
+            cp(T.AO[:, 0:L], T.ta[:].indirect(T.SL[:, 0:n]), "ta taz SL", "AO0", "S")
+        tt(Z(29, n), Z(28, n), Z(25, n), A.add, "sent1 gd", "good")
+        if not last:
+            tt(T.DX[:, 0:L], T.XI[:, 0:n].indirect(T.bc[:, 0:n]), T.ta[:, 0:L], A.mult, "XI bc ta", "DX")
+        tt(Z(30, n), Z(29, n), Z(21, n), A.mult, "good a0", "z30")
+        tt(T.WW[:, n:2 * n], Z(29, n), Z(31, n), A.mult, "good a1", "WW1")
+        tt(T.WW[:, 0:n], Z(30, n), Z(22, n), A.add, "z30 q0", "WW0")
+        if not last:
+            for h in range(NH):
+                for f, (l, r) in enumerate(((T.DX, T.nBO), (T.OH1, T.Cm))):
+                    o = T.pS[:, 8 * h:8 * h + 8, f, :]
+                    mm([(o, T.AO[:, L + 128 * h:L + 128 * h + 128], T.idB[:]), (o, l[:, 128 * h:128 * h + 128], r[:])], "idB nBO Cm AO1 DX OH1", "pS")
+            for h in range(NH):
+                mm([(T.pA[:, 128 * h:128 * h + 128], T.AO[:, 128 * h:128 * h + 128], T.idb[:])], "idb AO0", "pA")
+            for h in range(NH):
+                cp(T.AW[:, 64 * h:64 * h + 64:8, :], T.pA[:, 128 * h:128 * h + 128], "pA", "AW%d" % h, "S")
+        for t in range(2):
+            tt(T.D[:, L * t:L * t + L], T.WW[:, 0:2 * n].indirect(T.bc[:, n * t:n * t + n]), T.ta[:, 0:L], A.mult, "WW0 WW1 bc ta", "D%d" % t)
+            for h in range(NH):
+                mm([(YB[2 * t + h], T.D[:, L * t + 128 * h:L * t + 128 * h + 128], T.BO[:])], "BO D%d" % t, YK[2 * t + h], False, True)
+        for t in range(2):
+            for h in range(NH):
+                u = 2 * t + h
+                ts(T.AF[:, 64 * u:64 * u + 64:8, :], YB[u], -32768.0, 0.0, A.add, A.max, YK[u], "AF%d" % u)
+                mm([(T.pM[:, 128:192], T.AF[:, 64 * u + 7 * k:64 * u + 7 * k + 8, :], T["B%d" % t][:, 512 * h + 64 * k:512 * h + 64 * k + 64]) for k in range(8)],
+                   "AF%d B%d%d" % (u, t, h), "pM", t == 0 and h == 0, t == 1 and h == NH - 1)
+        if not last:
+            ts(T.X[:, 0:2 * L], T.pS[:, 0:8 * NH, :, :], 1024.0 - 32768.0, 0.0, A.add, A.max, "pS", "X")
+            mm([(T.pA[:, 256:288], T.AW[:, 64 * h + 7 * k:64 * h + 7 * k + 8, :], T.X[:, 256 * h + 32 * k:256 * h + 32 * k + 32])
+                for h in range(NH) for k in range(8)], "AW0 AW1 X", "pA")
+        ts(T.kp[:], T.pM[:, 128:192], 0.5, None, A.is_lt, None, "pM", "kp")
+        tt(T.kp[:], T.kp[:], T.mp[:], A.mult, "kp mp", "kp")
+        if not last:
+            tt(T.MSG[:, rnd, 0:32], T.pM[:, 128:160], T.kp[:, 0:32], A.add, "pM kp", "MSGm")
+            cp(T.MSG[:, rnd, 32:64], T.pA[:, 256:288], "pA", "MSGo")
+            deps("G", ["MSGo", "MSGm"], [])
+            rest = [e for e in chip if e not in out_e]
+            per = len(rest) // len(far)
+            items = [(h, rest[i * per:(i + 1) * per], "hm%d" % rnd, T.MSG[:, rnd, :], T.HM[:, rnd, :]) for i, h in enumerate(close)]
+            for q in near:
+                d = (rank - q) % N
+                j = 3 * rnd + d - 1
+                items.append((T.cores[q], out_e, "m%d" % j, T.MSG[:, rnd, :], T.IN[:, j, 12 - 4 * d:76 - 4 * d]))
+            ls[0] += send(g, T, topo, core, items, "ls")
+            for d in range(1, N):
+                lands("m%d" % (3 * rnd + d - 1), len(out_e), "IN%d" % (3 * rnd + d - 1))
+        tt(T.mp16[:], T.pM[:, 128:192], T.kp[:], A.add, "pM kp", "mp16")
+        cp(T.W[:, 0:GH], T.S0[:].indirect(T.mp16[:, 0:32]), "Sz0 Sp0 Sx0 mp16 sent", "Wa", "S")
+        cp(T.W[:, GH:V], T.S0[:].indirect(T.mp16[:, 32:64]), "Sz0 Sp0 Sx0 mp16", "Wb")
+        if last:
+            dma("S", T.y[:, 0:GH], T.W[:, 0:GH], "Wa", "ya")
+            dma("Y", T.y[:, GH:V], T.W[:, GH:V], "Wb", "yb")
+            break
+        cp(T.mp[:], T.mp16[:], "mp16", "mp")
+        ts(T.fz1[:], T.pM[:, 128:192], 0.25, BIG, A.is_equal, A.mult, "pM", "fz1")
+        tt(T.FZ[:], T.FZ[:], T.fz1[:], A.max, "FZ fz1", "FZ")
+        if rnd == 0:
+            fill(T.rrk[:, 8:48:16], 1.0, "rrk")
+        requests(rnd + 1)
+        near_of(T.L0, LS, 8, 0, 0, 6)
+        cost_of(T.L0, LS, 8, 0, 0, 6)
+        for d in (2, 1, 3):
+            j = 3 * rnd + d - 1
+            if d != 3:
+                refresh(N - d, j, 0, 32, "S", "W%d" % (N - d))
+            else:
+                refresh(1, j, CUT, 32, "S", "W1b")
+        ts(T.L0[:, 7:16], T.IN[:, 3 * rnd:3 * rnd + 3, 40:43], -1.0, 1024.0, A.mult, A.add, "L0 IN%d IN%d IN%d" % (3 * rnd, 3 * rnd + 1, 3 * rnd + 2), "Ls1")
+
+    for s in sorted(cnt):
+        if seen.get(("G", s), 0) < cnt[s]:
+            g.wait_ge(T.sem[s], cnt[s])
+    g.wait_ge(T.sem.ls, ls[0])

@@ -6,8 +6,13 @@ V, GH, RO = 1024, 512, 4
 BIG = 2.0 ** 94
 LNB = math.log(1.75)
 LN0 = 90 * math.log(2.0)
-ONV = {(4, 0): (0,), (4, 1): (3,), (8, 0): (0, 3, 6), (8, 1): (2, 5)}
-CUT = 24
+WAKE, GATHER, PE, LOAD, HOP = 130, 1.56, 0.75, 2400, 2400
+SPARE, LAG, CUTS, PASSES, FIX = 2.0, 2, 1, 2, 36
+ON = {(8, 0): "----", (8, 1): "----", (16, 0): "VSVSSSSS", (16, 1): "SSSSSSSS"}
+CUT = {(8, 0): [(0, 4)], (8, 1): [(0, 4)], (16, 0): [(0, 4), (8, 4)], (16, 1): [(0, 4), (8, 4)]}
+S16 = "VS"
+FAR0, NEAR0 = 2.2, 1.3
+ENDS = []
 
 
 def _sb(n, d="float32"):
@@ -18,29 +23,30 @@ H, I32, U16, F16 = "bfloat16", "int32", "uint16", "float16"
 SCRATCH = {
     "W": _sb(2560, H), "S0": _sb(2064, H), "S1": _sb(1552, H), "S2": _sb(1552, H), "S3": _sb(1552, H),
     "nbi": _sb(V + 16, I32), "pti": _sb(V, I32), "pli": _sb(V + 16, I32), "cst": _sb(V + 16),
-    "rq": _sb(28, I32), "rqb": _sb(28, I32), "thi": _sb(4, I32), "col": _sb(16), "coli": _sb(4, I32),
+    "rq": _sb(28, I32), "rqb": _sb(28, I32), "thi": _sb(4, I32), "col": _sb(20), "coli": _sb(4, I32),
     "row": _sb(144), "rowg": _sb(128), "rowj": _sb(128), "Rc": _sb(512, H),
-    "idb": _sb(128, H), "id12": _sb(128, H), "id8": _sb(128, H), "idB": _sb(128, H), "idm": _sb(128, H), "id32": _sb(128),
-    "BOc": _sb(128, H), "Cm": _sb(128, F16), "BN": _sb(256, H), "tn": _sb(32, H), "cb": _sb(16, U16),
-    "BO": _sb(128, H), "nBO": _sb(128, H), "tri": _sb(128, H), "EE": _sb(144, H), "SWs": _sb([4, 128], H), "SWb": _sb([4, 128], H),
-    "ta": _sb(1040, H), "tb": _sb(160, H), "tba": _sb(64), "tbb": _sb(64), "tcf": _sb(320), "tc": _sb(320, H), "bci": _sb(32, I32), "bc": _sb(32, U16),
-    "rep": _sb(4, U16), "dc": _sb(48), "r3": _sb(48),
+    "idb": _sb(128, H), "id12": _sb(128, H), "id4": _sb(128, H), "idB": _sb(128, H), "idB1": _sb(128, H), "idm": _sb(128, H), "id32": _sb(128),
+    "thM": _sb(128, F16), "on12": _sb(256, H), "zer": _sb(256, H), "THD": _sb(256, H),
+    "BOc": _sb(128, H), "Cm0": _sb(128, H), "Cm1": _sb(128, F16),
+    "BO": _sb(128, H), "nBO": _sb(128, H), "BOK": _sb(128, H), "tri": _sb(128, H), "EE": _sb(144, H), "SWs": _sb([4, 128], H), "SWb": _sb([4, 128], H),
+    "ta": _sb(1296, H), "taf": _sb(256), "tb": _sb(160, H), "tba": _sb(64), "tbb": _sb(64), "tcf": _sb(320), "tc": _sb(640, H),
+    "bci": _sb(32, I32), "bc": _sb(32, U16), "rep": _sb(4, U16), "dc": _sb(48), "r4": _sb(64),
     "rmin": _sb(256), "rmax": _sb(256), "rrk": _sb(48, H), "offc": _sb(16, I32), "wi": _sb(32), "wcol": _sb(2), "thr": _sb(16),
-    "mp": _sb(64), "mpa": _sb(64), "kp": _sb(64), "mp16": _sb(64, U16), "FZ": _sb(64, H), "fz1": _sb(64, H), "MK": _sb(64, H), "Ms": _sb(160, H),
+    "mp": _sb(64), "kp0": _sb(64), "kp": _sb(64), "mp16": _sb(64, U16), "FZ": _sb(64, H), "MK": _sb(64, H), "Ms": _sb(160, H),
     "AW": _sb([128, 16], H), "AF": _sb([256, 16], F16),
-    "L0": _sb(48, U16), "s1": _sb(16, U16), "b1": _sb(16, U16), "c0": _sb(16, U16), "c1": _sb(16, U16), "oi": _sb(16, I32),
-    "Q": _sb(256, U16), "Qf": _sb(256, F16), "CK": _sb(256), "TH": _sb(256), "BAN": _sb(256, H),
+    "L0": _sb(48, U16), "s1": _sb(16, U16), "b1": _sb(16, U16), "c0": _sb(16, U16), "c1": _sb(16, U16),
+    "Q": _sb(256, U16), "Qf": _sb(256, F16), "CK": _sb(256), "BAN": _sb(256, H),
     "OH0": _sb(256, H), "OH1": _sb(256, H), "G": _sb(4096, H), "GT": _sb(4096, H),
     "ov": _sb(256), "kR": _sb([8, 2, 16]), "kT": _sb(256), "km": _sb(256), "ki": _sb(16, I32), "ci": _sb(16, I32), "off": _sb(16, U16),
-    "hh": _sb(16, I32), "ht": _sb(16), "CS": _sb(32, H), "K1": _sb(256, H), "K1T": _sb(256), "bm": _sb(256), "bi": _sb(16, I32), "si": _sb(16, I32),
-    "AR0": _sb(256, H), "AR1": _sb(256, H), "FB": _sb(256, H), "B0": _sb(1024, H), "B1": _sb(1024, H), "LK": _sb(256, H), "PL": _sb(256, F16),
-    "z": _sb([32, 16]), "zi": _sb([5, 16], I32), "dI": _sb(16, I32), "ff": _sb(48, H), "inc": _sb(48, H), "fr": _sb(48), "WW": _sb(32), "XI": _sb(16, I32), "SL": _sb(16, U16),
-    "D": _sb(512, F16), "DX": _sb(256, F16), "AO": _sb(512, H), "X": _sb(512, F16),
+    "CS": _sb([2, 16], H), "K1": _sb(256, H), "K1T": _sb(256), "bm": _sb(256), "bi0": _sb(16, I32), "bi1": _sb(16, I32),
+    "AR0": _sb(256, H), "AR1": _sb(256, H), "FB": _sb(256, H), "B0": _sb(1024, H), "B1": _sb(1024, H), "LK": _sb(256, H), "PL0": _sb(256, F16), "PL1": _sb(256, F16),
+    "z": _sb([32, 16]), "zi": _sb([6, 16], I32), "dI": _sb(16, I32), "gd": _sb(16, H), "ff": _sb(48, H), "inc": _sb(48, H), "fr": _sb(64), "XI": _sb(16, I32), "SL": _sb(16, U16),
+    "D": _sb(256, H), "DX": _sb(256, F16), "AO": _sb(512, H), "X": _sb(512, F16),
     "MSG": _sb([3, 64], U16), "IN": _sb([9, 72], U16), "HB": _sb(128, H), "HM": _sb([3, 64], U16),
 }
-for _p in ("pX", "pA", "pB0", "pB1", "pM", "pT"):
+for _p in ("pA", "pB0", "pB1", "pM", "pY"):
     SCRATCH[_p] = ("psum", [128, 512], "float32")
-for _p in ("pQ", "pS"):
+for _p in ("pC0", "pC1", "pS"):
     SCRATCH[_p] = ("psum", [128, 16, 2, 16], "float32")
 SEMAPHORES = (["cV", "cS", "cP", "cG", "l0", "ls", "hx", "hm0", "hm1", "hm2", "xg1", "xg2", "xg3"] + ["m%d" % k for k in range(9)] + ["d%d" % k for k in range(24)])
 
@@ -94,12 +100,142 @@ def helper(g, core, T, topo):
     if core in close:
         q = far[close.index(core)]
         d = (r - q) % n
-        left = len(topo.engines(own[0], core)) - len(topo.engines(own[0], T.cores[near[0]]))
         for t in range(RO - 1):
-            g.wait_ge(T.sem["hm%d" % t], left // len(far))
+            g.wait_ge(T.sem["hm%d" % t], len(topo.engines(own[0], core)) // len(far))
             j = 3 * t + d - 1
             ls += send(g, T, topo, core, [(T.cores[q], es, "m%d" % j, T.HM[:, t, :], T.IN[:, j, 12 - 4 * d:76 - 4 * d])], "ls")
     g.wait_ge(T.sem.ls, ls)
+
+
+def new_plan():
+    return {"ops": [], "lastw": {}, "reads": {}, "chain": {}, "pin": {}}
+
+
+def add(P, cost, fn, R, Wr, lat=0, tok=None, start=False, stop=False):
+    R, Wr = R.split(), Wr.split()
+    k = len(P["ops"])
+    dep = {}
+    for x in R:
+        if x in P["lastw"]:
+            dep[P["lastw"][x]] = True
+    onP = "P" in cost
+    for x in Wr:
+        if x in P["lastw"]:
+            a = P["lastw"][x]
+            dep[a] = dep.get(a, False) or not (onP and "P" in P["ops"][a]["cost"])
+        for a in P["reads"].get(x, []):
+            dep[a] = True
+    banks = set(x.split(".")[0] for x in R + Wr if x[0] == "p" and x[1].isupper())
+    for b in banks:
+        if onP and b not in ("pA", "pS", "pB1"):
+            if start and b in P["chain"]:
+                dep.setdefault(P["chain"][b], False)
+            if stop:
+                P["chain"][b] = k
+    for e in cost:
+        if e in "GY":
+            if e in P["pin"]:
+                dep.setdefault(P["pin"][e], False)
+            P["pin"][e] = k
+    dep.pop(k, None)
+    for x in R:
+        P["reads"].setdefault(x, []).append(k)
+    for x in Wr:
+        P["lastw"][x] = k
+        P["reads"][x] = []
+    P["ops"].append({"cost": cost, "fn": fn, "dep": dep, "lat": lat, "tok": tok, "banks": banks})
+    return k
+
+
+def lay(P):
+    ops = P["ops"]
+    n = len(ops)
+    rest = [0.0] * n
+    for k in range(n - 1, -1, -1):
+        o = ops[k]
+        rest[k] += min(o["cost"].values())
+        for a, w in o["dep"].items():
+            rest[a] = max(rest[a], rest[k] + ((WAKE + ops[a]["lat"]) if w else 0))
+    before = [[(a, (WAKE + ops[a]["lat"]) if w else 0) for a, w in o["dep"].items()] for o in ops]
+    behind = [[] for o in ops]
+    for k in range(n):
+        for a, d in before[k]:
+            behind[a].append((k, d))
+
+    def place(order, edges):
+        line, bank, at = {}, {}, {}
+        for k in order:
+            o = ops[k]
+            t0 = max([at[a][1] + d for a, d in edges[k]] + [0.0])
+            best = None
+            for e, c in o["cost"].items():
+                busy = [x for x in line.get(e, []) if x[1] > t0] if e != "far" else []
+                for bk in o["banks"]:
+                    busy += [(a - WAKE, b + WAKE) for a, b, e2, _k in bank.get(bk, []) if e2 != e and b + WAKE > t0]
+                t = t0
+                for a, b in sorted(busy):
+                    if t + c <= a:
+                        break
+                    t = max(t, b)
+                if best is None or t + c + (SPARE * c if e == "V" else 0) < best[0]:
+                    best = (t + c + (SPARE * c if e == "V" else 0), t, t + c, e)
+            at[k] = best[1:]
+            line.setdefault(best[3], []).append(best[1:3])
+            for bk in o["banks"]:
+                bank.setdefault(bk, []).append(best[1:] + (k,))
+        return at, bank, max(at[k][1] + ops[k]["lat"] for k in range(n))
+
+    at, bank, end = place(sorted(range(n), key=lambda k: (-rest[k], k)), before)
+    now = at
+    for _ in range(PASSES):
+        back = place(sorted(range(n), key=lambda k: (-now[k][1], -k)), behind)[0]
+        now, bk2, end2 = place(sorted(range(n), key=lambda k: (-back[k][1], k)), before)
+        if end2 < end:
+            at, bank, end = now, bk2, end2
+    for k in range(n):
+        ops[k]["t0"], ops[k]["t1"], ops[k]["e"] = at[k]
+    ENDS.append(end)
+    for bk, uses in bank.items():
+        last = {}
+        for a, b, e, k in sorted(uses):
+            for e2, k2 in last.items():
+                if e2 != e:
+                    ops[k]["dep"][k2] = True
+            last[e] = k
+    return sorted(range(n), key=lambda k: (ops[k]["t0"], ops[k]["t1"], k))
+
+
+def issue(P, eng, T):
+    ops = P["ops"]
+    cnt, seen = {}, {}
+    for k in lay(P):
+        o = ops[k]
+        e = o["e"]
+        need = {}
+        for a, w in o["dep"].items():
+            if w and ops[a]["tok"] and e != "far":
+                s, v = ops[a]["tok"]
+                need[s] = max(need.get(s, 0), v)
+        for s, v in need.items():
+            if seen.get((e, s), 0) < v:
+                eng[e].wait_ge(T.sem[s], v)
+                seen[(e, s)] = v
+        if e == "far":
+            cnt[o["tok"][0]] = o["tok"][1]
+            continue
+        out = o["fn"](eng[e], e)
+        if o["tok"]:
+            out.then_inc(T.sem[o["tok"][0]], o["tok"][1])
+            cnt[o["tok"][0]] = o["tok"][1]
+        elif out is not None:
+            s = "c" + e
+            for ins in (out if isinstance(out, list) else [out]):
+                ins.then_inc(T.sem[s], 1)
+                cnt[s] = cnt.get(s, 0) + 1
+            o["tok"] = (s, cnt[s])
+    for s in sorted(cnt):
+        if seen.get(("G", s), 0) < cnt[s]:
+            eng["G"].wait_ge(T.sem[s], cnt[s])
 
 
 def rank_program(g, core, T, topo):
@@ -110,525 +246,438 @@ def rank_program(g, core, T, topo):
     N = len(T.cores)
     near, far, hands, close = ways(T, topo, rank)
     eng = {"V": g.vector, "S": g.scalar, "P": g.tensor, "G": g, "Y": g.sync}
-    cnt, seen, lastw, reads, nd, ls = {}, {}, {}, {}, [0], [0]
+    P = new_plan()
+    nd, ls = [0], [0]
+    plain = lambda n, r=1.0: max(64.0, n * r) + FIX
+    gath = lambda n, es="VS": {e: (60 if e == "V" else 78) + GATHER * n for e in es}
+    both = lambda n, r=1.0, es="VS": {e: plain(n, r if e == "V" else 1.0) for e in es}
 
-    def deps(e, R, Wr):
-        need = {}
-
-        def want(x):
-            if x[1] > need.get(x[0], 0):
-                need[x[0]] = x[1]
-        for k in R:
-            if k in lastw:
-                want(lastw[k])
-            if k[0] == "p" and k[1].isupper():
-                for x in reads.get(k, {}).values():
-                    if x[2] != e:
-                        want(x)
-        for k in Wr:
-            if k in lastw and not (e == "P" and lastw[k][2] == "P"):
-                want(lastw[k])
-            for x in reads.get(k, {}).values():
-                want(x)
-        for s, v in need.items():
-            if seen.get((e, s), 0) < v:
-                eng[e].wait_ge(T.sem[s], v)
-                seen[(e, s)] = v
-
-    def note(e, s, R, Wr):
-        x = (s, cnt[s], e)
-        for k in R:
-            reads.setdefault(k, {})[s] = x
-        for k in Wr:
-            lastw[k] = x
-            reads[k] = {}
-
-    def op(e, fn, R, Wr):
-        R, Wr = R.split(), Wr.split()
-        deps(e, R, Wr)
-        s = "c" + e
-        out = fn(eng[e])
-        for ins in (out if isinstance(out, list) else [out]):
-            ins.then_inc(T.sem[s], 1)
-            cnt[s] = cnt.get(s, 0) + 1
-        note(e, s, R, Wr)
-
-    def dma(e, out, in_, R, Wr):
-        R, Wr = R.split(), Wr.split()
-        deps(e, R, Wr)
+    def dma(e, out, in_, R, Wr, lat=1.0):
         s = "d%d" % nd[0]
         nd[0] += 1
-        eng[e].dma_start(out, in_).then_inc(T.sem[s], 16)
-        cnt[s] = 16
-        note(e, s, R, Wr)
+        add(P, {e: 50}, lambda q, _e: q.dma_start(out, in_), R, Wr, lat * LOAD, (s, 16))
 
-    def lands(s, n, key):
-        cnt[s] = n
-        lastw[key] = (s, n, "far")
+    def lands(s, n, R, key, lat):
+        add(P, {"far": 1}, None, R, key, lat * HOP, (s, n))
 
-    def ts(out, in0, s1, s2, o0, o1, R, Wr):
+    def ts(n, out, in0, s1, s2, o0, o1, R, Wr):
+        c = n if isinstance(n, dict) else {"V": plain(n)}
         if o1 is None:
-            op("V", lambda q: q.tensor_scalar(out, in0, s1, None, o0), R, Wr)
+            add(P, c, lambda q, e: q.tensor_scalar(out, in0, s1, None, o0), R, Wr)
         else:
-            op("V", lambda q: q.tensor_scalar(out, in0, s1, s2, o0, o1), R, Wr)
+            add(P, c, lambda q, e: q.tensor_scalar(out, in0, s1, s2, o0, o1), R, Wr)
 
-    def tt(out, a, b, o, R, Wr):
-        op("V", lambda q: q.tensor_tensor(out, a, b, o), R, Wr)
+    def tt(n, out, a, b, o, R, Wr):
+        add(P, n if isinstance(n, dict) else {"V": plain(n)}, lambda q, e: q.tensor_tensor(out, a, b, o), R, Wr)
 
-    def cp(out, a, R, Wr, e="V"):
-        if e == "V":
-            op("V", lambda q: q.tensor_copy(out, a), R, Wr)
-        else:
-            op("S", lambda q: q.activation(out, a, F.Copy), R, Wr)
+    def cp(n, out, a, R, Wr):
+        add(P, n if isinstance(n, dict) else {"V": plain(n)}, lambda q, e: q.tensor_copy(out, a) if e == "V" else q.activation(out, a, F.Copy), R, Wr)
 
-    def act(out, a, f, R, Wr, bias=0.0, scale=1.0):
-        op("S", lambda q: q.activation(out, a, f, bias=bias, scale=scale), R, Wr)
+    def lin(c, out, a, scale, bias, R, Wr):
+        add(P, c, lambda q, e: q.tensor_scalar(out, a, scale, bias, A.mult, A.add) if e == "V" else q.activation(out, a, F.Identity, bias=bias, scale=scale), R, Wr)
 
-    def mm(items, R, Wr, start=True, stop=True):
-        n = len(items)
-        op("P", lambda q: [q.matmul(o, l, r, start and i == 0, stop and i == n - 1) for i, (o, l, r) in enumerate(items)], R, Wr)
+    def relu(c, out, a, bias, R, Wr):
+        add(P, c, lambda q, e: q.tensor_scalar(out, a, bias, 0.0, A.add, A.max) if e == "V" else q.activation(out, a, F.Relu, bias=bias), R, Wr)
 
-    def scan(out, a, b, o0, o1, R, Wr):
-        op("V", lambda q: q.tensor_tensor_scan(out, a, b, 0.0, o0, o1), R, Wr)
+    def act(c, out, a, f, R, Wr):
+        add(P, {"S": c}, lambda q, e: q.activation(out, a, f), R, Wr)
 
-    def fill(ap, c, Wr):
-        op("V", lambda q: q.memset(ap, c), "", Wr)
+    def mm(n, items, R, Wr, start=True, stop=True):
+        m = len(items)
+        c = PE * (sum(max(64, x) for x in n) if isinstance(n, list) else m * max(64, n))
+        add(P, {"P": c}, lambda q, e: [q.matmul(o, l, r, start and i == 0, stop and i == m - 1) for i, (o, l, r) in enumerate(items)], R, Wr, 0, None, start, stop)
 
-    def iota(ap, pat, base, cm, Wr, flt=True):
+    def scan(n, out, a, b, o0, o1, R, Wr):
+        add(P, {"V": plain(n)}, lambda q, e: q.tensor_tensor_scan(out, a, b, 0.0, o0, o1), R, Wr)
+
+    def turn(n, out, a, R, Wr):
+        add(P, {"V": plain(n)}, lambda q, e: q.transpose(out, a), R, Wr)
+
+    def fill(n, ap, c, Wr):
+        add(P, {"V": plain(n)}, lambda q, e: q.memset(ap, c), "", Wr)
+
+    def iota(n, ap, pat, base, cm, Wr, flt=True):
         if flt:
-            op("G", lambda q: q.iota(ap, pat, base, cm, allow_small_or_imprecise_dtypes=True), "", Wr)
+            add(P, {"G": 160 + 2 * n}, lambda q, e: q.iota(ap, pat, base, cm, allow_small_or_imprecise_dtypes=True), "", Wr)
         else:
-            op("G", lambda q: q.iota(ap, pat, base, cm), "", Wr)
+            add(P, {"G": 160 + 2 * n}, lambda q, e: q.iota(ap, pat, base, cm), "", Wr)
+
+    def remote(items, sem, R, Wr, c=350):
+        def fn(q, e):
+            send(g, T, topo, core, items, sem)
+        add(P, {"G": c}, fn, R, Wr)
+        return sum(len(it[1]) for it in items)
+
+    big = []
+
+    def after(lag):
+        k = len(P["ops"]) - 1
+        if len(big) >= lag:
+            P["ops"][k]["dep"].setdefault(big[-lag], False)
+        big.append(k)
 
     C = lambda k: T.col[:, k:k + 1]
-    Z = lambda k, n: T.z[:, k, 0:n]
+    Z = lambda k, n=16: T.z[:, k, 0:n]
     SR = [T.S0, T.S1, T.S2, T.S3]
     SHR, AND = A.logical_shift_right, A.bitwise_and
+    span = lambda s, a, b: " ".join("%s%d" % (s, k) for k in range(a, b))
+    each = lambda s, n: " ".join(s % k for k in range(n))
 
     dma("Y", T.W[:, 0:GH], T.x[:, 0:GH], "", "Wa")
     dma("S", T.rq[:], T.req[:], "", "rq")
     dma("S", T.thi[:, 0:1], T.th[:], "", "thi")
-    dma("Y", T.nbi[:, 0:V], T.nb[:], "", "nbi")
-    dma("Y", T.pti[:], T.pt[:], "", "pti")
-    dma("Y", T.W[:, GH:V], T.x[:, GH:V], "", "Wb")
-    iota(T.coli[:, 0:1], [[0, 1]], 0, 1, "coli", False)
-    iota(T.row[:], [[1, 144]], 0, 0, "row")
-    iota(T.rowj[:], [[0, 8], [1, 16]], 0, 0, "rowj")
-    iota(T.rowg[:], [[1, 8], [0, 16]], 0, 0, "rowg")
-    iota(T.wi[:, 0:2], [[128, 2]], 0, 1, "wi0")
-    iota(T.wi[:, 16:32], [[16, 16]], 0, 0, "wi1")
-    iota(T.offc[:], [[512, 8], [16, 2]], 0, 0, "offc", False)
-    deps("G", ["Wa"], [])
+    dma("Y", T.nbi[:, 0:V], T.nb[:], "", "nbi", 2)
+    iota(1, T.coli[:, 0:1], [[0, 1]], 0, 1, "coli", False)
+    iota(144, T.row[:], [[1, 144]], 0, 0, "row")
+    iota(128, T.rowj[:], [[0, 8], [1, 16]], 0, 0, "rowj")
+    iota(128, T.rowg[:], [[1, 8], [0, 16]], 0, 0, "rowg")
+    iota(2, T.wi[:, 0:2], [[128, 2]], 0, 1, "wi0")
+    iota(16, T.wi[:, 16:32], [[16, 16]], 0, 0, "wi1")
+    iota(64, T.tba[:], [[1, 8], [0, 8]], 0, 0, "tba")
+    iota(64, T.tbb[:], [[0, 8], [1, 8]], 8, 0, "tbb")
     chip = topo.engines(core, hands[0])
     per = len(chip) // len(hands)
     wd = GH // len(hands)
-    l0 = send(g, T, topo, core, [(h, chip[i * per:(i + 1) * per], "hx", T.W[:, i * wd:(i + 1) * wd], T.HB[:, 0:wd]) for i, h in enumerate(hands)], "l0")
     out_e = topo.engines(core, T.cores[near[0]])
+    l0 = remote([(h, chip[i * per:(i + 1) * per], "hx", T.W[:, i * wd:(i + 1) * wd], T.HB[:, 0:wd]) for i, h in enumerate(hands)], "l0", "Wa", "out0", 1300)
     for q in near:
         d = (q - rank) % N
         a = V + (d - 1) * GH
-        l0 += send(g, T, topo, core, [(T.cores[q], out_e, "xg%d" % d, T.W[:, 0:GH], T.W[:, a:a + GH])], "l0")
+        l0 += remote([(T.cores[q], out_e, "xg%d" % d, T.W[:, 0:GH], T.W[:, a:a + GH])], "l0", "Wa", "out1")
+    iota(16, T.offc[:], [[512, 8], [16, 2]], 0, 0, "offc issued", False)
+    dma("Y", T.pti[:], T.pt[:], "issued", "pti", 1.5)
+    dma("Y", T.W[:, GH:V], T.x[:, GH:V], "", "Wb", 2)
     for d in range(1, N):
         q = (rank - d) % N
         nq, fq, hq, _c = ways(T, topo, q)
-        lands("xg%d" % d, len(out_e) if rank in nq else len(hq) * (len(topo.engines(hq[0], core)) // len(fq)), "W%d" % d)
-    lands("l0", l0, "sent")
-    fill(T.Rc[:], 0.0, "Rc")
-    iota(T.tba[:], [[1, 8], [0, 8]], 0, 0, "tba")
-    iota(T.tbb[:], [[0, 8], [1, 8]], 8, 0, "tbb")
-    op("G", lambda q: q.affine_select(T.Rc[:], T.Rc[:], [[16, 8], [1, 8], [0, 8]], A.not_equal, 1.0, 0, -1), "Rc", "Rc")
-    op("G", lambda q: q.affine_select(T.Rc[:], T.Rc[:], [[16, 8], [0, 8], [1, 8]], A.not_equal, 1.0, 8, -1), "Rc", "Rc")
-    iota(T.AW[:], [[0, 2048]], 0, 0, "AW0 AW1")
-    iota(T.bci[:], [[1, 32]], 0, 0, "bci", False)
-    iota(T.mpa[:], [[16, 64]], 1040, 0, "mpa")
-    iota(T.dc[:], [[1, 3], [0, 16]], 2, 0, "dc")
-    iota(T.tcf[:], [[4, 5], [1, 4], [0, 16]], -8, 0, "tcf")
+        lands("xg%d" % d, len(out_e) if rank in nq else len(hq) * (len(topo.engines(hq[0], core)) // len(fq)), "out0 out1",
+              "W%d0 W%d1" % (d, d), NEAR0 if rank in nq else FAR0)
+    lands("l0", l0, "out0 out1", "sent", 1)
+    fill(256, T.Rc[:], 0.0, "Rc")
+    add(P, {"G": 1230}, lambda q, e: q.affine_select(T.Rc[:], T.Rc[:], [[16, 8], [1, 8], [0, 8]], A.not_equal, 1.0, 0, -1), "Rc", "Rc")
+    add(P, {"G": 1230}, lambda q, e: q.affine_select(T.Rc[:], T.Rc[:], [[16, 8], [0, 8], [1, 8]], A.not_equal, 1.0, 8, -1), "Rc", "Rc")
+    iota(16, T.bci[:, 0:16], [[1, 16]], 0, 0, "bci0", False)
+    iota(16, T.bci[:, 16:32], [[4, 16]], 3, 0, "bci1", False)
+    iota(64, T.mp[:], [[16, 64]], 1040, 0, "mp")
+    iota(48, T.dc[:], [[1, 3], [0, 16]], 2, 0, "dc")
+    iota(320, T.tcf[:], [[4, 5], [1, 4], [0, 16]], -8, 0, "tcf")
+    iota(256, T.taf[:], [[1, 16], [0, 16]], 0, 0, "taf")
+    iota(1024, T.AW[:, 64:128, :], [[0, 1024]], 0, 0, "AW1")
+    fill(512, T.AW[:, 0:64, :], 0.0, "AW0")
 
-    ts(T.coli[:, 1:2], T.coli[:, 0:1], 15, None, AND, None, "coli", "coli1")
-    ts(T.coli[:, 2:3], T.coli[:, 0:1], 4, None, SHR, None, "coli", "coli2")
-    ts(T.coli[:, 3:4], T.coli[:, 0:1], 4, 1, SHR, AND, "coli", "coli3")
-    cp(T.col[:, 0:4], T.coli[:, 0:4], "coli coli1 coli2 coli3", "col")
-    ts(T.id32[:], T.row[:, 0:128], C(0), None, A.is_equal, None, "row col", "id32")
-    ts(T.ta[:, 0:128], T.rowj[:], C(1), None, A.is_equal, None, "rowj col", "ta")
-    for nm, sc in (("id12", 2.0 ** -12), ("idb", 1.0), ("id8", 8.0), ("idB", 32768.0), ("idm", -255.0)):
-        act(T[nm][:], T.id32[:], F.Identity, "id32", nm, scale=sc)
+    ts(1, T.coli[:, 1:2], T.coli[:, 0:1], 15, None, AND, None, "coli", "coli1")
+    ts(1, T.coli[:, 2:3], T.coli[:, 0:1], 4, None, SHR, None, "coli", "coli2")
+    ts(1, T.coli[:, 3:4], T.coli[:, 0:1], 4, 1, SHR, AND, "coli", "coli3")
+    cp(4, T.col[:, 0:4], T.coli[:, 0:4], "coli coli1 coli2 coli3", "col")
+    ts(128, T.id32[:], T.row[:, 0:128], C(0), None, A.is_equal, None, "row col", "id32")
+    ts(128, T.ta[:, 0:128], T.rowj[:], C(1), None, A.is_equal, None, "rowj col", "ta")
+    for nm, sc in (("id12", 2.0 ** -12), ("idb", 1.0), ("id4", 4.0), ("idB", 32768.0), ("idm", -255.0)):
+        lin(both(128), T[nm][:], T.id32[:], sc, 0.0, "id32", nm)
     for w in (128, 256, 512):
-        cp(T.ta[:, w:2 * w], T.ta[:, 0:w], "ta", "ta", "S")
-    ts(C(4), C(3), -1.0, 1.0, A.mult, A.add, "col", "col4")
-    ts(C(5), C(0), 16.0, None, A.add, None, "col", "col5")
-    ts(C(6), C(0), -16.0, None, A.add, None, "col", "col6")
-    ts(C(7), C(2), 16.0, 15.0, A.mult, A.add, "col", "col7")
-    ts(T.BOc[:], T.rowj[:], -1.0 / 16, 61.0 / 64, A.mult, A.add, "rowj", "BOc")
-    ts(C(9), C(1), 32.0, None, A.mult, None, "col", "col9")
-    ts(T.wi[:, 16:32], T.wi[:, 16:32], C(1), -LNB, A.add, A.mult, "wi1 col", "wi1")
-    ts(T.wi[:, 0:2], T.wi[:, 0:2], -LNB, LN0, A.mult, A.add, "wi0", "wi0")
-    ts(T.wi[:, 16:32], T.wi[:, 16:32], LN0 + math.log(2.53), None, A.add, None, "wi1", "wi1")
+        cp(both(w, 0.5), T.ta[:, w:2 * w], T.ta[:, 0:w], "ta", "ta")
+    for k, a, sc, off in ((4, 3, -1.0, 1.0), (5, 0, 1.0, 16.0), (6, 0, 1.0, -16.0), (7, 2, 16.0, 15.0), (8, 1, 16.0, 0.0), (9, 1, 32.0, 0.0), (15, 1, 1.0, -1024.0)):
+        lin(both(1), C(k), C(a), sc, off, "col", "col%d" % k)
+    ts(1, C(16), C(1), 15.0, None, A.is_equal, None, "col", "col16")
+    lin(both(128), T.BOc[:], T.rowj[:], -1.0 / 16, 61.0 / 64, "rowj", "BOc")
+    ts(16, T.wi[:, 16:32], T.wi[:, 16:32], C(1), -LNB, A.add, A.mult, "wi1 col", "wi1")
+    ts(2, T.wi[:, 0:2], T.wi[:, 0:2], -LNB, LN0, A.mult, A.add, "wi0", "wi0")
+    ts(16, T.wi[:, 16:32], T.wi[:, 16:32], LN0 + math.log(2.53), None, A.add, None, "wi1", "wi1")
     for k, (a, b) in enumerate(((0, 4), (5, 4), (6, 3), (0, 3))):
-        ts(T.SWb[:, k, :], T.row[:, 0:128], C(a), C(b), A.is_equal, A.mult, "row col col4 col5 col6", "SW%d" % k)
-    act(T.thr[:], T.wi[:, 16:32], F.Exp, "wi1", "thr")
-    act(T.wcol[:], T.wi[:, 0:2], F.Exp, "wi0", "wcol")
-    act(T.SWs[:], T.SWb[:], F.Identity, "SW0 SW1 SW2 SW3", "SWs", scale=2.0 ** -16)
-    fill(T.rmin[:], 0.0, "rmin")
-    fill(T.ta[:, V:V + 16], 0.0, "taz")
-    fill(T.rmin[:, 0:256:16], 1024.0, "rmin")
-    ts(T.BO[:], T.rowg[:], C(2), None, A.is_equal, None, "rowg col", "BO")
-    act(T.rmax[:], T.rmin[:], F.Identity, "rmin", "rmax", scale=-1.0)
-    ts(C(15), C(1), -1024.0, None, A.add, None, "col", "col15")
-    cp(T.tn[:, 0:16], T.ta[:, 0:16], "ta", "tn0", "S")
-    act(T.tn[:, 16:32], T.ta[:, 0:16], F.Identity, "ta", "tn1", scale=-1.0)
-    tt(T.BOc[:], T.BOc[:], T.BO[:], A.mult, "BOc BO", "BOc")
-    ts(T.Cm[:], T.BO[:], C(15), None, A.mult, None, "BO col15", "Cm")
-    act(T.nBO[:], T.BO[:], F.Identity, "BO", "nBO", scale=-1.0)
-    ts(T.tri[:], T.rowj[:], C(1), -1.0, A.is_le, A.mult, "rowj col", "tri")
-    ts(T.EE[:], T.row[:], C(7), None, A.is_equal, None, "row col7", "EE")
-    tt(T.tri[:], T.tri[:], T.BO[:], A.mult, "tri BO", "tri")
-    fill(T.L0[:], 0, "L0")
-    fill(T.nbi[:, V:V + 16], 0, "pad0")
-    fill(T.pli[:, V:V + 16], 0, "pad1")
-    fill(T.cst[:, V:V + 16], 0.0, "pad2")
-    tt(T.tri[:], T.tri[:], T.idm[:], A.add, "tri idm", "tri")
-    fill(T.L0[:, 23:24], 64, "L0")
-    ts(T.offc[:], T.offc[:], C(9), None, A.add, None, "offc col9", "offc")
-    fill(T.L0[:, 32:48], V + 8, "L0")
-    fill(T.ta[:, V:V + 1], 1.0, "taz")
-    fill(T.FZ[:], 0.0, "FZ")
-    fill(T.Ms[:], BIG, "Ms")
-    fill(T.tb[:], 0.0, "tb")
-    fill(T.BAN[:], 0.0, "BAN0 BAN1")
-    fill(T.rrk[:], 1.0, "rrk")
-    fill(T.r3[:], 0.0, "r3")
-    fill(T.rrk[:, 0:48:8], 0.0, "rrk")
-    fill(T.r3[:, 0:48:3], 1024.0, "r3")
+        ts(128, T.SWb[:, k, :], T.row[:, 0:128], C(a), C(b), A.is_equal, A.mult, "row col col4 col5 col6", "SW%d" % k)
+    act(1600, T.wcol[:], T.wi[:, 0:2], F.Exp, "wi0", "wcol")
+    act(100, T.thr[:], T.wi[:, 16:32], F.Exp, "wi1 wcol", "thr")
+    lin(both(512, 0.5), T.SWs[:], T.SWb[:], 2.0 ** -16, 0.0, "SW0 SW1 SW2 SW3", "SWs")
+    fill(256, T.rmin[:], 0.0, "rmin")
+    fill(16, T.rmin[:, 0:256:16], 1024.0, "rmin")
+    fill(16, T.ta[:, V:V + 16], 0.0, "taz")
+    fill(1, T.ta[:, V:V + 1], 1.0, "taz")
+    ts(128, T.BO[:], T.rowg[:], C(2), None, A.is_equal, None, "rowg col", "BO")
+    lin(both(256), T.rmax[:], T.rmin[:], -1.0, 0.0, "rmin", "rmax")
+    tt(256, T.BOc[:], T.BOc[:], T.BO[:], A.mult, "BOc BO", "BOc")
+    lin(both(128, 0.5, S16), T.Cm1[:], T.BO[:], C(15), 0.0, "BO col15", "Cm1")
+    lin(both(128, 0.5), T.Cm0[:], T.BO[:], C(8), 0.0, "BO col8", "Cm0")
+    ts(64, T.idB1[:], T.BO[:], C(16), 1040.0, A.mult, A.mult, "BO col16", "idB1")
+    tt(256, T.idB1[:], T.idB1[:], T.idB[:], A.max, "idB1 idB", "idB1")
+    lin(both(128, 0.5), T.nBO[:], T.BO[:], -1.0, 0.0, "BO", "nBO")
+    lin(both(128, 0.5), T.BOK[:], T.BO[:], 4096.0, 0.0, "BO", "BOK")
+    lin(both(256, 0.5), T.THD[:], T.ta[:, 0:256], 816.0, -1024.0, "ta", "THD")
+    ts(128, T.tri[:], T.rowj[:], C(1), -1.0, A.is_le, A.mult, "rowj col", "tri")
+    ts(144, T.EE[:], T.row[:], C(7), None, A.is_equal, None, "row col7", "EE")
+    tt(256, T.tri[:], T.tri[:], T.BO[:], A.mult, "tri BO", "tri")
+    tt(256, T.tri[:], T.tri[:], T.idm[:], A.add, "tri idm", "tri")
+    fill(24, T.L0[:], 0, "L0")
+    fill(1, T.L0[:, 23:24], 64, "L0")
+    fill(8, T.L0[:, 32:48], V + 8, "L0")
+    fill(16, T.nbi[:, V:V + 16], 0, "pad0")
+    fill(16, T.pli[:, V:V + 16], 0, "pad1")
+    fill(16, T.cst[:, V:V + 16], 0.0, "pad2")
+    ts(16, T.offc[:], T.offc[:], C(9), None, A.add, None, "offc col9", "offc")
+    fill(32, T.FZ[:], 0.0, "FZ")
+    fill(80, T.Ms[:], BIG, "Ms")
+    fill(80, T.tb[:], 0.0, "tb")
+    fill(64, T.BAN[:, 0:96], 0.0, span("BAN_", 0, 6))
+    fill(128, T.zer[:], 0.0, "zer")
+    fill(128, T.on12[:], 2.0 ** -12, "on12")
+    fill(24, T.rrk[:], 1.0, "rrk")
+    fill(3, T.rrk[:, 0:48:16], 0.0, "rrk")
+    fill(64, T.r4[:], 0.0, "r4")
+    fill(16, T.r4[:, 0:64:4], 1024.0, "r4")
+    fill(16, T.dI[:], 0, "dI")
+    fill(8, T.gd[:], 0.0, "gd")
     for s in range(4):
-        fill(SR[s][:, 0:16], 0.0, "Sz%d" % s)
-    ts(T.rqb[:], T.rq[:], 4, None, SHR, None, "rq", "rqb")
-    cp(C(10), T.thi[:, 0:1], "thi", "col10")
+        fill(8, SR[s][:, 0:16], 0.0, "Sz%d" % s)
+    ts(28, T.rqb[:], T.rq[:], 4, None, SHR, None, "rq", "rqb")
+    cp(1, C(10), T.thi[:, 0:1], "thi", "col10")
 
     def requests(t):
-        cp(T.L0[:, 0:7], T.rq[:, 7 * t:7 * t + 7], "rq L0", "Ls0")
-        cp(T.L0[:, 16:23], T.rqb[:, 7 * t:7 * t + 7], "rqb L0", "Lb0")
+        cp(7, T.L0[:, 0:7], T.rq[:, 7 * t:7 * t + 7], "rq L0", "Ls0")
+        cp(7, T.L0[:, 16:23], T.rqb[:, 7 * t:7 * t + 7], "rqb L0", "Lb0")
     requests(0)
-    ts(C(13), C(10), 2048.0, 2.0 ** -17, A.is_ge, A.mult, "col10", "col13")
-    ts(C(12), C(10), 2.0 ** -12, 2.0 ** -13, A.mult, A.add, "col10", "col12")
-    ts(C(14), C(1), 2.0 ** -16, 8.0, A.mult, A.add, "col", "col14")
-    ts(T.tba[:], T.tba[:], C(1), None, A.is_equal, None, "tba col", "tba")
-    tt(C(11), C(14), C(13), A.add, "col14 col13", "col11")
-    ts(T.tbb[:], T.tbb[:], C(1), None, A.is_equal, None, "tbb col", "tbb")
-    tt(T.tb[:, 0:64], T.tba[:], T.tbb[:], A.add, "tba tbb", "tb")
-    ts(T.cst[:, 0:V], T.pti[:], 1.5 * 2.0 ** 34, 1.5 * 2.0 ** 34, A.add, A.subtract, "pti", "cst")
-    ts(T.pli[:, 0:V], T.pti[:], 2047, None, AND, None, "pti", "pli")
+    ts(1, C(13), C(10), 2048.0, 2.0 ** -17, A.is_ge, A.mult, "col10", "col13")
+    lin(both(1), C(14), C(1), 2.0 ** -16, C(13), "col col13", "col14")
+    lin(both(1), C(11), C(10), 2.0 ** -12, C(14), "col10 col14", "col11")
+    lin(both(1), C(12), C(10), -1.0, 2048.0, "col10", "col12")
+    lin(both(128, 1.0, S16), T.thM[:], T.id32[:], C(12), -16.0, "id32 col12", "thM")
+    ts(64, T.tba[:], T.tba[:], C(1), None, A.is_equal, None, "tba col", "tba")
+    ts(64, T.tbb[:], T.tbb[:], C(1), None, A.is_equal, None, "tbb col", "tbb")
+    tt(128, T.tb[:, 0:64], T.tba[:], T.tbb[:], A.add, "tba tbb tb", "tb")
+    for u in range(2):
+        a, b = u * GH, u * GH + GH
+        ts(GH, T.cst[:, a:b], T.pti[:, a:b], 1.5 * 2.0 ** 34, 1.5 * 2.0 ** 34, A.add, A.subtract, "pti", "cst%d" % u)
+        ts(GH, T.pli[:, a:b], T.pti[:, a:b], 2047, None, AND, None, "pti", "pli%d" % u)
+    cp(512, T.AF[:, 0:64, :], T.AW[:, 64:128, :], "AW1", "AF0")
+    cp(32, T.bc[:], T.bci[:], "bci0 bci1", "bc")
+    lin(both(64), T.mp[:], T.mp[:], 1.0, C(1), "mp col", "mp")
+    ts(4, T.rep[:], T.rowg[:, 0:4], C(1), None, A.add, None, "rowg col", "rep")
+    ts(320, T.tc[:, 0:320], T.tcf[:], C(1), None, A.is_equal, None, "tcf col", "tc")
+    ts(160, T.tc[:, 320:640], T.tc[:, 0:320], C(16), None, A.max, None, "tc col16", "tc1")
+    ts(256, T.ta[:, V + 16:V + 272], T.taf[:], C(1), None, A.is_equal, None, "taf col", "tao")
+    for d in range(1, N):
+        dma("Y", SR[d][:, 1040:1552], T.W[:, V + (d - 1) * GH:V + d * GH], "W%d0 W%d1" % (d, d), "Sx%d" % d)
+    for u in range(1, 4):
+        dma("Y", T.AF[:, 64 * u:64 * u + 64, :], T.AF[:, 0:64, :], "AF0", "AF%d" % u)
+    dma("Y", T.S0[:, 1040:2064], T.x[:], "", "Sx0", 2)
+    for d in range(N):
+        dma("Y", SR[d][:, 16:1040], T.plans[:], "", "Sp%d" % d, 2 + 0.5 * d)
 
-    def later():
-        cp(T.AF[:, 0:64, :], T.AW[:, 64:128, :], "AW1", "AF0")
-        cp(T.bc[:], T.bci[:], "bci", "bc")
-        ts(T.mp[:], T.mpa[:], C(1), None, A.add, None, "mpa col", "mp")
-        ts(T.rep[:], T.rowg[:, 0:4], C(1), None, A.add, None, "rowg col", "rep")
-        ts(T.tc[:], T.tcf[:], C(1), None, A.is_equal, None, "tcf col", "tc")
-        for u in range(1, 4):
-            dma("Y", T.AF[:, 64 * u:64 * u + 64, :], T.AF[:, 0:64, :], "AF0", "AF%d" % u)
-        for d in range(1, N):
-            dma("Y", SR[d][:, 1040:1552], T.W[:, V + (d - 1) * GH:V + d * GH], "W%d" % d, "Sx%d" % d)
-        dma("Y", T.S0[:, 1040:2064], T.x[:], "", "Sx0")
-        for d in range(N):
-            dma("Y", SR[d][:, 16:1040], T.plans[:], "", "Sp%d" % d)
-
-    WALL = "Wa Wb W1 W1b W2 W3"
-    LS, LB, LC = "Ls0 Ls1 pad0 pad1 pad2", "Lb0 Lb1", "L0 Lc1"
+    WALL = "Wa Wb W10 W11 W20 W21 W30 W31"
+    TA = "ta taz "
+    ta = T.ta[:, 0:V + 16]
 
     def to_list(out, bank, src, L, key):
-        mm([(out, T.EE[:, 15 - j:143 - j], src[:, j:L:16]) for j in range(16)], "EE " + key, bank)
+        mm(16, [(out, T.EE[:, 15 - j:143 - j], src[:, j:L:16]) for j in range(16)], "EE " + key, bank)
 
-    def marks_1(t, NB, sl, bl, sk, bk):
-        L = 32 * NB
+    def marks_1(t, NH, sl, bl, b0, sk, bk):
         AR = T["AR%d" % t]
-        cp(T.FB[:, 0:L], T.tb[:].indirect(bl), "tb " + bk, "FB", "S")
-        cp(AR[:, 0:L], T.ta[:].indirect(sl), "ta taz " + sk, "AR%d" % t, "S")
-        for h in range(L // 128):
-            mm([(T["pB%d" % h][:], T.FB[:, 128 * h:128 * h + 128], T.Rc[:])], "FB Rc", "pB%d" % h)
-        for h in range(L // 128):
-            mm([(T.pA[:, 128 * h:128 * h + 128], AR[:, 128 * h:128 * h + 128], T.idb[:])], "idb AR%d" % t, "pA")
-        one_b(t, 0)
-        for h in range(L // 128):
-            act(T.AW[:, 64 * h:64 * h + 64:8, :], T.pA[:, 128 * h:128 * h + 128], F.Identity, "pA wcol", "AW%d" % h, scale=T.wcol[:, h:h + 1])
+        cp(gath(128 * NH), T.FB[:, 0:128 * NH], T.tb[:].indirect(bl[:, b0:b0 + 8 * NH]), "tb " + bk, "FB")
+        cp(gath(128 * NH), AR[:, 0:128 * NH], ta.indirect(sl[:, 0:8 * NH]), TA + sk, each("AR%d%%d" % t, NH))
+        for h in range(NH):
+            a, b = 128 * h, 128 * h + 128
+            mm(512, [(T["pB%d" % h][:], T.FB[:, a:b], T.Rc[:])], "FB Rc", "pB%d.a pB%d.b" % (h, h))
+            mm(128, [(T.pA[:, a:b], AR[:, a:b], T.idb[:])], "idb AR%d%d" % (t, h), "pA.a%d" % h)
+            relu(both(512), T["B%d" % t][:, 512 * h:512 * h + 512], T["pB%d" % h][:], -1.0, "pB%d.a pB%d.b" % (h, h), "B%d%d" % (t, h))
+            lin(both(128), T.AW[:, 64 * h:64 * h + 64:8, :], T.pA[:, a:b], T.wcol[:, h:h + 1], 0.0, "pA.a%d wcol" % h, "AW%d" % h)
 
-    def one_b(t, h):
-        act(T["B%d" % t][:, 512 * h:512 * h + 512], T["pB%d" % h][:], F.Relu, "pB%d" % h, "B%d%d" % (t, h), bias=-1.0)
-
-    def marks_2(t, NB):
-        L = 32 * NB
+    def marks_2(t, NH, bl, bk):
+        L, n = 128 * NH, 8 * NH
         B = T["B%d" % t]
-        for h in range(L // 128):
-            mm([(T.pM[:, 0:64], T.AW[:, 64 * h + 7 * k:64 * h + 7 * k + 8, :], B[:, 512 * h + 64 * k:512 * h + 64 * k + 64]) for k in range(8)],
-               "AW%d B%d%d" % (h, t, h), "pM", h == 0, h == L // 128 - 1)
-
-    def marks_3(t, NB, bl, bk):
-        L, n = 32 * NB, 2 * NB
-        tt(T.Ms[:, 0:64], T.pM[:, 0:64], (T.FZ if t == 0 else T.MK)[:], A.add, "pM FZ MK", "Ms")
-        tt(T.LK[:, 0:L], T.Ms[:].indirect(bl), T["AR%d" % t][:, 0:L], A.mult, "Ms AR%d " % t + bk, "LK")
-        to_list(T.pS[:, 0, 0, 0:n], "pS", T.LK, L, "LK")
-
-    def reached(t, n):
-        tt(Z(1 + t, n), T.pS[:, 0, 0, 0:n], T.thr[:, 0:n], A.is_lt, "pS thr", "got%d" % t)
-        tt(Z(9 + t, n), Z(1 + t, n), Z(7 + t, n), A.mult, "got%d st%d" % (t, t), "gs%d" % t)
-
-    def plan(t, NB, S16, sk):
-        L, n = 32 * NB, 2 * NB
-        tt(T.PL[:, 0:L], T.pli[:].indirect(S16[:, 0:n]), T["OH%d" % t][:, 0:L], A.mult, "pli OH%d " % t + sk, "PL")
-        if t == 1:
-            to_list(T.pT[:, 64:64 + n], "pT", T.PL, L, "PL")
-            act(Z(4, n), T.pT[:, 64:64 + n], F.Identity, "pT", "pl1", bias=16.0)
-
-    def near_of(S16, sk, NB, v, a, b):
-        cp(T.Q[:, 32 * a + v:32 * b:2], T.nbi[:].indirect(S16[:, NB * v + a:NB * v + b]), "nbi " + sk, "Q%d" % v)
-
-    def cost_of(S16, sk, NB, v, a, b):
-        act(T.CK[:, 32 * a + v:32 * b:2], T.cst[:].indirect(S16[:, NB * v + a:NB * v + b]), F.Identity, "cst col11 " + sk, "CK%d" % v, bias=C(11), scale=2.0 ** -23)
-
-    def step(t, NB, S16, sk, ban, hook):
-        L, n = 32 * NB, 2 * NB
-        run = lambda k: hook.get(k, lambda: None)()
-        a0 = 6 if "head" in hook else 0
-        near_of(S16, sk, NB, 0, a0, NB)
-        near_of(S16, sk, NB, 1, 0, NB)
-        run("head")
-        cost_of(S16, sk, NB, 0, a0, NB)
-        cost_of(S16, sk, NB, 1, 0, NB)
-        run("early")
-        onv = ONV[(NB, t)]
-        done = []
-        kq = T.pQ[:, 0:NB, :, :]
-
-        def turn(a, b):
-            keys = range(a, b)
-            op("V", lambda q: q.transpose(T.GT[:, 512 * a:512 * b], T.G[:, 512 * a:512 * b]), " ".join("G%d" % k for k in keys), " ".join("GT%d" % k for k in keys))
-            done.extend(keys)
-        for b in range(NB):
-            cp(T.G[:, 512 * b:512 * b + 512], T.W[:].indirect(T.Q[:, 32 * b:32 * b + 32]), WALL + " Q0 Q1", "G%d" % b, "V" if b in onv else "S")
-            if b == 0:
-                ts(T.Qf[:, 0:L], T.Q[:, 0:L], -1024.0, None, A.add, None, "Q0 Q1", "Qf")
-            run(b)
-            if b % 2 == 1:
-                k = b // 2
-                if k == 0:
-                    mm([(T.pX[:, 0:L], T.id32[:], T.CK[:, 0:L])], "id32 CK0 CK1", "pX", True, False)
-                if b == NB - 1 and ban is not None:
-                    mm([(T.pX[:, 0:L], T.id8[:], T[ban][:, 0:L])], "id8 %s0 %s1" % (ban, ban), "pX", False, False)
-                mm([(T.pX[:, 64 * k:64 * k + 64], T.id12[:], T.G[:, 1024 * k + i:1024 * k + 1024:16]) for i in range(16)], "id12 G%d G%d" % (b - 1, b), "pX", False, b == NB - 1)
-            if b in onv and b - len(done) >= 2:
-                turn(len(done), b - 1 if b < NB - 1 else b)
-        act(T.TH[:, 0:L], T.CK[:, 0:L], F.Identity, "CK0 CK1 col12", "TH", bias=C(12))
-        run("gathered")
-        if len(done) < NB - 1:
-            turn(len(done), NB - 1)
-        turn(len(done), NB)
-        run("mid")
-        mm([(kq, T.BOc[:], T.ta[:, 0:L])] + [(T.pQ[:, 0:NB, e, :], T.SWs[:, 2 * e + v, :], T.Qf[:, v:L:2]) for e in range(2) for v in range(2)],
-           "BOc ta SWs Qf", "pQ", True, False)
-        tt(T.ov[:, 0:L], T.pX[:, 0:L], T.TH[:, 0:L], A.is_gt, "pX TH", "ov")
-        for v in range(2):
-            tt(T.kR[:, 0:NB, v, :], T.pX[:, v:L:2], T.ov[:, v:L:2], A.add, "pX ov", "kR%d" % v)
-        op("V", lambda q: q.transpose(T.kT[:, 0:L], T.kR[:, 0:NB, :, :]), "kR0 kR1", "kT")
-        scan(T.km[:, 0:L], T.rmin[:, 0:L], T.kT[:, 0:L], A.add, A.min, "rmin kT", "km")
-        ts(T.ki[:, 0:n], T.km[:, 15:L:16], 2.0 ** 17, None, A.mult, None, "km", "ki")
-        ts(T.ci[:, 0:n], T.ki[:, 0:n], 1, 15, SHR, AND, "ki", "ci")
-        ts(T.hh[:, 0:n], T.ki[:, 0:n], 1, None, AND, None, "ki", "hh")
-        tt(T.off[:, 0:n], T.ci[:, 0:n], T.offc[:, 0:n], A.add, "ci offc", "off")
-        cp(T.K1[:, 0:L], T.GT[:, 0:16 * L].indirect(T.off[:, 0:n]), " ".join("GT%d" % a for a in range(NB)) + " off", "K1", "S")
-        cp(T.CS[:, 0:n], T.ci[:, 0:n], "ci", "CS0")
-        ts(T.ht[:, 0:n], T.hh[:, 0:n], 65536.0, 131103.0 + 2.0 ** 20, A.mult, A.add, "hh", "ht")
-        tt(T.CS[:, 16:16 + n], T.ki[:, 0:n], T.ht[:, 0:n], A.is_gt, "ki ht", "CS1")
-        for f in range(2):
-            bank = ("pT", "pA")[f]
-            for v in range(2):
-                mm([(T[bank][:, 384 + NB * v:384 + NB * (v + 1)], T.SWb[:, 2 * v + e, :], T.CS[:, 16 * f + e:16 * f + n:2]) for e in range(2)], "SWs CS%d" % f, bank)
-        mm([(kq, T.idb[:], T.K1[:, 0:L])], "idb K1", "pQ", False, True)
-        cl = T["c%d" % t]
-        cp(cl[:, 0:n], T.pT[:, 384:384 + n], "pT", "cl%d" % t)
-        run("chosen")
-        if NB == 8:
-            one_b(t, 1)
-        marks_2(t, NB)
-        op("V", lambda q: q.transpose(T.K1T[:, 0:L], kq), "pQ", "K1T")
-        cp(Z(7 + t, n), T.pA[:, 384:384 + n], "pA", "st%d" % t, "S")
-        cp(T["OH%d" % t][:, 0:L], T.ta[:].indirect(cl[:, 0:n]), "ta taz cl%d" % t, "OH%d" % t, "S")
-        scan(T.bm[:, 0:L], T.rmax[:, 0:L], T.K1T[:, 0:L], A.add, A.max, "rmax K1T", "bm")
-        run("late")
-        for v in range(2):
-            ts(T.bi[:, NB * v:NB * (v + 1)], T.bm[:, 16 * v + 15:L:32], 65536.0, None, A.mult, None, "bm", "bi%d" % v)
+        for h in range(NH):
+            mm(64, [(T.pM[:, 0:64], T.AW[:, 64 * h + 7 * k:64 * h + 7 * k + 8, :], B[:, 512 * h + 64 * k:512 * h + 64 * k + 64]) for k in range(8)],
+               "AW%d B%d%d" % (h, t, h), "pM.w", h == 0, h == NH - 1)
+        tt(64, T.Ms[:, 0:64], T.pM[:, 0:64], (T.FZ if t == 0 else T.MK)[:], A.add, "pM.w " + ("FZ" if t == 0 else "MK"), "Ms")
+        tt(gath(L, "V"), T.LK[:, 0:L], T.Ms[:].indirect(bl), T["AR%d" % t][:, 0:L], A.mult, "Ms " + each("AR%d%%d" % t, NH) + " " + bk, "LK")
         if t == 0:
-            ts(T.si[:, 0:n], T.bi[:, 0:n], 1023, None, AND, None, "bi0 bi1", "si")
-            cp(T.s1[:, 0:n], T.si[:, 0:n], "si", "s1")
-        else:
-            ts(T.zi[:, 1, 0:n], T.bi[:, 0:n], 4095, None, AND, None, "bi0 bi1", "b1")
+            ts(32, T.MK[:], T.Ms[:, 0:64], 0.0, BIG, A.is_gt, A.mult, "Ms", "MK")
+        to_list(T.pS[:, 0, 0, 0:n], "pS.a", T.LK, L, "LK")
+        tt(16, Z(1 + t, n), T.pS[:, 0, 0, 0:n], T.thr[:, 0:n], A.is_lt, "pS.a thr", "got%d" % t)
 
-    def refresh(d, j, a, b, e, key):
-        at, m = V + (d - 1) * GH, 12 - 4 * (N - d)
-        cp(T.W[:, at + 16 * a:at + 16 * b], SR[d][:].indirect(T.IN[:, j, m + a:m + b]), "Sz%d Sp%d Sx%d IN%d" % (d, d, d, j), key, e)
-
-    for rnd in range(RO):
-        NB = 4 if rnd == 0 else 8
-        L, n, NH = 32 * NB, 2 * NB, NB // 4
-        last = rnd == RO - 1
-        sl0, bl0 = T.L0[:, 0:n], T.L0[:, 16:16 + n]
-        j0 = 3 * (rnd - 1)
-        INS = "IN%d IN%d IN%d" % (j0, j0 + 1, j0 + 2)
-        YB = [T.pX[:, 0:128], T.pQ[:, 0:4, :, :], T.pB0[:, 0:128], T.pB1[:, 0:128]]
-        YK = ("pX", "pQ", "pB0", "pB1")
-
-        def head0():
-            refresh(1, j0 + 2, 0, CUT, "V", "W1")
-            cp(T.L0[:, 39:48], T.IN[:, j0:j0 + 3, 56:59], "L0 " + INS, "Lc1")
-
-        def ban0():
-            cp(T.BAN[:, 192:256:2], T.ta[:].indirect(T.L0[:, 38:40]), "ta taz " + LC, "BAN0", "S")
-            cp(T.BAN[:, 1:256:2], T.ta[:].indirect(T.L0[:, 40:48]), "ta taz " + LC, "BAN1", "S")
-
-        def lists0():
-            cp(T.oi[:, 0:9], T.L0[:, 7:16], LS, "oi")
-            ts(T.oi[:, 0:9], T.oi[:, 0:9], 4, None, SHR, None, "oi", "oi")
-            cp(T.L0[:, 23:32], T.oi[:, 0:9], "L0 oi", "Lb1")
-
-        hook = {"mid": lambda: marks_1(0, NB, sl0, bl0, LS, LB)}
-        if rnd > 0:
-            hook.update({"head": head0, "early": ban0, 0: lists0})
-        else:
-            hook["gathered"] = later
-        step(0, NB, T.L0, LS, "BAN" if rnd > 0 else None, hook)
-
-        def after0a():
-            marks_3(0, NB, bl0, LB)
-            ts(T.zi[:, 0, 0:n], T.bi[:, 0:n], 4095, None, AND, None, "bi0 bi1", "b0")
-            ts(T.zi[:, 2, 0:n], T.bi[:, 0:n], 4, 255, SHR, AND, "bi0 bi1", "sb")
-            ts(T.MK[:], T.Ms[:, 0:64], 0.0, BIG, A.is_gt, A.mult, "Ms", "MK")
-
-        def after0b():
-            reached(0, n)
-            ts(Z(19, n), Z(9, n), -64.0, 64.0, A.mult, A.add, "gs0", "z19")
-            tt(Z(13, n), Z(9, n), T.zi[:, 0, 0:n], A.mult, "gs0 b0", "bg0")
-            tt(T.b1[:, 0:n], Z(19, n), T.zi[:, 2, 0:n], A.max, "z19 sb", "bl1")
-            ts(Z(15, n), Z(13, n), 1024.0, 16.0, A.is_ge, A.mult, "bg0", "ask0")
-            cp(Z(5, n), T.c0[:, 0:n], "cl0", "ch0")
-            tt(T.cb[:, 0:n], Z(15, n), Z(5, n), A.add, "ask0 ch0", "cb")
-            plan(0, NB, T.L0, LS)
-            tt(Z(11, n), Z(1, n), Z(9, n), A.subtract, "got0 gs0", "gd0")
-
-        def ban1():
+    def front(S, sk, cut, a, b):
+        for c0, nb in cut:
             for v in range(2):
-                cp(T.BN[:, v:L:2], T.tn[:].indirect(T.cb[:, NB * v:NB * (v + 1)]), "tn0 tn1 cb", "BN%d" % v, "S")
+                c = c0 + nb * v
+                lo, hi = max(a, c), min(b, c + nb)
+                if lo < hi:
+                    at = slice(16 * c0 + v + 32 * (lo - c), 16 * c0 + 32 * (hi - c), 2)
+                    cp(gath(16 * (hi - lo), S16), T.Q[:, at], T.nbi[:].indirect(S[:, lo:hi]), "nbi pad0 " + sk, span("Q", lo, hi))
+                    lin(gath(16 * (hi - lo)), T.CK[:, at], T.cst[:].indirect(S[:, lo:hi]), 2.0 ** -23, C(11), "cst0 cst1 pad2 col11 " + sk, span("CK", lo, hi))
 
-        def after0c():
-            to_list(T.pT[:, 64:64 + n], "pT", T.PL, L, "PL")
-            act(Z(22, n), Z(1, n), F.Identity, "got0", "q0", scale=0.25)
+    def chunk(t, h, c0, nb, on, ban):
+        n, m, L = 2 * nb, 16 * nb, 32 * nb
+        a, k0 = 16 * c0, c0 // 2
+        pC = T["pC%d" % h]
+        pX, kq = pC[:, 0:nb, :, :], pC[:, 8:8 + nb, :, :]
+        half = lambda v: pC[:, 0:nb, :, v:16:2]
+        K = lambda s: span(s, c0, c0 + n)
+        Kv = lambda s, v: span(s, c0 + nb * v, c0 + nb * v + nb)
+        X, KQ = "pC%d.x" % h, "pC%d.q" % h
+        lin(both(L, 0.5, S16), T.Qf[:, a:a + L], T.Q[:, a:a + L], 1.0, -1024.0, K("Q"), K("Qf"))
+        mm(L, [(pX, T.thM[:], T.on12[:, 0:L])], "thM on12", X, True, False)
+        for b in range(nb):
+            k = k0 + b
+            cp(gath(512, on[k].replace("-", "VS")), T.G[:, 512 * k:512 * k + 512], T.W[:].indirect(T.Q[:, 32 * k:32 * k + 32]),
+               WALL + " Q%d Q%d" % (c0 + b, c0 + nb + b), "G%d" % k)
+            after(LAG)
+            if b == nb - 1:
+                mm(4 * L, [(pX, T.id32[:], T.CK[:, a:a + L])], "id32 " + K("CK"), X, False, False)
+                if ban is not None:
+                    mm(m, [(half(v), T.id4[:], T[ban][:, a + m * v:a + m * v + m]) for v in range(2)], "id4 " + K(ban + "_"), X, False, False)
+            if b % 2 == 1:
+                mm(64, [(pC[:, b - 1:b + 1, :, :], T.id12[:], T.G[:, 512 * (k - 1) + i:512 * (k + 1):16]) for i in range(16)], "id12 G%d G%d" % (k - 1, k), X, False, b == nb - 1)
+            if b % CUTS == CUTS - 1:
+                r, w = 512 * (k + 1 - CUTS), 512 * CUTS
+                turn(w / 2, T.GT[:, r:r + w], T.G[:, r:r + w], span("G", k + 1 - CUTS, k + 1), span("GT", k + 1 - CUTS, k + 1))
+        tt(L, T.ov[:, a:a + L], pX, T.CK[:, a:a + L], A.is_gt, X + " " + K("CK"), K("ov"))
+        for v in range(2):
+            tt(m, T.kR[:, k0:k0 + nb, v, :], half(v), T.ov[:, a + v:a + L:2], A.add, X + " " + K("ov"), span("kR%d_" % v, k0, k0 + nb))
+        mm([L, m, m, m, m], [(kq, T.BOc[:], T.ta[:, 0:L])] + [(pC[:, 8:8 + nb, e, :], T.SWs[:, 2 * e + v, :], T.Qf[:, a + v:a + L:2]) for e in range(2) for v in range(2)],
+           "BOc ta SWs " + K("Qf"), KQ, True, False)
+        turn(L, T.kT[:, a:a + L], T.kR[:, k0:k0 + nb, :, :], span("kR0_", k0, k0 + nb) + " " + span("kR1_", k0, k0 + nb), K("kT"))
+        scan(L, T.km[:, a:a + L], T.rmin[:, 0:L], T.kT[:, a:a + L], A.add, A.min, "rmin " + K("kT"), K("km"))
+        cs = slice(c0, c0 + n)
+        lin(both(n, 1.0, S16), T.ki[:, cs], T.km[:, a + 15:a + L:16], 2.0 ** 17, 0.0, K("km"), K("ki"))
+        ts(n, T.ci[:, cs], T.ki[:, cs], 1, 15, SHR, AND, K("ki"), K("ci"))
+        tt(n, T.off[:, cs], T.ci[:, cs], T.offc[:, 0:n], A.add, "offc " + K("ci"), K("off"))
+        cp(gath(L), T.K1[:, a:a + L], T.GT[:, 16 * a:16 * (a + L)].indirect(T.off[:, cs]), span("GT", k0, k0 + nb) + " " + K("off"), K("K1_"))
+        mm(L, [(kq, T.idb[:], T.K1[:, a:a + L])], "idb " + K("K1_"), KQ, False, True)
+        turn(L, T.K1T[:, a:a + L], kq, KQ, K("K1T"))
+        scan(L, T.bm[:, a:a + L], T.rmax[:, 0:L], T.K1T[:, a:a + L], A.add, A.max, "rmax " + K("K1T"), K("bm"))
+        bi = T["bi%d" % t]
+        for v in range(2):
+            lin(both(nb, 1.0, S16), bi[:, c0 + nb * v:c0 + nb * v + nb], T.bm[:, a + 16 * v + 15:a + L:32], 65536.0, 0.0, K("bm"), Kv("bi%d_" % t, v))
+        if t == 0:
+            ts(n, T.zi[:, 5, cs], bi[:, cs], 1023, None, AND, None, K("bi0_"), K("si"))
+            cp(both(n, 1.0, S16), T.s1[:, cs], T.zi[:, 5, cs], K("si"), K("s1_"))
 
-        def late1():
-            tt(Z(21, n), Z(1, n), Z(3, n), A.mult, "got0 pl0", "a0")
-            marks_3(1, NB, T.b1[:, 0:n], "bl1")
+    def stuck(t, n, cut):
+        cp(both(n, 1.0, S16), T.CS[:, 0, 0:n], T.ci[:, 0:n], span("ci", 0, n), "CS")
+        ts(n, T.zi[:, 4, 0:n], T.ki[:, 0:n], 1, None, AND, None, span("ki", 0, n), "hh")
+        lin(both(n, 1.0, S16), Z(20, n), T.zi[:, 4, 0:n], 65536.0, 131071.0, "hh", "ht")
+        tt(n, T.CS[:, 1, 0:n], T.ki[:, 0:n], Z(20, n), A.is_gt, span("ki", 0, n) + " ht", "CSs")
+        for c0, nb in cut:
+            for v in range(2):
+                mm(n, [(T.pS[:, 12:14, 0, c0 + nb * v:c0 + nb * v + nb], T.SWb[:, 2 * v + e, :], T.CS[:, :, c0 + e:c0 + 2 * nb:2]) for e in range(2)], "SWs CS CSs", "pS.b")
+        cl = T["c%d" % t]
+        cp(both(n, 1.0, S16), cl[:, 0:n], T.pS[:, 12, 0, 0:n], "pS.b", "cl%d" % t)
+        cp(gath(16 * n), T["OH%d" % t][:, 0:16 * n], ta.indirect(cl[:, 0:n]), TA + "cl%d" % t, span("OH%d_" % t, 0, n))
+        tt(n, Z(9 + t, n), T.pS[:, 13, 0, 0:n], Z(1 + t, n), A.mult, "pS.b got%d" % t, "gs%d" % t)
 
-        hook = {"early": after0a, 1: after0b, NB // 2: ban1, "gathered": after0c, "mid": lambda: marks_1(1, NB, T.s1[:, 0:n], T.b1[:, 0:n], "s1", "bl1"),
-                "chosen": lambda: act(Z(3, n), T.pT[:, 64:64 + n], F.Identity, "pT", "pl0", bias=15.75), "late": late1}
-        step(1, NB, T.s1, "s1", "BN", hook)
+    def plan(t, L, S, sk):
+        tt(gath(L, "V"), T["PL%d" % t][:, 0:L], T.pli[:].indirect(S[:, 0:L // 16]), T["OH%d" % t][:, 0:L], A.mult, "pli0 pli1 pad1 " + span("OH%d_" % t, 0, L // 16) + " " + sk, "PL%d" % t)
+
+    def refresh(d, j, a, b):
+        at, m = V + (d - 1) * GH, 12 - 4 * (N - d)
+        cp(gath(256 * (b - a)), T.W[:, at + 256 * a:at + 256 * b], SR[d][:].indirect(T.IN[:, j, m + 16 * a:m + 16 * b]), "Sz%d Sp%d Sx%d IN%d" % (d, d, d, j), span("W%d" % d, a, b))
+
+    front(T.L0, "L0 Ls0", CUT[(8, 0)], 0, 8)
+    for rnd in range(RO):
+        n = 8 if rnd == 0 else 16
+        L, NH = 16 * n, n // 8
+        last = rnd == RO - 1
+        LS, LB = "L0 Ls0 Ls1", "L0 Lb0 Lb1"
+        marks_1(0, NH, T.L0, T.L0, 16, LS, LB)
+        marks_2(0, NH, T.L0[:, 16:16 + n], LB)
+        for h, (c0, nb) in enumerate(CUT[(n, 0)]):
+            chunk(0, h, c0, nb, ON[(n, 0)], "BAN" if rnd > 0 else None)
+            front(T.s1, span("s1_", c0, c0 + 2 * nb), CUT[(n, 1)], c0, c0 + 2 * nb)
+        BI0, BI1, S1 = span("bi0_", 0, n), span("bi1_", 0, n), span("s1_", 0, n)
+        stuck(0, n, CUT[(n, 0)])
+        plan(0, L, T.L0, LS)
+        ts(n, T.zi[:, 0, 0:n], T.bi0[:, 0:n], 4095, None, AND, None, BI0, "b0")
+        ts(n, T.zi[:, 2, 0:n], T.bi0[:, 0:n], 4, 255, SHR, AND, BI0, "sb")
+        lin(both(n), Z(19, n), Z(9, n), -64.0, 64.0, "gs0", "z19")
+        tt(n, T.b1[:, 0:n], Z(19, n), T.zi[:, 2, 0:n], A.max, "z19 sb", "bl1")
+        tt(n, Z(13, n), Z(9, n), T.zi[:, 0, 0:n], A.mult, "gs0 b0", "bg0")
+        tt(n, Z(11, n), Z(1, n), Z(9, n), A.subtract, "got0 gs0", "gd0")
+        if not last:
+            ts(n, Z(15, n), Z(13, n), 1024.0, 320.0, A.is_ge, A.mult, "bg0", "ask0")
+        marks_1(1, NH, T.s1, T.b1, 0, S1, "bl1")
+        marks_2(1, NH, T.b1[:, 0:n], "bl1")
+        for h, (c0, nb) in enumerate(CUT[(n, 1)]):
+            chunk(1, h, c0, nb, ON[(n, 1)], "OH0")
+        stuck(1, n, CUT[(n, 1)])
+        plan(1, L, T.s1, S1)
+        YB = [T.pY, T.pB0]
+        YK = ("pY.a", "pB0.a")
         for t in range(2):
-            for h in range(NH):
-                mm([(YB[2 * t + h], T["AR%d" % t][:, 128 * h:128 * h + 128], T.idB[:])], "idB AR%d" % t, YK[2 * t + h], True, False)
-        plan(1, NB, T.s1, "s1")
-        reached(1, n)
+            mm([L] + [128] * (2 * NH), [(YB[t][:, 0:L], T.idb[:], T.zer[:, 0:L])] +
+               [(YB[t][:, 128 * h:128 * h + 128], x[:, 128 * h:128 * h + 128], y[:]) for h in range(NH) for x, y in ((T["AR%d" % t], T.idB), (T["PL%d" % t], T.BO))],
+               "idb zer idB BO PL%d " % t + each("AR%d%%d" % t, NH), YK[t], True, False)
         bI, dI = T.zi[:, 3, 0:n], T.dI[:, 0:n]
-        tt(Z(14, n), Z(10, n), T.zi[:, 1, 0:n], A.mult, "gs1 b1", "bg1")
-        tt(bI, Z(13, n), Z(14, n), A.max, "bg0 bg1", "bI")
-        ts(dI, bI, 9, None, SHR, None, "bI", "dI")
-        if n == 16:
-            tt(T.ff[:], T.dI[:].indirect(T.rep[:, 0:3]), T.dc[:], A.is_equal, "dI rep dc", "ff0 ff1 ff2")
-        else:
-            for d in range(3):
-                ts(T.ff[:, n * d:n * d + n], dI, float(d + 2), None, A.is_equal, None, "dI", "ff%d" % d)
-        scan(T.inc[:, 0:3 * n], T.rrk[:, 0:3 * n], T.ff[:, 0:3 * n], A.mult, A.add, "rrk ff0 ff1 ff2", "inc")
+        ts(n, T.zi[:, 1, 0:n], T.bi1[:, 0:n], 4095, None, AND, None, BI1, "b1")
+        tt(n, Z(14, n), Z(10, n), T.zi[:, 1, 0:n], A.mult, "gs1 b1", "bg1")
+        tt(n, bI, Z(13, n), Z(14, n), A.max, "bg0 bg1", "bI")
+        ts(n, dI, bI, 9, None, SHR, None, "bI", "dI")
+        tt(gath(48, "V"), T.ff[:], T.dI[:].indirect(T.rep[:, 0:3]), T.dc[:], A.is_equal, "dI rep dc", "ff")
+        scan(24, T.inc[:], T.rrk[:], T.ff[:], A.mult, A.add, "rrk ff", "inc")
+        tt(n, Z(12, n), Z(2, n), Z(10, n), A.subtract, "got1 gs1", "gd1")
+        tt(n, T.gd[:, 0:n], Z(11, n), Z(12, n), A.add, "gd0 gd1", "gd")
+        mm(16, [(T.pM[:, 67:128:4], T.idm[:], T.gd[:])], "idm gd", "pM.r3")
         for d in range(3):
-            o = T.pM[:, 64 + d:64 + 3 * n:3]
-            mm([(o, T.tri[:], T.ff[:, n * d:n * d + n]), (o, T.BO[:], T.inc[:, n * d:n * d + n])], "tri BO ff0 ff1 ff2 inc", "pM")
-        tt(Z(12, n), Z(2, n), Z(10, n), A.subtract, "got1 gs1", "gd1")
-        if not last:
-            ts(Z(26, n), dI, 64.0, None, A.mult, None, "dI", "z26")
-            ts(T.XI[:, 0:n], bI, 511, None, AND, None, "bI", "XI")
-        tt(Z(25, n), Z(11, n), Z(12, n), A.add, "gd0 gd1", "gd")
-        scan(T.fr[:, 0:3 * n], T.r3[:, 0:3 * n], T.pM[:, 64:64 + 3 * n], A.add, A.min, "r3 pM", "fr")
-        rk = T.fr[:, 2:3 * n:3]
-        tt(Z(31, n), Z(2, n), Z(4, n), A.mult, "got1 pl1", "a1")
-        if not last:
-            ts(Z(27, n), rk, 255.0, 48.0, A.add, A.min, "fr", "z27")
-        ts(Z(28, n), rk, -207.5, None, A.is_lt, None, "fr", "sent1")
-        if not last:
-            tt(T.SL[:, 0:n], Z(26, n), Z(27, n), A.add, "z26 z27", "SL")
-            cp(T.AO[:, L:2 * L], T.tc[:].indirect(T.SL[:, 0:n]), "tc SL", "AO1", "S")
-            cp(T.AO[:, 0:L], T.ta[:].indirect(T.SL[:, 0:n]), "ta taz SL", "AO0", "S")
-        tt(Z(29, n), Z(28, n), Z(25, n), A.add, "sent1 gd", "good")
-        if not last:
-            tt(T.DX[:, 0:L], T.XI[:, 0:n].indirect(T.bc[:, 0:n]), T.ta[:, 0:L], A.mult, "XI bc ta", "DX")
-        tt(Z(30, n), Z(29, n), Z(21, n), A.mult, "good a0", "z30")
-        tt(T.WW[:, n:2 * n], Z(29, n), Z(31, n), A.mult, "good a1", "WW1")
-        tt(T.WW[:, 0:n], Z(30, n), Z(22, n), A.add, "z30 q0", "WW0")
-        if not last:
-            for h in range(NH):
-                for f, (l, r) in enumerate(((T.DX, T.nBO), (T.OH1, T.Cm))):
-                    o = T.pS[:, 8 * h:8 * h + 8, f, :]
-                    mm([(o, T.AO[:, L + 128 * h:L + 128 * h + 128], T.idB[:]), (o, l[:, 128 * h:128 * h + 128], r[:])], "idB nBO Cm AO1 DX OH1", "pS")
-            for h in range(NH):
-                mm([(T.pA[:, 128 * h:128 * h + 128], T.AO[:, 128 * h:128 * h + 128], T.idb[:])], "idb AO0", "pA")
-            for h in range(NH):
-                cp(T.AW[:, 64 * h:64 * h + 64:8, :], T.pA[:, 128 * h:128 * h + 128], "pA", "AW%d" % h, "S")
+            o = T.pM[:, 64 + d:128:4]
+            mm(16, [(o, T.tri[:], T.ff[:, 16 * d:16 * d + 16]), (o, T.BO[:], T.inc[:, 16 * d:16 * d + 16])], "tri BO ff inc", "pM.r%d" % d)
+        scan(64, T.fr[:], T.r4[:], T.pM[:, 64:128], A.add, A.min, "r4 pM.r0 pM.r1 pM.r2 pM.r3", "fr")
+        tt(gath(L, "V"), T.D[:, 0:L], T.fr[:].indirect(T.bc[:, 16:16 + n]), T.THD[:, 0:L], A.is_le, "fr bc THD", "D")
         for t in range(2):
-            tt(T.D[:, L * t:L * t + L], T.WW[:, 0:2 * n].indirect(T.bc[:, n * t:n * t + n]), T.ta[:, 0:L], A.mult, "WW0 WW1 bc ta", "D%d" % t)
+            mm(128, [(YB[t][:, 128 * h:128 * h + 128], T.D[:, 128 * h:128 * h + 128], T.BOK[:]) for h in range(NH)], "BOK D", YK[t], False, True)
+        if not last:
+            lin(both(n, 1.0, S16), Z(26, n), dI, 64.0, 0.0, "dI", "z26")
+            tt(n, Z(25, n), Z(26, n), Z(15, n), A.add, "z26 ask0", "z25")
+            ts(n, T.XI[:, 0:n], bI, 511, None, AND, None, "bI", "XI")
+            ts(n, Z(27, n), T.fr[:, 3:4 * n:4], 255.0, 48.0, A.add, A.min, "fr", "z27")
+            tt(n, T.SL[:, 0:n], Z(25, n), Z(27, n), A.add, "z25 z27", "SL")
+            cp(gath(L), T.AO[:, 256:256 + L], T.tc[:].indirect(T.SL[:, 0:n]), "tc tc1 SL", "AO1")
+            cp(gath(L), T.AO[:, 0:L], ta.indirect(T.SL[:, 0:n]), TA + "SL", "AO0")
+            tt(gath(L, "V"), T.DX[:, 0:L], T.XI[:, 0:n].indirect(T.bc[:, 0:n]), T.ta[:, 0:L], A.mult, "XI bc ta", "DX")
             for h in range(NH):
-                mm([(YB[2 * t + h], T.D[:, L * t + 128 * h:L * t + 128 * h + 128], T.BO[:])], "BO D%d" % t, YK[2 * t + h], False, True)
+                a, b = 128 * h, 128 * h + 128
+                o = T.pS[:, 8 * h:8 * h + 8, 0, :]
+                mm(128, [(o, T.DX[:, a:b], T.nBO[:]), (o, T.AO[:, 256 + a:256 + b], T.idB[:])], "idB nBO AO1 DX", "pS.a" if h == 0 else "pS.b")
+                o = T.pS[:, 8 * h:8 * h + 8, 1, :]
+                mm(128, [(o, T.OH0[:, a:b], T.Cm0[:]), (o, T.OH1[:, a:b], T.Cm1[:]), (o, T.AO[:, 256 + a:256 + b], T.idB1[:])],
+                   "idB1 Cm0 Cm1 AO1 " + span("OH0_", 0, n) + " " + span("OH1_", 0, n), "pS.c%d" % h)
+                mm(128, [(T.pA[:, a:b], T.AO[:, a:b], T.idb[:])], "idb AO0", "pA.a%d" % h)
+            cp(both(L), T.AW[:, 0:64 * NH:8, :], T.pA[:, 0:L], each("pA.a%d", NH), each("AW%d", NH))
         for t in range(2):
-            for h in range(NH):
-                u = 2 * t + h
-                ts(T.AF[:, 64 * u:64 * u + 64:8, :], YB[u], -32768.0, 0.0, A.add, A.max, YK[u], "AF%d" % u)
-                mm([(T.pM[:, 128:192], T.AF[:, 64 * u + 7 * k:64 * u + 7 * k + 8, :], T["B%d" % t][:, 512 * h + 64 * k:512 * h + 64 * k + 64]) for k in range(8)],
-                   "AF%d B%d%d" % (u, t, h), "pM", t == 0 and h == 0, t == 1 and h == NH - 1)
+            relu(both(L, 1.0, S16), T.AF[:, 128 * t:128 * t + 64 * NH:8, :], YB[t][:, 0:L], 16.0 - 32768.0 - 4096.0, YK[t], "AF%d AF%d" % (2 * t, 2 * t + 1))
+            mm(64, [(T.pM[:, 128:192], T.AF[:, 128 * t + 64 * h + 7 * k:128 * t + 64 * h + 7 * k + 8, :], T["B%d" % t][:, 512 * h + 64 * k:512 * h + 64 * k + 64])
+                    for h in range(NH) for k in range(8)], "AF%d AF%d " % (2 * t, 2 * t + 1) + each("B%d%%d" % t, NH), "pM.m", t == 0, t == 1)
         if not last:
-            ts(T.X[:, 0:2 * L], T.pS[:, 0:8 * NH, :, :], 1024.0 - 32768.0, 0.0, A.add, A.max, "pS", "X")
-            mm([(T.pA[:, 256:288], T.AW[:, 64 * h + 7 * k:64 * h + 7 * k + 8, :], T.X[:, 256 * h + 32 * k:256 * h + 32 * k + 32])
-                for h in range(NH) for k in range(8)], "AW0 AW1 X", "pA")
-        ts(T.kp[:], T.pM[:, 128:192], 0.5, None, A.is_lt, None, "pM", "kp")
-        tt(T.kp[:], T.kp[:], T.mp[:], A.mult, "kp mp", "kp")
+            relu(both(2 * L, 1.0, S16), T.X[:, 0:2 * L], T.pS[:, 0:8 * NH, :, :], 1024.0 - 32768.0, "pS.a pS.b pS.c0 pS.c1", "X")
+            mm(32, [(T.pA[:, 256:288], T.AW[:, 64 * h + 7 * k:64 * h + 7 * k + 8, :], T.X[:, 256 * h + 32 * k:256 * h + 32 * k + 32])
+                    for h in range(NH) for k in range(8)], "AW0 AW1 X", "pA.o")
+        ts(64, T.kp0[:], T.pM[:, 128:192], 0.5, None, A.is_lt, None, "pM.m", "kp0")
+        tt(128, T.kp[:], T.kp0[:], T.mp[:], A.mult, "kp0 mp", "kp")
         if not last:
-            tt(T.MSG[:, rnd, 0:32], T.pM[:, 128:160], T.kp[:, 0:32], A.add, "pM kp", "MSGm")
-            cp(T.MSG[:, rnd, 32:64], T.pA[:, 256:288], "pA", "MSGo")
-            deps("G", ["MSGo", "MSGm"], [])
-            rest = [e for e in chip if e not in out_e]
-            per = len(rest) // len(far)
-            items = [(h, rest[i * per:(i + 1) * per], "hm%d" % rnd, T.MSG[:, rnd, :], T.HM[:, rnd, :]) for i, h in enumerate(close)]
+            tt(32, T.MSG[:, rnd, 0:32], T.pM[:, 128:160], T.kp[:, 0:32], A.add, "pM.m kp", "MSGm")
+            cp(both(32, 1.0, S16), T.MSG[:, rnd, 32:64], T.pA[:, 256:288], "pA.o", "MSGo")
+            per = len(chip) // len(far)
+            ls[0] += remote([(h, chip[i * per:(i + 1) * per], "hm%d" % rnd, T.MSG[:, rnd, :], T.HM[:, rnd, :]) for i, h in enumerate(close)], "ls", "MSGm MSGo", "msg")
             for q in near:
                 d = (rank - q) % N
                 j = 3 * rnd + d - 1
-                items.append((T.cores[q], out_e, "m%d" % j, T.MSG[:, rnd, :], T.IN[:, j, 12 - 4 * d:76 - 4 * d]))
-            ls[0] += send(g, T, topo, core, items, "ls")
+                ls[0] += remote([(T.cores[q], out_e, "m%d" % j, T.MSG[:, rnd, :], T.IN[:, j, 12 - 4 * d:76 - 4 * d])], "ls", "", "msg2")
             for d in range(1, N):
-                lands("m%d" % (3 * rnd + d - 1), len(out_e), "IN%d" % (3 * rnd + d - 1))
-        tt(T.mp16[:], T.pM[:, 128:192], T.kp[:], A.add, "pM kp", "mp16")
-        cp(T.W[:, 0:GH], T.S0[:].indirect(T.mp16[:, 0:32]), "Sz0 Sp0 Sx0 mp16 sent", "Wa", "S")
-        cp(T.W[:, GH:V], T.S0[:].indirect(T.mp16[:, 32:64]), "Sz0 Sp0 Sx0 mp16", "Wb")
+                lands("m%d" % (3 * rnd + d - 1), len(out_e), "msg", "IN%d" % (3 * rnd + d - 1), 1.2 if (rank + d) % N in near else 2)
+        tt(64, T.mp16[:], T.pM[:, 128:192], T.kp[:], A.add, "pM.m kp", "mp16")
+        cp(gath(GH), T.W[:, 0:GH], T.S0[:].indirect(T.mp16[:, 0:32]), "Sz0 Sp0 Sx0 mp16 sent", "Wa")
+        cp(gath(GH), T.W[:, GH:V], T.S0[:].indirect(T.mp16[:, 32:64]), "Sz0 Sp0 Sx0 mp16", "Wb")
         if last:
             dma("S", T.y[:, 0:GH], T.W[:, 0:GH], "Wa", "ya")
             dma("Y", T.y[:, GH:V], T.W[:, GH:V], "Wb", "yb")
             break
-        cp(T.mp[:], T.mp16[:], "mp16", "mp")
-        ts(T.fz1[:], T.pM[:, 128:192], 0.25, BIG, A.is_equal, A.mult, "pM", "fz1")
-        tt(T.FZ[:], T.FZ[:], T.fz1[:], A.max, "FZ fz1", "FZ")
-        if rnd == 0:
-            fill(T.rrk[:, 8:48:16], 1.0, "rrk")
+        cp(both(64, 1.0, S16), T.mp[:], T.mp16[:], "mp16", "mp")
+        tt(128, T.FZ[:], T.kp0[:], T.MK[:], A.mult, "kp0 MK", "FZ")
         requests(rnd + 1)
-        near_of(T.L0, LS, 8, 0, 0, 6)
-        cost_of(T.L0, LS, 8, 0, 0, 6)
-        for d in (2, 1, 3):
-            j = 3 * rnd + d - 1
-            if d != 3:
-                refresh(N - d, j, 0, 32, "S", "W%d" % (N - d))
-            else:
-                refresh(1, j, CUT, 32, "S", "W1b")
-        ts(T.L0[:, 7:16], T.IN[:, 3 * rnd:3 * rnd + 3, 40:43], -1.0, 1024.0, A.mult, A.add, "L0 IN%d IN%d IN%d" % (3 * rnd, 3 * rnd + 1, 3 * rnd + 2), "Ls1")
+        front(T.L0, "L0 Ls0", CUT[(16, 0)], 0, 6)
+        j0 = 3 * rnd
+        INS = "IN%d IN%d IN%d" % (j0, j0 + 1, j0 + 2)
+        for d in range(1, N):
+            refresh(N - d, j0 + d - 1, 0, 2)
+        ts(9, T.L0[:, 7:16], T.IN[:, j0:j0 + 3, 40:43], -1.0, 1024.0, A.mult, A.add, "L0 " + INS, "Ls1")
+        cp(9, T.L0[:, 39:48], T.IN[:, j0:j0 + 3, 56:59], "L0 " + INS, "Lc1")
+        front(T.L0, LS, CUT[(16, 0)], 6, 16)
+        cp(gath(160), T.BAN[:, 96:256], T.ta[:].indirect(T.L0[:, 38:48]), TA + "tao L0 Lc1", span("BAN_", 6, 16))
+        ts(9, T.L0[:, 23:32], T.L0[:, 7:16], 1.0 / 16, -15.0 / 32, A.mult, A.add, LS, "Lb1")
 
-    for s in sorted(cnt):
-        if seen.get(("G", s), 0) < cnt[s]:
-            g.wait_ge(T.sem[s], cnt[s])
+    issue(P, eng, T)
     g.wait_ge(T.sem.ls, ls[0])

@@ -6,12 +6,18 @@ V, GH, RO = 1024, 512, 4
 BIG = 2.0 ** 94
 LNB = math.log(1.75)
 LN0 = 90 * math.log(2.0)
-WAKE, GATHER, PE, LOAD, HOP = 130, 1.56, 0.75, 2400, 2400
-SPARE, LAG, CUTS, PASSES, FIX = 2.0, 2, 1, 2, 36
+WAKE, GATHER, PE, LOAD, HOP = 130, 1.56, 0.72, 2400, 2400
+SPARE, LAG, CUTS, PASSES, FIX = 1.0, 2, 1, 2, 36
 ON = {(8, 0): "----", (8, 1): "----", (16, 0): "VSVSSSSS", (16, 1): "SSSSSSSS"}
 CUT = {(8, 0): [(0, 4)], (8, 1): [(0, 4)], (16, 0): [(0, 4), (8, 4)], (16, 1): [(0, 4), (8, 4)]}
 S16 = "VS"
+FIXS = 70
+AT = {'last Wa 1': 'S', 'last Wb 1': 'V', 'front Wa 1': 'S', 'front Wb 1': 'V', 'front W 1': 'S', 'front W 3': 'V', 'r2 end AF 1': 'S', 'r2 end AF 2': 'S',
+      'r2 end AO 1': 'S', 'r2 end AO 2': 'V', 'front W 2': 'S', 'front Q 3': 'V', 'front Q 4': 'V', 'front CK 4': 'V', 'front Q 5': 'V', 'r2 m0 AW 2': 'S',
+      'r2 m1 bl 1': 'S', 'r2 m1 B 1': 'S', 'r2 s11 ki 1': 'S', 'r1 s00 ki 1': 'V', 'r1 m1 ht 1': 'S', 'r1 m1 bl 1': 'S'}
+SITES = []
 FAR0, NEAR0 = 2.2, 1.3
+PARTS = 2
 ENDS = []
 
 
@@ -21,18 +27,18 @@ def _sb(n, d="float32"):
 
 H, I32, U16, F16 = "bfloat16", "int32", "uint16", "float16"
 SCRATCH = {
-    "W": _sb(2560, H), "S0": _sb(2064, H), "S1": _sb(1552, H), "S2": _sb(1552, H), "S3": _sb(1552, H),
+    "W": _sb(2560, H), "S0": _sb(2048, H), "S1": _sb(2048, H), "S2": _sb(2048, H), "S3": _sb(2048, H),
     "nbi": _sb(V + 16, I32), "pti": _sb(V, I32), "pli": _sb(V + 16, I32), "cst": _sb(V + 16),
     "rq": _sb(28, I32), "rqb": _sb(28, I32), "thi": _sb(4, I32), "col": _sb(20), "coli": _sb(4, I32),
     "row": _sb(144), "rowg": _sb(128), "rowj": _sb(128), "Rc": _sb(512, H),
-    "idb": _sb(128, H), "id12": _sb(128, H), "id4": _sb(128, H), "idB": _sb(128, H), "idB1": _sb(128, H), "idm": _sb(128, H), "id32": _sb(128),
-    "thM": _sb(128, F16), "on12": _sb(256, H), "zer": _sb(256, H), "THD": _sb(256, H),
+    "idb": _sb(128, H), "id12": _sb(128, H), "id4": _sb(128, H), "idB": _sb(128, H), "RX": _sb([8, 2, 16], H), "idF": _sb(128, H), "idm": _sb(128, H), "id32": _sb(128),
+    "thM": _sb(128, F16), "on12": _sb(256, H), "zer": _sb(512, H), "THD": _sb(256, H),
     "BOc": _sb(128, H), "Cm0": _sb(128, H), "Cm1": _sb(128, F16),
     "BO": _sb(128, H), "nBO": _sb(128, H), "BOK": _sb(128, H), "tri": _sb(128, H), "EE": _sb(144, H), "SWs": _sb([4, 128], H), "SWb": _sb([4, 128], H),
-    "ta": _sb(1296, H), "taf": _sb(256), "tb": _sb(160, H), "tba": _sb(64), "tbb": _sb(64), "tcf": _sb(320), "tc": _sb(640, H),
+    "ta": _sb(1296, H), "taf": _sb(256), "tb": _sb(192, H), "tba": _sb(64), "tbb": _sb(64), "tcf": _sb(384), "tc": _sb(768, H),
     "bci": _sb(32, I32), "bc": _sb(32, U16), "rep": _sb(4, U16), "dc": _sb(48), "r4": _sb(64),
     "rmin": _sb(256), "rmax": _sb(256), "rrk": _sb(48, H), "offc": _sb(16, I32), "wi": _sb(32), "wcol": _sb(2), "thr": _sb(16),
-    "mp": _sb(64), "kp0": _sb(64), "kp": _sb(64), "mp16": _sb(64, U16), "FZ": _sb(64, H), "MK": _sb(64, H), "Ms": _sb(160, H),
+    "mp": _sb(64), "mp16": _sb(64, U16), "FZ": _sb(64, H), "MK": _sb(64, H), "Ms": _sb(192, H), "DC": _sb(48),
     "AW": _sb([128, 16], H), "AF": _sb([256, 16], F16),
     "L0": _sb(48, U16), "s1": _sb(16, U16), "b1": _sb(16, U16), "c0": _sb(16, U16), "c1": _sb(16, U16),
     "Q": _sb(256, U16), "Qf": _sb(256, F16), "CK": _sb(256), "BAN": _sb(256, H),
@@ -40,15 +46,15 @@ SCRATCH = {
     "ov": _sb(256), "kR": _sb([8, 2, 16]), "kT": _sb(256), "km": _sb(256), "ki": _sb(16, I32), "ci": _sb(16, I32), "off": _sb(16, U16),
     "CS": _sb([2, 16], H), "K1": _sb(256, H), "K1T": _sb(256), "bm": _sb(256), "bi0": _sb(16, I32), "bi1": _sb(16, I32),
     "AR0": _sb(256, H), "AR1": _sb(256, H), "FB": _sb(256, H), "B0": _sb(1024, H), "B1": _sb(1024, H), "LK": _sb(256, H), "PL0": _sb(256, F16), "PL1": _sb(256, F16),
-    "z": _sb([32, 16]), "zi": _sb([6, 16], I32), "dI": _sb(16, I32), "gd": _sb(16, H), "ff": _sb(48, H), "inc": _sb(48, H), "fr": _sb(64), "XI": _sb(16, I32), "SL": _sb(16, U16),
+    "z": _sb([32, 16]), "zi": _sb([6, 16], I32), "dI": _sb([2, 16], I32), "gs": _sb([2, 16]), "gd": _sb(64, H), "ff": _sb([2, 48], H), "inc": _sb([2, 48], H), "fr": _sb(64), "XI": _sb(16, I32), "SL": _sb(16, U16),
     "D": _sb(256, H), "DX": _sb(256, F16), "AO": _sb(512, H), "X": _sb(512, F16),
-    "MSG": _sb([3, 64], U16), "IN": _sb([9, 72], U16), "HB": _sb(128, H), "HM": _sb([3, 64], U16),
+    "MSG": _sb([4, 64], U16), "IN": _sb([9, 72], U16), "HB": _sb(128, H), "HM": _sb([3, 64], U16),
 }
 for _p in ("pA", "pB0", "pB1", "pM", "pY"):
     SCRATCH[_p] = ("psum", [128, 512], "float32")
 for _p in ("pC0", "pC1", "pS"):
     SCRATCH[_p] = ("psum", [128, 16, 2, 16], "float32")
-SEMAPHORES = (["cV", "cS", "cP", "cG", "l0", "ls", "hx", "hm0", "hm1", "hm2", "xg1", "xg2", "xg3"] + ["m%d" % k for k in range(9)] + ["d%d" % k for k in range(24)])
+SEMAPHORES = (["cV", "cS", "cP", "cG", "l0", "ls", "hx", "xg1", "xg2", "xg3"] + ["hm%d" % k for k in range(6)] + ["m%d" % k for k in range(18)] + ["d%d" % k for k in range(32)])
 
 
 def bits(es):
@@ -101,14 +107,16 @@ def helper(g, core, T, topo):
         q = far[close.index(core)]
         d = (r - q) % n
         for t in range(RO - 1):
-            g.wait_ge(T.sem["hm%d" % t], len(topo.engines(own[0], core)) // len(far))
             j = 3 * t + d - 1
-            ls += send(g, T, topo, core, [(T.cores[q], es, "m%d" % j, T.HM[:, t, :], T.IN[:, j, 12 - 4 * d:76 - 4 * d])], "ls")
+            for u in range(PARTS):
+                w = 64 // PARTS
+                g.wait_ge(T.sem["hm%d" % (2 * t + u)], (len(topo.engines(own[0], core)) - u * len(es)) // len(far))
+                ls += send(g, T, topo, core, [(T.cores[q], es, "m%d" % (2 * j + u), T.HM[:, t, w * u:w * u + w], T.IN[:, j, 12 - 4 * d + w * u:12 - 4 * d + w * u + w])], "ls")
     g.wait_ge(T.sem.ls, ls)
 
 
 def new_plan():
-    return {"ops": [], "lastw": {}, "reads": {}, "chain": {}, "pin": {}}
+    return {"ops": [], "lastw": {}, "reads": {}, "chain": {}, "pin": {}, "at": "set", "sites": {}}
 
 
 def add(P, cost, fn, R, Wr, lat=0, tok=None, start=False, stop=False):
@@ -127,7 +135,7 @@ def add(P, cost, fn, R, Wr, lat=0, tok=None, start=False, stop=False):
             dep[a] = True
     banks = set(x.split(".")[0] for x in R + Wr if x[0] == "p" and x[1].isupper())
     for b in banks:
-        if onP and b not in ("pA", "pS", "pB1"):
+        if onP and b not in ("pA", "pB1"):
             if start and b in P["chain"]:
                 dep.setdefault(P["chain"][b], False)
             if stop:
@@ -143,6 +151,13 @@ def add(P, cost, fn, R, Wr, lat=0, tok=None, start=False, stop=False):
     for x in Wr:
         P["lastw"][x] = k
         P["reads"][x] = []
+    if len(cost) > 1:
+        site = P["at"] + " " + Wr[0].rstrip("0123456789_")
+        P["sites"][site] = P["sites"].get(site, 0) + 1
+        site += " %d" % P["sites"][site]
+        SITES.append(site)
+        if AT.get(site, "-") in cost:
+            cost = {AT[site]: cost[AT[site]]}
     P["ops"].append({"cost": cost, "fn": fn, "dep": dep, "lat": lat, "tok": tok, "banks": banks})
     return k
 
@@ -250,7 +265,7 @@ def rank_program(g, core, T, topo):
     nd, ls = [0], [0]
     plain = lambda n, r=1.0: max(64.0, n * r) + FIX
     gath = lambda n, es="VS": {e: (60 if e == "V" else 78) + GATHER * n for e in es}
-    both = lambda n, r=1.0, es="VS": {e: plain(n, r if e == "V" else 1.0) for e in es}
+    both = lambda n, r=1.0, es="VS": {e: plain(n, r) if e == "V" else plain(n) + FIXS for e in es}
 
     def dma(e, out, in_, R, Wr, lat=1.0):
         s = "d%d" % nd[0]
@@ -345,8 +360,8 @@ def rank_program(g, core, T, topo):
         a = V + (d - 1) * GH
         l0 += remote([(T.cores[q], out_e, "xg%d" % d, T.W[:, 0:GH], T.W[:, a:a + GH])], "l0", "Wa", "out1")
     iota(16, T.offc[:], [[512, 8], [16, 2]], 0, 0, "offc issued", False)
-    dma("Y", T.pti[:], T.pt[:], "issued", "pti", 1.5)
-    dma("Y", T.W[:, GH:V], T.x[:, GH:V], "", "Wb", 2)
+    dma("Y", T.W[:, GH:V], T.x[:, GH:V], "issued", "Wb", 1.5)
+    dma("Y", T.pti[:], T.pt[:], "", "pti", 2.2)
     for d in range(1, N):
         q = (rank - d) % N
         nq, fq, hq, _c = ways(T, topo, q)
@@ -358,9 +373,9 @@ def rank_program(g, core, T, topo):
     add(P, {"G": 1230}, lambda q, e: q.affine_select(T.Rc[:], T.Rc[:], [[16, 8], [0, 8], [1, 8]], A.not_equal, 1.0, 8, -1), "Rc", "Rc")
     iota(16, T.bci[:, 0:16], [[1, 16]], 0, 0, "bci0", False)
     iota(16, T.bci[:, 16:32], [[4, 16]], 3, 0, "bci1", False)
-    iota(64, T.mp[:], [[16, 64]], 1040, 0, "mp")
-    iota(48, T.dc[:], [[1, 3], [0, 16]], 2, 0, "dc")
-    iota(320, T.tcf[:], [[4, 5], [1, 4], [0, 16]], -8, 0, "tcf")
+    iota(64, T.mp[:], [[16, 64]], 0, 0, "mp")
+    iota(48, T.dc[:], [[1, 3], [0, 16]], 3, 0, "dc")
+    iota(384, T.tcf[:], [[4, 6], [1, 4], [0, 16]], -12, 0, "tcf")
     iota(256, T.taf[:], [[1, 16], [0, 16]], 0, 0, "taf")
     iota(1024, T.AW[:, 64:128, :], [[0, 1024]], 0, 0, "AW1")
     fill(512, T.AW[:, 0:64, :], 0.0, "AW0")
@@ -371,14 +386,14 @@ def rank_program(g, core, T, topo):
     cp(4, T.col[:, 0:4], T.coli[:, 0:4], "coli coli1 coli2 coli3", "col")
     ts(128, T.id32[:], T.row[:, 0:128], C(0), None, A.is_equal, None, "row col", "id32")
     ts(128, T.ta[:, 0:128], T.rowj[:], C(1), None, A.is_equal, None, "rowj col", "ta")
-    for nm, sc in (("id12", 2.0 ** -12), ("idb", 1.0), ("id4", 4.0), ("idB", 32768.0), ("idm", -255.0)):
+    for nm, sc in (("id12", 2.0 ** -12), ("idb", 1.0), ("id4", 4.0), ("idB", 32768.0), ("idm", -255.0), ("idF", BIG)):
         lin(both(128), T[nm][:], T.id32[:], sc, 0.0, "id32", nm)
     for w in (128, 256, 512):
         cp(both(w, 0.5), T.ta[:, w:2 * w], T.ta[:, 0:w], "ta", "ta")
     for k, a, sc, off in ((4, 3, -1.0, 1.0), (5, 0, 1.0, 16.0), (6, 0, 1.0, -16.0), (7, 2, 16.0, 15.0), (8, 1, 16.0, 0.0), (9, 1, 32.0, 0.0), (15, 1, 1.0, -1024.0)):
         lin(both(1), C(k), C(a), sc, off, "col", "col%d" % k)
     ts(1, C(16), C(1), 15.0, None, A.is_equal, None, "col", "col16")
-    lin(both(128), T.BOc[:], T.rowj[:], -1.0 / 16, 61.0 / 64, "rowj", "BOc")
+    lin(both(128), T.BOc[:], T.rowj[:], -1.0 / 16, 15.0 / 16 + 1536.0 / 65536, "rowj", "BOc")
     ts(16, T.wi[:, 16:32], T.wi[:, 16:32], C(1), -LNB, A.add, A.mult, "wi1 col", "wi1")
     ts(2, T.wi[:, 0:2], T.wi[:, 0:2], -LNB, LN0, A.mult, A.add, "wi0", "wi0")
     ts(16, T.wi[:, 16:32], T.wi[:, 16:32], LN0 + math.log(2.53), None, A.add, None, "wi1", "wi1")
@@ -396,8 +411,9 @@ def rank_program(g, core, T, topo):
     tt(256, T.BOc[:], T.BOc[:], T.BO[:], A.mult, "BOc BO", "BOc")
     lin(both(128, 0.5, S16), T.Cm1[:], T.BO[:], C(15), 0.0, "BO col15", "Cm1")
     lin(both(128, 0.5), T.Cm0[:], T.BO[:], C(8), 0.0, "BO col8", "Cm0")
-    ts(64, T.idB1[:], T.BO[:], C(16), 1040.0, A.mult, A.mult, "BO col16", "idB1")
-    tt(256, T.idB1[:], T.idB1[:], T.idB[:], A.max, "idB1 idB", "idB1")
+    cp(both(128, 0.5), T.RX[:, :, 0, :], T.idB[:], "idB", "RX0")
+    ts(64, T.RX[:, :, 1, :], T.BO[:], C(16), 1040.0, A.mult, A.mult, "BO col16", "RX1")
+    tt(256, T.RX[:, :, 1, :], T.RX[:, :, 1, :], T.idB[:], A.max, "RX1 idB", "RX1")
     lin(both(128, 0.5), T.nBO[:], T.BO[:], -1.0, 0.0, "BO", "nBO")
     lin(both(128, 0.5), T.BOK[:], T.BO[:], 4096.0, 0.0, "BO", "BOK")
     lin(both(256, 0.5), T.THD[:], T.ta[:, 0:256], 816.0, -1024.0, "ta", "THD")
@@ -406,27 +422,26 @@ def rank_program(g, core, T, topo):
     tt(256, T.tri[:], T.tri[:], T.BO[:], A.mult, "tri BO", "tri")
     tt(256, T.tri[:], T.tri[:], T.idm[:], A.add, "tri idm", "tri")
     fill(24, T.L0[:], 0, "L0")
-    fill(1, T.L0[:, 23:24], 64, "L0")
+    fill(1, T.L0[:, 23:24], 96, "L0")
     fill(8, T.L0[:, 32:48], V + 8, "L0")
     fill(16, T.nbi[:, V:V + 16], 0, "pad0")
     fill(16, T.pli[:, V:V + 16], 0, "pad1")
     fill(16, T.cst[:, V:V + 16], 0.0, "pad2")
     ts(16, T.offc[:], T.offc[:], C(9), None, A.add, None, "offc col9", "offc")
     fill(32, T.FZ[:], 0.0, "FZ")
-    fill(80, T.Ms[:], BIG, "Ms")
-    fill(80, T.tb[:], 0.0, "tb")
+    fill(96, T.Ms[:], BIG, "Ms")
+    fill(96, T.tb[:], 0.0, "tb")
     fill(64, T.BAN[:, 0:96], 0.0, span("BAN_", 0, 6))
-    fill(128, T.zer[:], 0.0, "zer")
+    fill(256, T.zer[:], 0.0, "zer")
     fill(128, T.on12[:], 2.0 ** -12, "on12")
     fill(24, T.rrk[:], 1.0, "rrk")
     fill(3, T.rrk[:, 0:48:16], 0.0, "rrk")
-    fill(64, T.r4[:], 0.0, "r4")
-    fill(16, T.r4[:, 0:64:4], 1024.0, "r4")
-    fill(16, T.dI[:], 0, "dI")
-    fill(8, T.gd[:], 0.0, "gd")
-    for s in range(4):
-        fill(8, SR[s][:, 0:16], 0.0, "Sz%d" % s)
-    ts(28, T.rqb[:], T.rq[:], 4, None, SHR, None, "rq", "rqb")
+    fill(64, T.r4[:], -4096.0, "r4")
+    fill(16, T.r4[:, 0:64:4], -207.0, "r4")
+    fill(32, T.dI[:], 0, "dI0 dI1")
+    fill(32, T.gs[:], 0.0, "gs0 gs1")
+    fill(32, T.gd[:], 0.0, "gd")
+    ts(28, T.rqb[:], T.rq[:], 1.0 / 16, 32 - 15.0 / 32, A.mult, A.add, "rq", "rqb")
     cp(1, C(10), T.thi[:, 0:1], "thi", "col10")
 
     def requests(t):
@@ -440,7 +455,7 @@ def rank_program(g, core, T, topo):
     lin(both(128, 1.0, S16), T.thM[:], T.id32[:], C(12), -16.0, "id32 col12", "thM")
     ts(64, T.tba[:], T.tba[:], C(1), None, A.is_equal, None, "tba col", "tba")
     ts(64, T.tbb[:], T.tbb[:], C(1), None, A.is_equal, None, "tbb col", "tbb")
-    tt(128, T.tb[:, 0:64], T.tba[:], T.tbb[:], A.add, "tba tbb tb", "tb")
+    tt(128, T.tb[:, 32:96], T.tba[:], T.tbb[:], A.add, "tba tbb tb", "tb")
     for u in range(2):
         a, b = u * GH, u * GH + GH
         ts(GH, T.cst[:, a:b], T.pti[:, a:b], 1.5 * 2.0 ** 34, 1.5 * 2.0 ** 34, A.add, A.subtract, "pti", "cst%d" % u)
@@ -449,16 +464,22 @@ def rank_program(g, core, T, topo):
     cp(32, T.bc[:], T.bci[:], "bci0 bci1", "bc")
     lin(both(64), T.mp[:], T.mp[:], 1.0, C(1), "mp col", "mp")
     ts(4, T.rep[:], T.rowg[:, 0:4], C(1), None, A.add, None, "rowg col", "rep")
-    ts(320, T.tc[:, 0:320], T.tcf[:], C(1), None, A.is_equal, None, "tcf col", "tc")
-    ts(160, T.tc[:, 320:640], T.tc[:, 0:320], C(16), None, A.max, None, "tc col16", "tc1")
+    ts(384, T.tc[:, 0:384], T.tcf[:], C(1), None, A.is_equal, None, "tcf col", "tc")
+    ts(192, T.tc[:, 384:768], T.tc[:, 0:384], C(16), None, A.max, None, "tc col16", "tc1")
     ts(256, T.ta[:, V + 16:V + 272], T.taf[:], C(1), None, A.is_equal, None, "taf col", "tao")
+    def keep(d):
+        if d == 0:
+            dma("Y", T.S0[:, 0:V], T.W[:, 0:V], "Wa Wb W10 W20 W30", "Sx0")
+        else:
+            dma("Y", SR[d][:, 0:GH], T.W[:, V + (d - 1) * GH:V + d * GH], "W%d0 W%d1" % (d, d), "Sx%d" % d)
+    for d in (1, 2, 3, 0):
+        keep(d)
     for d in range(1, N):
-        dma("Y", SR[d][:, 1040:1552], T.W[:, V + (d - 1) * GH:V + d * GH], "W%d0 W%d1" % (d, d), "Sx%d" % d)
+        fill(256, SR[d][:, GH:V], 0.0, "Sz%d" % d)
     for u in range(1, 4):
         dma("Y", T.AF[:, 64 * u:64 * u + 64, :], T.AF[:, 0:64, :], "AF0", "AF%d" % u)
-    dma("Y", T.S0[:, 1040:2064], T.x[:], "", "Sx0", 2)
     for d in range(N):
-        dma("Y", SR[d][:, 16:1040], T.plans[:], "", "Sp%d" % d, 2 + 0.5 * d)
+        dma("Y", SR[d][:, V:2 * V], T.plans[:], "", "Sp%d" % d, 2 + 0.5 * d)
 
     WALL = "Wa Wb W10 W11 W20 W21 W30 W31"
     TA = "ta taz "
@@ -481,13 +502,14 @@ def rank_program(g, core, T, topo):
     def marks_2(t, NH, bl, bk):
         L, n = 128 * NH, 8 * NH
         B = T["B%d" % t]
+        mm(64, [(T.pM[:, 0:64], T.idF[:], (T.FZ if t == 0 else T.MK)[:])], "idF " + ("FZ" if t == 0 else "MK"), "pM.w", True, False)
         for h in range(NH):
             mm(64, [(T.pM[:, 0:64], T.AW[:, 64 * h + 7 * k:64 * h + 7 * k + 8, :], B[:, 512 * h + 64 * k:512 * h + 64 * k + 64]) for k in range(8)],
-               "AW%d B%d%d" % (h, t, h), "pM.w", h == 0, h == NH - 1)
-        tt(64, T.Ms[:, 0:64], T.pM[:, 0:64], (T.FZ if t == 0 else T.MK)[:], A.add, "pM.w " + ("FZ" if t == 0 else "MK"), "Ms")
+               "AW%d B%d%d" % (h, t, h), "pM.w", False, h == NH - 1)
+        cp(both(64), T.Ms[:, 32:96], T.pM[:, 0:64], "pM.w", "Ms")
         tt(gath(L, "V"), T.LK[:, 0:L], T.Ms[:].indirect(bl), T["AR%d" % t][:, 0:L], A.mult, "Ms " + each("AR%d%%d" % t, NH) + " " + bk, "LK")
         if t == 0:
-            ts(32, T.MK[:], T.Ms[:, 0:64], 0.0, BIG, A.is_gt, A.mult, "Ms", "MK")
+            ts(32, T.MK[:], T.Ms[:, 32:96], 0.0, None, A.is_gt, None, "Ms", "MK")
         to_list(T.pS[:, 0, 0, 0:n], "pS.a", T.LK, L, "LK")
         tt(16, Z(1 + t, n), T.pS[:, 0, 0, 0:n], T.thr[:, 0:n], A.is_lt, "pS.a thr", "got%d" % t)
 
@@ -504,12 +526,12 @@ def rank_program(g, core, T, topo):
     def chunk(t, h, c0, nb, on, ban):
         n, m, L = 2 * nb, 16 * nb, 32 * nb
         a, k0 = 16 * c0, c0 // 2
-        pC = T["pC%d" % h]
+        pC = T["pC%d" % (h % 2)]
         pX, kq = pC[:, 0:nb, :, :], pC[:, 8:8 + nb, :, :]
         half = lambda v: pC[:, 0:nb, :, v:16:2]
         K = lambda s: span(s, c0, c0 + n)
         Kv = lambda s, v: span(s, c0 + nb * v, c0 + nb * v + nb)
-        X, KQ = "pC%d.x" % h, "pC%d.q" % h
+        X, KQ = "pC%d.x" % (h % 2), "pC%d.q" % (h % 2)
         lin(both(L, 0.5, S16), T.Qf[:, a:a + L], T.Q[:, a:a + L], 1.0, -1024.0, K("Q"), K("Qf"))
         mm(L, [(pX, T.thM[:], T.on12[:, 0:L])], "thM on12", X, True, False)
         for b in range(nb):
@@ -545,8 +567,8 @@ def rank_program(g, core, T, topo):
         for v in range(2):
             lin(both(nb, 1.0, S16), bi[:, c0 + nb * v:c0 + nb * v + nb], T.bm[:, a + 16 * v + 15:a + L:32], 65536.0, 0.0, K("bm"), Kv("bi%d_" % t, v))
         if t == 0:
-            ts(n, T.zi[:, 5, cs], bi[:, cs], 1023, None, AND, None, K("bi0_"), K("si"))
-            cp(both(n, 1.0, S16), T.s1[:, cs], T.zi[:, 5, cs], K("si"), K("s1_"))
+            ts(n, T.zi[:, 0, cs], bi[:, cs], 4095, None, AND, None, K("bi0_"), K("b0_"))
+            ts(n, T.s1[:, cs], T.zi[:, 0, cs], -512.0, 1024.0, A.add, A.min, K("b0_"), K("s1_"))
 
     def stuck(t, n, cut):
         cp(both(n, 1.0, S16), T.CS[:, 0, 0:n], T.ci[:, 0:n], span("ci", 0, n), "CS")
@@ -559,14 +581,14 @@ def rank_program(g, core, T, topo):
         cl = T["c%d" % t]
         cp(both(n, 1.0, S16), cl[:, 0:n], T.pS[:, 12, 0, 0:n], "pS.b", "cl%d" % t)
         cp(gath(16 * n), T["OH%d" % t][:, 0:16 * n], ta.indirect(cl[:, 0:n]), TA + "cl%d" % t, span("OH%d_" % t, 0, n))
-        tt(n, Z(9 + t, n), T.pS[:, 13, 0, 0:n], Z(1 + t, n), A.mult, "pS.b got%d" % t, "gs%d" % t)
+        tt(n, T.gs[:, t, 0:n], T.pS[:, 13, 0, 0:n], Z(1 + t, n), A.mult, "pS.b got%d" % t, "gs%d" % t)
 
     def plan(t, L, S, sk):
         tt(gath(L, "V"), T["PL%d" % t][:, 0:L], T.pli[:].indirect(S[:, 0:L // 16]), T["OH%d" % t][:, 0:L], A.mult, "pli0 pli1 pad1 " + span("OH%d_" % t, 0, L // 16) + " " + sk, "PL%d" % t)
 
     def refresh(d, j, a, b):
         at, m = V + (d - 1) * GH, 12 - 4 * (N - d)
-        cp(gath(256 * (b - a)), T.W[:, at + 256 * a:at + 256 * b], SR[d][:].indirect(T.IN[:, j, m + 16 * a:m + 16 * b]), "Sz%d Sp%d Sx%d IN%d" % (d, d, d, j), span("W%d" % d, a, b))
+        cp(gath(256 * (b - a)), T.W[:, at + 256 * a:at + 256 * b], SR[d][:].indirect(T.IN[:, j, m + 16 * a:m + 16 * b]), "Sz%d Sp%d Sx%d IM%d" % (d, d, d, j), span("W%d" % d, a, b))
 
     front(T.L0, "L0 Ls0", CUT[(8, 0)], 0, 8)
     for rnd in range(RO):
@@ -574,26 +596,31 @@ def rank_program(g, core, T, topo):
         L, NH = 16 * n, n // 8
         last = rnd == RO - 1
         LS, LB = "L0 Ls0 Ls1", "L0 Lb0 Lb1"
+        P["at"], P["sites"] = "r%d m0" % NH, {}
         marks_1(0, NH, T.L0, T.L0, 16, LS, LB)
         marks_2(0, NH, T.L0[:, 16:16 + n], LB)
         for h, (c0, nb) in enumerate(CUT[(n, 0)]):
+            P["at"] = "r%d s0%d" % (NH, h)
             chunk(0, h, c0, nb, ON[(n, 0)], "BAN" if rnd > 0 else None)
             front(T.s1, span("s1_", c0, c0 + 2 * nb), CUT[(n, 1)], c0, c0 + 2 * nb)
         BI0, BI1, S1 = span("bi0_", 0, n), span("bi1_", 0, n), span("s1_", 0, n)
+        P["at"] = "r%d m1" % NH
         stuck(0, n, CUT[(n, 0)])
         plan(0, L, T.L0, LS)
-        ts(n, T.zi[:, 0, 0:n], T.bi0[:, 0:n], 4095, None, AND, None, BI0, "b0")
-        ts(n, T.zi[:, 2, 0:n], T.bi0[:, 0:n], 4, 255, SHR, AND, BI0, "sb")
-        lin(both(n), Z(19, n), Z(9, n), -64.0, 64.0, "gs0", "z19")
-        tt(n, T.b1[:, 0:n], Z(19, n), T.zi[:, 2, 0:n], A.max, "z19 sb", "bl1")
-        tt(n, Z(13, n), Z(9, n), T.zi[:, 0, 0:n], A.mult, "gs0 b0", "bg0")
-        tt(n, Z(11, n), Z(1, n), Z(9, n), A.subtract, "got0 gs0", "gd0")
+        tt(n, T.zi[:, 2, 0:n], T.gs[:, 0, 0:n], T.zi[:, 0, 0:n], A.mult, "gs0 " + span("b0_", 0, n), "bg0")
+        lin(both(n), T.b1[:, 0:n], T.zi[:, 2, 0:n], 1.0 / 16, -15.0 / 32, "bg0", "bl1")
+        tt(n, Z(11, n), Z(1, n), T.gs[:, 0, 0:n], A.subtract, "got0 gs0", "gd0")
+        ts(n, T.dI[:, 0, 0:n], T.zi[:, 2, 0:n], 9, None, SHR, None, "bg0", "dI0")
+        tt(gath(48, "V"), T.ff[:, 0, :], T.dI[:, 0, :].indirect(T.rep[:, 0:3]), T.dc[:], A.is_equal, "dI0 rep dc", "ff0")
+        scan(24, T.inc[:, 0, :], T.rrk[:], T.ff[:, 0, :], A.mult, A.add, "rrk ff0", "inc0")
         if not last:
-            ts(n, Z(15, n), Z(13, n), 1024.0, 320.0, A.is_ge, A.mult, "bg0", "ask0")
+            ts(n, Z(15, n), T.zi[:, 2, 0:n], 1536.0, 384.0, A.is_ge, A.mult, "bg0", "ask0")
         marks_1(1, NH, T.s1, T.b1, 0, S1, "bl1")
         marks_2(1, NH, T.b1[:, 0:n], "bl1")
         for h, (c0, nb) in enumerate(CUT[(n, 1)]):
+            P["at"] = "r%d s1%d" % (NH, h)
             chunk(1, h, c0, nb, ON[(n, 1)], "OH0")
+        P["at"] = "r%d end" % NH
         stuck(1, n, CUT[(n, 1)])
         plan(1, L, T.s1, S1)
         YB = [T.pY, T.pB0]
@@ -602,82 +629,91 @@ def rank_program(g, core, T, topo):
             mm([L] + [128] * (2 * NH), [(YB[t][:, 0:L], T.idb[:], T.zer[:, 0:L])] +
                [(YB[t][:, 128 * h:128 * h + 128], x[:, 128 * h:128 * h + 128], y[:]) for h in range(NH) for x, y in ((T["AR%d" % t], T.idB), (T["PL%d" % t], T.BO))],
                "idb zer idB BO PL%d " % t + each("AR%d%%d" % t, NH), YK[t], True, False)
-        bI, dI = T.zi[:, 3, 0:n], T.dI[:, 0:n]
-        ts(n, T.zi[:, 1, 0:n], T.bi1[:, 0:n], 4095, None, AND, None, BI1, "b1")
-        tt(n, Z(14, n), Z(10, n), T.zi[:, 1, 0:n], A.mult, "gs1 b1", "bg1")
-        tt(n, bI, Z(13, n), Z(14, n), A.max, "bg0 bg1", "bI")
-        ts(n, dI, bI, 9, None, SHR, None, "bI", "dI")
-        tt(gath(48, "V"), T.ff[:], T.dI[:].indirect(T.rep[:, 0:3]), T.dc[:], A.is_equal, "dI rep dc", "ff")
-        scan(24, T.inc[:], T.rrk[:], T.ff[:], A.mult, A.add, "rrk ff", "inc")
-        tt(n, Z(12, n), Z(2, n), Z(10, n), A.subtract, "got1 gs1", "gd1")
-        tt(n, T.gd[:, 0:n], Z(11, n), Z(12, n), A.add, "gd0 gd1", "gd")
-        mm(16, [(T.pM[:, 67:128:4], T.idm[:], T.gd[:])], "idm gd", "pM.r3")
-        for d in range(3):
-            o = T.pM[:, 64 + d:128:4]
-            mm(16, [(o, T.tri[:], T.ff[:, 16 * d:16 * d + 16]), (o, T.BO[:], T.inc[:, 16 * d:16 * d + 16])], "tri BO ff inc", "pM.r%d" % d)
-        scan(64, T.fr[:], T.r4[:], T.pM[:, 64:128], A.add, A.min, "r4 pM.r0 pM.r1 pM.r2 pM.r3", "fr")
+        bI, dI = T.zi[:, 3, 0:n], T.zi[:, 5, 0:n]
+        tt(gath(48, "V"), T.DC[:], T.gs[:, 1, :].indirect(T.rep[:, 0:3]), T.dc[:], A.mult, "gs1 rep dc", "DC")
+        ts(n, T.dI[:, 1, 0:n], T.bi1[:, 0:n], 9, 7, SHR, AND, BI1, "dI1")
+        tt(gath(48, "V"), T.ff[:, 1, :], T.dI[:, 1, :].indirect(T.rep[:, 0:3]), T.DC[:], A.is_equal, "dI1 rep DC", "ff1")
+        scan(24, T.inc[:, 1, :], T.rrk[:], T.ff[:, 1, :], A.mult, A.add, "rrk ff1", "inc1")
+        tt(n, Z(12, n), Z(2, n), T.gs[:, 1, 0:n], A.subtract, "got1 gs1", "gd1")
+        tt(n, T.gd[:, 3:4 * n:4], Z(11, n), Z(12, n), A.add, "gd0 gd1", "gd")
+        mm(64, [(T.pM[:, 64:128], T.idm[:], T.gd[:])], "idm gd", "pM.r", True, False)
+        for t in range(2):
+            for x, y, k in ((T.tri, T.ff, "ff"), (T.BO, T.inc, "inc")):
+                mm(16, [(T.pM[:, 64 + d:128:4], x[:], y[:, t, 16 * d:16 * d + 16]) for d in range(3)], "tri BO %s%d" % (k, t), "pM.r", False, t == 1 and k == "inc")
+        add(P, {"V": plain(64)}, lambda q, e: q.tensor_tensor_scan(T.fr[:], T.r4[:], T.pM[:, 64:128], -207.0, A.max, A.min), "r4 pM.r", "fr")
         tt(gath(L, "V"), T.D[:, 0:L], T.fr[:].indirect(T.bc[:, 16:16 + n]), T.THD[:, 0:L], A.is_le, "fr bc THD", "D")
         for t in range(2):
             mm(128, [(YB[t][:, 128 * h:128 * h + 128], T.D[:, 128 * h:128 * h + 128], T.BOK[:]) for h in range(NH)], "BOK D", YK[t], False, True)
         if not last:
-            lin(both(n, 1.0, S16), Z(26, n), dI, 64.0, 0.0, "dI", "z26")
+            ts(n, T.zi[:, 1, 0:n], T.bi1[:, 0:n], 4095, None, AND, None, BI1, "b1")
+            tt(n, Z(14, n), T.gs[:, 1, 0:n], T.zi[:, 1, 0:n], A.mult, "gs1 b1", "bg1")
+            tt(n, bI, T.zi[:, 2, 0:n], Z(14, n), A.max, "bg0 bg1", "bI")
+            ts(n, dI, bI, 9, None, SHR, None, "bI", "dI")
+            lin(both(n, 1.0, S16), Z(26, n), dI, 64.0, 255.0, "dI", "z26")
             tt(n, Z(25, n), Z(26, n), Z(15, n), A.add, "z26 ask0", "z25")
             ts(n, T.XI[:, 0:n], bI, 511, None, AND, None, "bI", "XI")
-            ts(n, Z(27, n), T.fr[:, 3:4 * n:4], 255.0, 48.0, A.add, A.min, "fr", "z27")
-            tt(n, T.SL[:, 0:n], Z(25, n), Z(27, n), A.add, "z25 z27", "SL")
+            tt(n, T.SL[:, 0:n], Z(25, n), T.fr[:, 3:4 * n:4], A.add, "z25 fr", "SL")
             cp(gath(L), T.AO[:, 256:256 + L], T.tc[:].indirect(T.SL[:, 0:n]), "tc tc1 SL", "AO1")
             cp(gath(L), T.AO[:, 0:L], ta.indirect(T.SL[:, 0:n]), TA + "SL", "AO0")
             tt(gath(L, "V"), T.DX[:, 0:L], T.XI[:, 0:n].indirect(T.bc[:, 0:n]), T.ta[:, 0:L], A.mult, "XI bc ta", "DX")
+            part = lambda x, h: x[:, 128 * h:128 * h + 128]
+            mm([2 * L] + [128] * (2 * NH), [(T.pS[:, 0:8 * NH, :, :], T.idb[:], T.zer[:, 0:2 * L])] +
+               [(T.pS[:, 8 * h:8 * h + 8, 1, :], part(x, h), y[:]) for h in range(NH) for x, y in ((T.OH0, T.Cm0), (T.OH1, T.Cm1))],
+               "idb zer Cm0 Cm1 " + span("OH0_", 0, n) + " " + span("OH1_", 0, n), "pS.a pS.b", True, False)
+            mm(128, [(T.pS[:, 8 * h:8 * h + 8, 0, :], part(T.DX, h), T.nBO[:]) for h in range(NH)], "nBO DX", "pS.a pS.b", False, False)
+            mm(256, [(T.pS[:, 8 * h:8 * h + 8, :, :], part(T.AO, 2 + h), T.RX[:]) for h in range(NH)], "RX0 RX1 AO1", "pS.a pS.b", False, True)
             for h in range(NH):
-                a, b = 128 * h, 128 * h + 128
-                o = T.pS[:, 8 * h:8 * h + 8, 0, :]
-                mm(128, [(o, T.DX[:, a:b], T.nBO[:]), (o, T.AO[:, 256 + a:256 + b], T.idB[:])], "idB nBO AO1 DX", "pS.a" if h == 0 else "pS.b")
-                o = T.pS[:, 8 * h:8 * h + 8, 1, :]
-                mm(128, [(o, T.OH0[:, a:b], T.Cm0[:]), (o, T.OH1[:, a:b], T.Cm1[:]), (o, T.AO[:, 256 + a:256 + b], T.idB1[:])],
-                   "idB1 Cm0 Cm1 AO1 " + span("OH0_", 0, n) + " " + span("OH1_", 0, n), "pS.c%d" % h)
-                mm(128, [(T.pA[:, a:b], T.AO[:, a:b], T.idb[:])], "idb AO0", "pA.a%d" % h)
+                mm(128, [(part(T.pA, h), part(T.AO, h), T.idb[:])], "idb AO0", "pA.a%d" % h)
             cp(both(L), T.AW[:, 0:64 * NH:8, :], T.pA[:, 0:L], each("pA.a%d", NH), each("AW%d", NH))
         for t in range(2):
-            relu(both(L, 1.0, S16), T.AF[:, 128 * t:128 * t + 64 * NH:8, :], YB[t][:, 0:L], 16.0 - 32768.0 - 4096.0, YK[t], "AF%d AF%d" % (2 * t, 2 * t + 1))
+            relu(both(L, 1.0, S16), T.AF[:, 128 * t:128 * t + 64 * NH:8, :], YB[t][:, 0:L], 1024.0 - 32768.0 - 4096.0, YK[t], "AF%d AF%d" % (2 * t, 2 * t + 1))
             mm(64, [(T.pM[:, 128:192], T.AF[:, 128 * t + 64 * h + 7 * k:128 * t + 64 * h + 7 * k + 8, :], T["B%d" % t][:, 512 * h + 64 * k:512 * h + 64 * k + 64])
                     for h in range(NH) for k in range(8)], "AF%d AF%d " % (2 * t, 2 * t + 1) + each("B%d%%d" % t, NH), "pM.m", t == 0, t == 1)
         if not last:
-            relu(both(2 * L, 1.0, S16), T.X[:, 0:2 * L], T.pS[:, 0:8 * NH, :, :], 1024.0 - 32768.0, "pS.a pS.b pS.c0 pS.c1", "X")
+            relu(both(2 * L, 1.0, S16), T.X[:, 0:2 * L], T.pS[:, 0:8 * NH, :, :], 1024.0 - 32768.0, "pS.a pS.b", "X")
             mm(32, [(T.pA[:, 256:288], T.AW[:, 64 * h + 7 * k:64 * h + 7 * k + 8, :], T.X[:, 256 * h + 32 * k:256 * h + 32 * k + 32])
                     for h in range(NH) for k in range(8)], "AW0 AW1 X", "pA.o")
-        ts(64, T.kp0[:], T.pM[:, 128:192], 0.5, None, A.is_lt, None, "pM.m", "kp0")
-        tt(128, T.kp[:], T.kp0[:], T.mp[:], A.mult, "kp0 mp", "kp")
+        tt(32, T.MSG[:, rnd, 0:32], T.pM[:, 128:160], T.mp[:, 0:32], A.max, "pM.m mp", "MSG0")
+        tt(32, T.mp16[:, 0:32], T.pM[:, 160:192], T.mp[:, 32:64], A.max, "pM.m mp", "mp16")
         if not last:
-            tt(32, T.MSG[:, rnd, 0:32], T.pM[:, 128:160], T.kp[:, 0:32], A.add, "pM.m kp", "MSGm")
-            cp(both(32, 1.0, S16), T.MSG[:, rnd, 32:64], T.pA[:, 256:288], "pA.o", "MSGo")
-            per = len(chip) // len(far)
-            ls[0] += remote([(h, chip[i * per:(i + 1) * per], "hm%d" % rnd, T.MSG[:, rnd, :], T.HM[:, rnd, :]) for i, h in enumerate(close)], "ls", "MSGm MSGo", "msg")
-            for q in near:
-                d = (rank - q) % N
-                j = 3 * rnd + d - 1
-                ls[0] += remote([(T.cores[q], out_e, "m%d" % j, T.MSG[:, rnd, :], T.IN[:, j, 12 - 4 * d:76 - 4 * d])], "ls", "", "msg2")
-            for d in range(1, N):
-                lands("m%d" % (3 * rnd + d - 1), len(out_e), "msg", "IN%d" % (3 * rnd + d - 1), 1.2 if (rank + d) % N in near else 2)
-        tt(64, T.mp16[:], T.pM[:, 128:192], T.kp[:], A.add, "pM.m kp", "mp16")
-        cp(gath(GH), T.W[:, 0:GH], T.S0[:].indirect(T.mp16[:, 0:32]), "Sz0 Sp0 Sx0 mp16 sent", "Wa")
-        cp(gath(GH), T.W[:, GH:V], T.S0[:].indirect(T.mp16[:, 32:64]), "Sz0 Sp0 Sx0 mp16", "Wb")
+            cp(both(32, 1.0, S16), T.MSG[:, rnd, 32:64], T.pA[:, 256:288], "pA.o", "MSG1")
+            for u in range(2):
+                piece = lambda x, k, o: x[:, k, o + 32 * u:o + 32 * u + 32]
+                on = chip if u == 0 else [e for e in chip if e not in out_e]
+                per = len(on) // len(far)
+                over = [(h, on[i * per:(i + 1) * per], "hm%d" % (2 * rnd + u), piece(T.MSG, rnd, 0), piece(T.HM, rnd, 0)) for i, h in enumerate(close)]
+                straight = []
+                for q in near:
+                    d = (rank - q) % N
+                    j = 3 * rnd + d - 1
+                    straight.append((T.cores[q], out_e, "m%d" % (2 * j + u), piece(T.MSG, rnd, 0), piece(T.IN, j, 12 - 4 * d)))
+                for items in ([over, straight] if u == 0 else [over + straight]):
+                    ls[0] += remote(items, "ls", "MSG%d" % u, "msg%d" % u)
+                for d in range(1, N):
+                    j = 3 * rnd + d - 1
+                    lands("m%d" % (2 * j + u), len(out_e), "msg%d" % u, ("IM%d", "IN%d")[u] % j, 1.0 if (rank + d) % N in near else 1.9)
+        P["at"] = "last" if last else "front"
+        cp(gath(GH), T.W[:, 0:GH], T.S0[:].indirect(T.MSG[:, rnd, 0:32]), "Sp0 Sx0 MSG0 sent", "Wa")
+        cp(gath(GH), T.W[:, GH:V], T.S0[:].indirect(T.mp16[:, 0:32]), "Sp0 Sx0 mp16", "Wb")
         if last:
             dma("S", T.y[:, 0:GH], T.W[:, 0:GH], "Wa", "ya")
             dma("Y", T.y[:, GH:V], T.W[:, GH:V], "Wb", "yb")
             break
-        cp(both(64, 1.0, S16), T.mp[:], T.mp16[:], "mp16", "mp")
-        tt(128, T.FZ[:], T.kp0[:], T.MK[:], A.mult, "kp0 MK", "FZ")
+        tt(64, T.FZ[:], T.pM[:, 128:192], T.MK[:], A.is_lt, "pM.m MK", "FZ")
         requests(rnd + 1)
         front(T.L0, "L0 Ls0", CUT[(16, 0)], 0, 6)
         j0 = 3 * rnd
         INS = "IN%d IN%d IN%d" % (j0, j0 + 1, j0 + 2)
         for d in range(1, N):
             refresh(N - d, j0 + d - 1, 0, 2)
+        for d in (2, 1, 3, 0):
+            if d == 0 or rnd < RO - 2:
+                keep(d)
         ts(9, T.L0[:, 7:16], T.IN[:, j0:j0 + 3, 40:43], -1.0, 1024.0, A.mult, A.add, "L0 " + INS, "Ls1")
         cp(9, T.L0[:, 39:48], T.IN[:, j0:j0 + 3, 56:59], "L0 " + INS, "Lc1")
         front(T.L0, LS, CUT[(16, 0)], 6, 16)
         cp(gath(160), T.BAN[:, 96:256], T.ta[:].indirect(T.L0[:, 38:48]), TA + "tao L0 Lc1", span("BAN_", 6, 16))
-        ts(9, T.L0[:, 23:32], T.L0[:, 7:16], 1.0 / 16, -15.0 / 32, A.mult, A.add, LS, "Lb1")
+        ts(9, T.L0[:, 23:32], T.L0[:, 7:16], 1.0 / 16, 32 - 15.0 / 32, A.mult, A.add, LS, "Lb1")
 
     issue(P, eng, T)
     g.wait_ge(T.sem.ls, ls[0])

@@ -1,4 +1,5 @@
 import math
+import numpy as np
 from concourse.bass import DstId, RemoteDMATransfer
 from concourse.mybir import AluOpType as A, ActivationFunctionType as F
 
@@ -6,19 +7,14 @@ V, GH, RO = 1024, 512, 4
 BIG = 2.0 ** 94
 LNB = math.log(1.75)
 LN0 = 90 * math.log(2.0)
-WAKE, GATHER, PE, LOAD, HOP = 130, 1.56, 0.72, 2400, 2400
-SPARE, LAG, CUTS, PASSES, FIX = 1.0, 2, 1, 2, 36
-ON = {(8, 0): "----", (8, 1): "----", (16, 0): "VSVSSSSS", (16, 1): "SSSSSSSS"}
-CUT = {(8, 0): [(0, 4)], (8, 1): [(0, 4)], (16, 0): [(0, 4), (8, 4)], (16, 1): [(0, 4), (8, 4)]}
-S16 = "VS"
-FIXS = 70
-AT = {'last Wa 1': 'S', 'last Wb 1': 'V', 'front Wa 1': 'S', 'front Wb 1': 'V', 'front W 1': 'S', 'front W 3': 'V', 'r2 end AF 1': 'S', 'r2 end AF 2': 'S',
-      'r2 end AO 1': 'S', 'r2 end AO 2': 'V', 'front W 2': 'S', 'front Q 3': 'V', 'front Q 4': 'V', 'front CK 4': 'V', 'front Q 5': 'V', 'r2 m0 AW 2': 'S',
-      'r2 m1 bl 1': 'S', 'r2 m1 B 1': 'S', 'r2 s11 ki 1': 'S', 'r1 s00 ki 1': 'V', 'r1 m1 ht 1': 'S', 'r1 m1 bl 1': 'S'}
-SITES = []
-FAR0, NEAR0 = 2.2, 1.3
-PARTS = 2
-ENDS = []
+WAKE, CROSS, GATHER, PE, FIX, FIXS, LOAD, HOP = 130, 0, 1.56, 0.72, 36, 70, 2400, 2400
+FAR0, NEAR0, FAR1, NEAR1, PT0 = 2.5, 1.3, 1.75, 1.0, 2.0
+SPARE, TRIES, WARM, SEED = 1.0, (2000, 13000), 300.0, 1
+CUT = {8: [(0, 4)], 16: [(0, 4), (8, 4)]}
+START = {"r2 s00": "VSVS", "r2 s01": "SSSS", "r2 s10": "SSSS", "r2 s11": "SSSS"}
+WIDE = {"r2 s01": (2, 0, 2, 0), "r2 s10": (2, 0, 2, 0), "r2 s11": (2, 0, 1, 1)}
+TURN = {"r2 s00": (0, 2, 0, 2), "r2 s01": (0, 2, 0, 2), "r2 s10": (0, 2, 0, 2), "r2 s11": (0, 2, 1, 1)}
+LAID, ENDS = {}, []
 
 
 def _sb(n, d="float32"):
@@ -28,26 +24,26 @@ def _sb(n, d="float32"):
 H, I32, U16, F16 = "bfloat16", "int32", "uint16", "float16"
 SCRATCH = {
     "W": _sb(2560, H), "S0": _sb(2048, H), "S1": _sb(2048, H), "S2": _sb(2048, H), "S3": _sb(2048, H),
-    "nbi": _sb(V + 16, I32), "pti": _sb(V, I32), "pli": _sb(V + 16, I32), "cst": _sb(V + 16),
+    "nbi": _sb(V + 16, I32), "pti": _sb(V, I32), "pli": _sb(V + 16, I32), "cst": _sb(V + 16, I32),
     "rq": _sb(28, I32), "rqb": _sb(28, I32), "thi": _sb(4, I32), "col": _sb(20), "coli": _sb(4, I32),
-    "row": _sb(144), "rowg": _sb(128), "rowj": _sb(128), "Rc": _sb(512, H),
-    "idb": _sb(128, H), "id12": _sb(128, H), "id4": _sb(128, H), "idB": _sb(128, H), "RX": _sb([8, 2, 16], H), "idF": _sb(128, H), "idm": _sb(128, H), "id32": _sb(128),
-    "thM": _sb(128, F16), "on12": _sb(256, H), "zer": _sb(512, H), "THD": _sb(256, H),
+    "row": _sb(144), "rowg": _sb(128), "rowj": _sb(128), "Rc": _sb(512, H), "RA": _sb(128, H), "RX": _sb([8, 2, 16], H),
+    "idb": _sb(128, H), "id12": _sb(128, H), "id4": _sb(128, H), "idB": _sb(128, H), "idF": _sb(128, H), "idm": _sb(128, H), "idw": _sb(128, H), "id32": _sb(128),
+    "thM": _sb(128, F16), "on12": _sb(128, H), "zer": _sb(592, H), "tx": _sb(512),
     "BOc": _sb(128, H), "Cm0": _sb(128, H), "Cm1": _sb(128, F16),
     "BO": _sb(128, H), "nBO": _sb(128, H), "BOK": _sb(128, H), "tri": _sb(128, H), "EE": _sb(144, H), "SWs": _sb([4, 128], H), "SWb": _sb([4, 128], H),
-    "ta": _sb(1296, H), "taf": _sb(256), "tb": _sb(192, H), "tba": _sb(64), "tbb": _sb(64), "tcf": _sb(384), "tc": _sb(768, H),
-    "bci": _sb(32, I32), "bc": _sb(32, U16), "rep": _sb(4, U16), "dc": _sb(48), "r4": _sb(64),
-    "rmin": _sb(256), "rmax": _sb(256), "rrk": _sb(48, H), "offc": _sb(16, I32), "wi": _sb(32), "wcol": _sb(2), "thr": _sb(16),
-    "mp": _sb(64), "mp16": _sb(64, U16), "FZ": _sb(64, H), "MK": _sb(64, H), "Ms": _sb(192, H), "DC": _sb(48),
+    "ta": _sb(1296, H), "taf": _sb(256), "tb": _sb(192, H), "tba": _sb(128), "tcf": _sb(384, H), "tc": _sb(768, H), "sel": _sb(128, H),
+    "bc": _sb(36, U16), "dc": _sb(48), "r4": _sb(64),
+    "rmin": _sb(128), "rmax": _sb(128), "rrk": _sb(48, H), "offc": _sb(8, I32), "wi": _sb(32), "wcol": _sb(2), "thr": _sb(16),
+    "mp": _sb(64), "mp16": _sb(32, U16), "FZ": _sb(64, H), "MK": _sb(64, H), "Ms": _sb(192, H), "DC": _sb(48),
     "AW": _sb([128, 16], H), "AF": _sb([256, 16], F16),
-    "L0": _sb(48, U16), "s1": _sb(16, U16), "b1": _sb(16, U16), "c0": _sb(16, U16), "c1": _sb(16, U16),
+    "L0": _sb(50, U16), "s1": _sb(16, U16), "b1": _sb(16, U16), "cl": _sb([2, 16], U16),
     "Q": _sb(256, U16), "Qf": _sb(256, F16), "CK": _sb(256), "BAN": _sb(256, H),
     "OH0": _sb(256, H), "OH1": _sb(256, H), "G": _sb(4096, H), "GT": _sb(4096, H),
-    "ov": _sb(256), "kR": _sb([8, 2, 16]), "kT": _sb(256), "km": _sb(256), "ki": _sb(16, I32), "ci": _sb(16, I32), "off": _sb(16, U16),
-    "CS": _sb([2, 16], H), "K1": _sb(256, H), "K1T": _sb(256), "bm": _sb(256), "bi0": _sb(16, I32), "bi1": _sb(16, I32),
+    "ov": _sb(256), "kR": _sb([8, 2, 16]), "kT": _sb(256), "km": _sb(256), "ki": _sb([2, 16], I32), "off": _sb(16, U16),
+    "CS": _sb([2, 16], H), "K1": _sb(256), "kq": _sb(256), "K1T": _sb(256), "bm": _sb(256), "bi": _sb(16, I32), "bj": _sb([2, 2, 4], I32),
     "AR0": _sb(256, H), "AR1": _sb(256, H), "FB": _sb(256, H), "B0": _sb(1024, H), "B1": _sb(1024, H), "LK": _sb(256, H), "PL0": _sb(256, F16), "PL1": _sb(256, F16),
-    "z": _sb([32, 16]), "zi": _sb([6, 16], I32), "dI": _sb([2, 16], I32), "gs": _sb([2, 16]), "gd": _sb(64, H), "ff": _sb([2, 48], H), "inc": _sb([2, 48], H), "fr": _sb(64), "XI": _sb(16, I32), "SL": _sb(16, U16),
-    "D": _sb(256, H), "DX": _sb(256, F16), "AO": _sb(512, H), "X": _sb(512, F16),
+    "z": _sb([12, 16]), "zi": _sb([5, 16], I32), "dI": _sb([2, 16], I32), "gs": _sb([4, 16], H), "idk": _sb([7, 128], H), "ff": _sb([2, 48], H), "inc": _sb([2, 48], H),
+    "fr": _sb(64), "XI": _sb(16, I32), "SL": _sb(16, U16), "DX": _sb(256, F16), "AO": _sb(256, H), "X": _sb(512, F16),
     "MSG": _sb([4, 64], U16), "IN": _sb([9, 72], U16), "HB": _sb(128, H), "HM": _sb([3, 64], U16),
 }
 for _p in ("pA", "pB0", "pB1", "pM", "pY"):
@@ -108,15 +104,11 @@ def helper(g, core, T, topo):
         d = (r - q) % n
         for t in range(RO - 1):
             j = 3 * t + d - 1
-            for u in range(PARTS):
-                w = 64 // PARTS
-                g.wait_ge(T.sem["hm%d" % (2 * t + u)], (len(topo.engines(own[0], core)) - u * len(es)) // len(far))
-                ls += send(g, T, topo, core, [(T.cores[q], es, "m%d" % (2 * j + u), T.HM[:, t, w * u:w * u + w], T.IN[:, j, 12 - 4 * d + w * u:12 - 4 * d + w * u + w])], "ls")
+            for u in range(2):
+                g.wait_ge(T.sem["hm%d" % (2 * t + u)], len(topo.engines(own[0], core)) // len(far))
+                a = 12 - 4 * d + 32 * u
+                ls += send(g, T, topo, core, [(T.cores[q], es, "m%d" % (2 * j + u), T.HM[:, t, 32 * u:32 * u + 32], T.IN[:, j, a:a + 32])], "ls")
     g.wait_ge(T.sem.ls, ls)
-
-
-def new_plan():
-    return {"ops": [], "lastw": {}, "reads": {}, "chain": {}, "pin": {}, "at": "set", "sites": {}}
 
 
 def add(P, cost, fn, R, Wr, lat=0, tok=None, start=False, stop=False):
@@ -133,9 +125,9 @@ def add(P, cost, fn, R, Wr, lat=0, tok=None, start=False, stop=False):
             dep[a] = dep.get(a, False) or not (onP and "P" in P["ops"][a]["cost"])
         for a in P["reads"].get(x, []):
             dep[a] = True
-    banks = set(x.split(".")[0] for x in R + Wr if x[0] == "p" and x[1].isupper())
+    banks = sorted(set(x.split(".")[0] for x in R + Wr if x[0] == "p" and x[1].isupper()))
     for b in banks:
-        if onP and b not in ("pA", "pB1"):
+        if onP and b != "pA":
             if start and b in P["chain"]:
                 dep.setdefault(P["chain"][b], False)
             if stop:
@@ -151,73 +143,124 @@ def add(P, cost, fn, R, Wr, lat=0, tok=None, start=False, stop=False):
     for x in Wr:
         P["lastw"][x] = k
         P["reads"][x] = []
-    if len(cost) > 1:
-        site = P["at"] + " " + Wr[0].rstrip("0123456789_")
-        P["sites"][site] = P["sites"].get(site, 0) + 1
-        site += " %d" % P["sites"][site]
-        SITES.append(site)
-        if AT.get(site, "-") in cost:
-            cost = {AT[site]: cost[AT[site]]}
-    P["ops"].append({"cost": cost, "fn": fn, "dep": dep, "lat": lat, "tok": tok, "banks": banks})
-    return k
+    site = P["at"] + " " + Wr[0].rstrip("0123456789_")
+    P["sites"][site] = P["sites"].get(site, 0) + 1
+    P["ops"].append({"site": "%s %d" % (site, P["sites"][site]), "cost": cost, "fn": fn, "dep": dep, "lat": lat, "tok": tok, "banks": banks})
 
 
 def lay(P):
     ops = P["ops"]
     n = len(ops)
+    before = [[(a, (WAKE + ops[a]["lat"]) if w else 0) for a, w in o["dep"].items()] for o in ops]
     rest = [0.0] * n
     for k in range(n - 1, -1, -1):
-        o = ops[k]
-        rest[k] += min(o["cost"].values())
-        for a, w in o["dep"].items():
-            rest[a] = max(rest[a], rest[k] + ((WAKE + ops[a]["lat"]) if w else 0))
-    before = [[(a, (WAKE + ops[a]["lat"]) if w else 0) for a, w in o["dep"].items()] for o in ops]
-    behind = [[] for o in ops]
-    for k in range(n):
+        rest[k] += min(ops[k]["cost"].values())
         for a, d in before[k]:
-            behind[a].append((k, d))
+            rest[a] = max(rest[a], rest[k] + d + (CROSS if d == WAKE and not set(ops[a]["cost"]) & set(ops[k]["cost"]) else 0))
+    site = [o["site"] for o in ops]
+    ways_ = [list(o["cost"].items()) for o in ops]
 
-    def place(order, edges):
-        line, bank, at = {}, {}, {}
-        for k in order:
-            o = ops[k]
-            t0 = max([at[a][1] + d for a, d in edges[k]] + [0.0])
+    def late(line, t, pad):
+        i = len(line)
+        while i > 0 and line[i - 1][1] + pad > t:
+            i -= 1
+        return line[i:]
+
+    def enter(line, x):
+        i = len(line)
+        while i > 0 and line[i - 1][0] > x[0]:
+            i -= 1
+        line.insert(i, x)
+
+    def place(on, up, a0, a1, start=None):
+        if start is None:
+            line, bank, at, key, end = {e: [] for e in ("V", "S", "P", "G", "Y", "far")}, {}, [None] * n, [0.0] * n, 0.0
+        else:
+            end, at, key = start[0], list(start[1]), list(start[4])
+            bank, line = {b: x[-40:] for b, x in start[2].items()}, {e: x[-150:] for e, x in start[3].items()}
+            if a1 == n:
+                bank = {b: list(x) for b, x in start[2].items()}
+        for k in range(a0, a1):
+            x = -rest[k] - up.get(site[k], 0)
+            for a, d in before[k]:
+                if key[a] >= x:
+                    x = key[a] + 1e-3
+            key[k] = x
+        for k in sorted(range(a0, a1), key=lambda k: key[k]):
             best = None
-            for e, c in o["cost"].items():
-                busy = [x for x in line.get(e, []) if x[1] > t0] if e != "far" else []
-                for bk in o["banks"]:
-                    busy += [(a - WAKE, b + WAKE) for a, b, e2, _k in bank.get(bk, []) if e2 != e and b + WAKE > t0]
+            for e, c in ways_[k]:
+                if len(ways_[k]) > 1 and on.get(site[k], e) != e:
+                    continue
+                t0 = 0.0
+                for a, d in before[k]:
+                    x = at[a][1] + (d + CROSS if d == WAKE and at[a][2] != e else d)
+                    if x > t0:
+                        t0 = x
+                busy = late(line[e], t0, 0) if e != "far" else []
+                if ops[k]["banks"]:
+                    busy = sorted(busy + [(a - WAKE - CROSS, b + WAKE + CROSS) for bk in ops[k]["banks"] for a, b, e2, j in late(bank.setdefault(bk, []), t0, WAKE + CROSS) if e2 != e])
                 t = t0
-                for a, b in sorted(busy):
+                for a, b in busy:
                     if t + c <= a:
                         break
-                    t = max(t, b)
-                if best is None or t + c + (SPARE * c if e == "V" else 0) < best[0]:
-                    best = (t + c + (SPARE * c if e == "V" else 0), t, t + c, e)
+                    if b > t:
+                        t = b
+                by = t + c + (SPARE * c if e == "V" else 0)
+                if best is None or by < best[0]:
+                    best = (by, t, t + c, e)
             at[k] = best[1:]
-            line.setdefault(best[3], []).append(best[1:3])
-            for bk in o["banks"]:
-                bank.setdefault(bk, []).append(best[1:] + (k,))
-        return at, bank, max(at[k][1] + ops[k]["lat"] for k in range(n))
+            enter(line[best[3]], best[1:3])
+            for bk in ops[k]["banks"]:
+                enter(bank[bk], best[1:] + (k,))
+            end = max(end, best[2] + ops[k]["lat"])
+        return end, at, bank, line, key
 
-    at, bank, end = place(sorted(range(n), key=lambda k: (-rest[k], k)), before)
-    now = at
-    for _ in range(PASSES):
-        back = place(sorted(range(n), key=lambda k: (-now[k][1], -k)), behind)[0]
-        now, bk2, end2 = place(sorted(range(n), key=lambda k: (-back[k][1], k)), before)
-        if end2 < end:
-            at, bank, end = now, bk2, end2
-    for k in range(n):
-        ops[k]["t0"], ops[k]["t1"], ops[k]["e"] = at[k]
+    def anneal(on, up, names, worth, tries):
+        free = [x for x in dict.fromkeys(site[k] for k in range(n) if len(ways_[k]) > 1) if x in names]
+        now = worth(on, up)
+        best = (now, on, up)
+        for it in range(tries):
+            on2, up2 = dict(on), dict(up)
+            for _ in range((1, 1, 2, 3)[rng.randint(4)]):
+                if rng.rand() < 0.35:
+                    x, e = free[rng.randint(len(free))], "VS-"[rng.randint(3)]
+                    if e == "-":
+                        on2.pop(x, None)
+                    else:
+                        on2[x] = e
+                else:
+                    x = names[rng.randint(len(names))]
+                    up2[x] = (up2.get(x, 0) + (-1500, -600, -300, 300, 600, 1500, 3000)[rng.randint(7)]) if rng.rand() < 0.4 else 0
+            end = worth(on2, up2)
+            if end <= now + WARM * (1 - it / tries) * rng.rand() ** 3:
+                now, on, up = end, on2, up2
+                if end < best[0]:
+                    best = (end, on, up)
+        return best[1:]
+
+    head = min(k for k in range(n) if site[k].startswith("front"))
+    mark = min(k for k in range(n) if site[k] == "r2 s01 ov 1")
+    upto = min(k for k in range(mark, n) if site[k].startswith("r2 m1"))
+    shape = tuple(o["lat"] for o in ops)
+    rng = np.random.RandomState(SEED)
+    if shape not in LAID:
+        on, up = {"%s G %d" % (s, i + 1): e for s, es in START.items() for i, e in enumerate(es)}, {}
+        on.update({"last Wa 1": "S", "last Wb 1": "V"})
+        on, up = anneal(on, up, list(dict.fromkeys(site[:head])), lambda on, up: place(on, up, head, upto, place(on, up, 0, head))[1][mark][1], TRIES[0])
+        start = place(on, up, 0, head)
+        LAID[shape] = anneal(on, up, list(dict.fromkeys(site[head:])), lambda on, up: place(on, up, head, n, start)[0], TRIES[1])
+    end, at, bank = place(*LAID[shape], head, n, place(*LAID[shape], 0, head))[:3]
     ENDS.append(end)
-    for bk, uses in bank.items():
+    for k in range(n):
+        ops[k]["e"] = at[k][2]
+    for uses in bank.values():
         last = {}
-        for a, b, e, k in sorted(uses):
+        for a, b, e, k in uses:
             for e2, k2 in last.items():
                 if e2 != e:
                     ops[k]["dep"][k2] = True
             last[e] = k
-    return sorted(range(n), key=lambda k: (ops[k]["t0"], ops[k]["t1"], k))
+    return sorted(range(n), key=lambda k: (at[k][0], at[k][1], k))
 
 
 def issue(P, eng, T):
@@ -226,18 +269,18 @@ def issue(P, eng, T):
     for k in lay(P):
         o = ops[k]
         e = o["e"]
+        if e == "far":
+            cnt[o["tok"][0]] = o["tok"][1]
+            continue
         need = {}
         for a, w in o["dep"].items():
-            if w and ops[a]["tok"] and e != "far":
+            if w and ops[a]["tok"]:
                 s, v = ops[a]["tok"]
                 need[s] = max(need.get(s, 0), v)
         for s, v in need.items():
             if seen.get((e, s), 0) < v:
                 eng[e].wait_ge(T.sem[s], v)
                 seen[(e, s)] = v
-        if e == "far":
-            cnt[o["tok"][0]] = o["tok"][1]
-            continue
         out = o["fn"](eng[e], e)
         if o["tok"]:
             out.then_inc(T.sem[o["tok"][0]], o["tok"][1])
@@ -261,11 +304,12 @@ def rank_program(g, core, T, topo):
     N = len(T.cores)
     near, far, hands, close = ways(T, topo, rank)
     eng = {"V": g.vector, "S": g.scalar, "P": g.tensor, "G": g, "Y": g.sync}
-    P = new_plan()
-    nd, ls = [0], [0]
-    plain = lambda n, r=1.0: max(64.0, n * r) + FIX
+    P = {"ops": [], "lastw": {}, "reads": {}, "chain": {}, "pin": {}, "at": "set", "sites": {}}
+    nd, ls, big = [0], [0], []
+    plain = lambda n: max(64.0, n) + FIX
     gath = lambda n, es="VS": {e: (60 if e == "V" else 78) + GATHER * n for e in es}
-    both = lambda n, r=1.0, es="VS": {e: plain(n, r) if e == "V" else plain(n) + FIXS for e in es}
+    both = lambda n, r=1.0: {"V": plain(n * r), "S": plain(n) + FIXS}
+    vec = lambda n: n if isinstance(n, dict) else {"V": plain(n)}
 
     def dma(e, out, in_, R, Wr, lat=1.0):
         s = "d%d" % nd[0]
@@ -276,17 +320,16 @@ def rank_program(g, core, T, topo):
         add(P, {"far": 1}, None, R, key, lat * HOP, (s, n))
 
     def ts(n, out, in0, s1, s2, o0, o1, R, Wr):
-        c = n if isinstance(n, dict) else {"V": plain(n)}
         if o1 is None:
-            add(P, c, lambda q, e: q.tensor_scalar(out, in0, s1, None, o0), R, Wr)
+            add(P, vec(n), lambda q, e: q.tensor_scalar(out, in0, s1, None, o0), R, Wr)
         else:
-            add(P, c, lambda q, e: q.tensor_scalar(out, in0, s1, s2, o0, o1), R, Wr)
+            add(P, vec(n), lambda q, e: q.tensor_scalar(out, in0, s1, s2, o0, o1), R, Wr)
 
     def tt(n, out, a, b, o, R, Wr):
-        add(P, n if isinstance(n, dict) else {"V": plain(n)}, lambda q, e: q.tensor_tensor(out, a, b, o), R, Wr)
+        add(P, vec(n), lambda q, e: q.tensor_tensor(out, a, b, o), R, Wr)
 
-    def cp(n, out, a, R, Wr):
-        add(P, n if isinstance(n, dict) else {"V": plain(n)}, lambda q, e: q.tensor_copy(out, a) if e == "V" else q.activation(out, a, F.Copy), R, Wr)
+    def cp(c, out, a, R, Wr):
+        add(P, vec(c), lambda q, e: q.tensor_copy(out, a) if e == "V" else q.activation(out, a, F.Copy), R, Wr)
 
     def lin(c, out, a, scale, bias, R, Wr):
         add(P, c, lambda q, e: q.tensor_scalar(out, a, scale, bias, A.mult, A.add) if e == "V" else q.activation(out, a, F.Identity, bias=bias, scale=scale), R, Wr)
@@ -297,19 +340,19 @@ def rank_program(g, core, T, topo):
     def act(c, out, a, f, R, Wr):
         add(P, {"S": c}, lambda q, e: q.activation(out, a, f), R, Wr)
 
-    def mm(n, items, R, Wr, start=True, stop=True):
+    def mm(n, items, R, Wr, start=True, stop=True, least=64):
         m = len(items)
-        c = PE * (sum(max(64, x) for x in n) if isinstance(n, list) else m * max(64, n))
+        c = PE * (sum(max(least, x) for x in n) if isinstance(n, list) else m * max(least, n))
         add(P, {"P": c}, lambda q, e: [q.matmul(o, l, r, start and i == 0, stop and i == m - 1) for i, (o, l, r) in enumerate(items)], R, Wr, 0, None, start, stop)
 
-    def scan(n, out, a, b, o0, o1, R, Wr):
-        add(P, {"V": plain(n)}, lambda q, e: q.tensor_tensor_scan(out, a, b, 0.0, o0, o1), R, Wr)
+    def scan(n, out, a, b, first, o0, o1, R, Wr):
+        add(P, vec(n), lambda q, e: q.tensor_tensor_scan(out, a, b, first, o0, o1), R, Wr)
 
     def turn(n, out, a, R, Wr):
-        add(P, {"V": plain(n)}, lambda q, e: q.transpose(out, a), R, Wr)
+        add(P, vec(n), lambda q, e: q.transpose(out, a), R, Wr)
 
     def fill(n, ap, c, Wr):
-        add(P, {"V": plain(n)}, lambda q, e: q.memset(ap, c), "", Wr)
+        add(P, vec(n), lambda q, e: q.memset(ap, c), "", Wr)
 
     def iota(n, ap, pat, base, cm, Wr, flt=True):
         if flt:
@@ -317,26 +360,21 @@ def rank_program(g, core, T, topo):
         else:
             add(P, {"G": 160 + 2 * n}, lambda q, e: q.iota(ap, pat, base, cm), "", Wr)
 
+    def put(n, ap, pat, val, base, key):
+        add(P, {"G": 200 + 2 * n}, lambda q, e: q.affine_select(ap, ap, pat, A.not_equal, val, base, -1), key, key)
+
     def remote(items, sem, R, Wr, c=350):
         def fn(q, e):
             send(g, T, topo, core, items, sem)
         add(P, {"G": c}, fn, R, Wr)
         return sum(len(it[1]) for it in items)
 
-    big = []
-
-    def after(lag):
-        k = len(P["ops"]) - 1
-        if len(big) >= lag:
-            P["ops"][k]["dep"].setdefault(big[-lag], False)
-        big.append(k)
-
     C = lambda k: T.col[:, k:k + 1]
-    Z = lambda k, n=16: T.z[:, k, 0:n]
+    Z = lambda k, n: T.z[:, k, 0:n]
     SR = [T.S0, T.S1, T.S2, T.S3]
     SHR, AND = A.logical_shift_right, A.bitwise_and
     span = lambda s, a, b: " ".join("%s%d" % (s, k) for k in range(a, b))
-    each = lambda s, n: " ".join(s % k for k in range(n))
+    part = lambda x, h: x[:, 128 * h:128 * h + 128]
 
     dma("Y", T.W[:, 0:GH], T.x[:, 0:GH], "", "Wa")
     dma("S", T.rq[:], T.req[:], "", "rq")
@@ -348,8 +386,8 @@ def rank_program(g, core, T, topo):
     iota(128, T.rowg[:], [[1, 8], [0, 16]], 0, 0, "rowg")
     iota(2, T.wi[:, 0:2], [[128, 2]], 0, 1, "wi0")
     iota(16, T.wi[:, 16:32], [[16, 16]], 0, 0, "wi1")
-    iota(64, T.tba[:], [[1, 8], [0, 8]], 0, 0, "tba")
-    iota(64, T.tbb[:], [[0, 8], [1, 8]], 8, 0, "tbb")
+    iota(64, T.tba[:, 0:64], [[1, 8], [0, 8]], 0, 0, "tba")
+    iota(64, T.tba[:, 64:128], [[0, 8], [1, 8]], 8, 0, "tbb")
     chip = topo.engines(core, hands[0])
     per = len(chip) // len(hands)
     wd = GH // len(hands)
@@ -359,24 +397,33 @@ def rank_program(g, core, T, topo):
         d = (q - rank) % N
         a = V + (d - 1) * GH
         l0 += remote([(T.cores[q], out_e, "xg%d" % d, T.W[:, 0:GH], T.W[:, a:a + GH])], "l0", "Wa", "out1")
-    iota(16, T.offc[:], [[512, 8], [16, 2]], 0, 0, "offc issued", False)
-    dma("Y", T.W[:, GH:V], T.x[:, GH:V], "issued", "Wb", 1.5)
-    dma("Y", T.pti[:], T.pt[:], "", "pti", 2.2)
+    iota(8, T.offc[:], [[512, 4], [16, 2]], 0, 0, "offc issued", False)
+    dma("Y", T.pti[:], T.pt[:], "issued", "pti", PT0)
+    dma("Y", T.W[:, GH:V], T.x[:, GH:V], "", "Wb", PT0 + 0.3)
     for d in range(1, N):
         q = (rank - d) % N
         nq, fq, hq, _c = ways(T, topo, q)
-        lands("xg%d" % d, len(out_e) if rank in nq else len(hq) * (len(topo.engines(hq[0], core)) // len(fq)), "out0 out1",
-              "W%d0 W%d1" % (d, d), NEAR0 if rank in nq else FAR0)
+        lands("xg%d" % d, len(out_e) if rank in nq else len(hq) * (len(topo.engines(hq[0], core)) // len(fq)), "out0 out1", "W%d" % d, NEAR0 if rank in nq else FAR0)
     lands("l0", l0, "out0 out1", "sent", 1)
     fill(256, T.Rc[:], 0.0, "Rc")
-    add(P, {"G": 1230}, lambda q, e: q.affine_select(T.Rc[:], T.Rc[:], [[16, 8], [1, 8], [0, 8]], A.not_equal, 1.0, 0, -1), "Rc", "Rc")
-    add(P, {"G": 1230}, lambda q, e: q.affine_select(T.Rc[:], T.Rc[:], [[16, 8], [0, 8], [1, 8]], A.not_equal, 1.0, 8, -1), "Rc", "Rc")
-    iota(16, T.bci[:, 0:16], [[1, 16]], 0, 0, "bci0", False)
-    iota(16, T.bci[:, 16:32], [[4, 16]], 3, 0, "bci1", False)
+    put(512, T.Rc[:], [[16, 8], [1, 8], [0, 8]], 1.0, 0, "Rc")
+    put(512, T.Rc[:], [[16, 8], [0, 8], [1, 8]], 1.0, 8, "Rc")
     iota(64, T.mp[:], [[16, 64]], 0, 0, "mp")
     iota(48, T.dc[:], [[1, 3], [0, 16]], 3, 0, "dc")
-    iota(384, T.tcf[:], [[4, 6], [1, 4], [0, 16]], -12, 0, "tcf")
+    iota(128, T.sel[:], [[0, 8], [32, 4], [0, 4]], 0, 0, "sel")
     iota(256, T.taf[:], [[1, 16], [0, 16]], 0, 0, "taf")
+    for k, (pat, base) in enumerate((([[0, 96], [1, 4]], 0), ([[0, 24], [1, 4], [0, 4]], 4), ([[1, 6], [0, 64]], 5), ([[0, 6], [1, 4], [0, 16]], 12))):
+        add(P, {"G": 930}, lambda q, e, k=k, pat=pat, base=base: q.iota(T.tcf[32 * k:32 * k + 32, :], pat, base, 0, allow_small_or_imprecise_dtypes=True),
+            "tcf%d" % (k - 1) if k else "taf", "tcf%d" % k)
+    add(P, {"G": 420}, lambda q, e: q.iota(T.BOK[:], [[0, 128]], 0, 0, allow_small_or_imprecise_dtypes=True), "tcf3", "BOK")
+    fill(64, T.RA[:], 0.0, "RA")
+    fill(128, T.RX[:], 0.0, "RX")
+    low, high, flat = [[16, 8], [0, 4], [1, 4]], [[16, 8], [1, 4], [0, 4]], [[16, 8], [0, 16]]
+    for out, key, val, pat, base in ([(T.BOK[:], "BOK", 4096.0, flat, r) for r in (12, 13, 14)] + [(T.RA[:], "RA", 1.0, low, 0), (T.RA[:], "RA", 1.0, high, 4)] +
+                                     [(T.RX[:, :, f, :], "RX", 32768.0, pat, base) for f in range(2) for pat, base in ((high, 8), (low, 12))] +
+                                     [(T.RX[:, :, 1, :], "RX", 1040.0, flat, 11)]):
+        put(128, out, pat, val, base, key)
+    iota(512, T.tx[:], [[1, 512]], 0, 0, "tx")
     iota(1024, T.AW[:, 64:128, :], [[0, 1024]], 0, 0, "AW1")
     fill(512, T.AW[:, 0:64, :], 0.0, "AW0")
 
@@ -386,13 +433,13 @@ def rank_program(g, core, T, topo):
     cp(4, T.col[:, 0:4], T.coli[:, 0:4], "coli coli1 coli2 coli3", "col")
     ts(128, T.id32[:], T.row[:, 0:128], C(0), None, A.is_equal, None, "row col", "id32")
     ts(128, T.ta[:, 0:128], T.rowj[:], C(1), None, A.is_equal, None, "rowj col", "ta")
-    for nm, sc in (("id12", 2.0 ** -12), ("idb", 1.0), ("id4", 4.0), ("idB", 32768.0), ("idm", -255.0), ("idF", BIG)):
+    for nm, sc in (("id12", 2.0 ** -12), ("idb", 1.0), ("id4", 4.0), ("idB", 32768.0), ("idm", -255.0), ("idF", BIG), ("idw", 1.75 ** -128)):
         lin(both(128), T[nm][:], T.id32[:], sc, 0.0, "id32", nm)
     for w in (128, 256, 512):
         cp(both(w, 0.5), T.ta[:, w:2 * w], T.ta[:, 0:w], "ta", "ta")
     for k, a, sc, off in ((4, 3, -1.0, 1.0), (5, 0, 1.0, 16.0), (6, 0, 1.0, -16.0), (7, 2, 16.0, 15.0), (8, 1, 16.0, 0.0), (9, 1, 32.0, 0.0), (15, 1, 1.0, -1024.0)):
         lin(both(1), C(k), C(a), sc, off, "col", "col%d" % k)
-    ts(1, C(16), C(1), 15.0, None, A.is_equal, None, "col", "col16")
+    ts(1, C(16), C(1), 11.0, None, A.is_equal, None, "col", "col16")
     lin(both(128), T.BOc[:], T.rowj[:], -1.0 / 16, 15.0 / 16 + 1536.0 / 65536, "rowj", "BOc")
     ts(16, T.wi[:, 16:32], T.wi[:, 16:32], C(1), -LNB, A.add, A.mult, "wi1 col", "wi1")
     ts(2, T.wi[:, 0:2], T.wi[:, 0:2], -LNB, LN0, A.mult, A.add, "wi0", "wi0")
@@ -402,318 +449,303 @@ def rank_program(g, core, T, topo):
     act(1600, T.wcol[:], T.wi[:, 0:2], F.Exp, "wi0", "wcol")
     act(100, T.thr[:], T.wi[:, 16:32], F.Exp, "wi1 wcol", "thr")
     lin(both(512, 0.5), T.SWs[:], T.SWb[:], 2.0 ** -16, 0.0, "SW0 SW1 SW2 SW3", "SWs")
-    fill(256, T.rmin[:], 0.0, "rmin")
-    fill(16, T.rmin[:, 0:256:16], 1024.0, "rmin")
+    for x, c in (("rmin", 1024.0), ("rmax", -1024.0)):
+        fill(128, T[x][:], 0.0, x)
+        fill(8, T[x][:, 0:128:16], c, x)
     fill(16, T.ta[:, V:V + 16], 0.0, "taz")
     fill(1, T.ta[:, V:V + 1], 1.0, "taz")
     ts(128, T.BO[:], T.rowg[:], C(2), None, A.is_equal, None, "rowg col", "BO")
-    lin(both(256), T.rmax[:], T.rmin[:], -1.0, 0.0, "rmin", "rmax")
     tt(256, T.BOc[:], T.BOc[:], T.BO[:], A.mult, "BOc BO", "BOc")
-    lin(both(128, 0.5, S16), T.Cm1[:], T.BO[:], C(15), 0.0, "BO col15", "Cm1")
+    lin(both(128, 0.5), T.Cm1[:], T.BO[:], C(15), 0.0, "BO col15", "Cm1")
     lin(both(128, 0.5), T.Cm0[:], T.BO[:], C(8), 0.0, "BO col8", "Cm0")
-    cp(both(128, 0.5), T.RX[:, :, 0, :], T.idB[:], "idB", "RX0")
-    ts(64, T.RX[:, :, 1, :], T.BO[:], C(16), 1040.0, A.mult, A.mult, "BO col16", "RX1")
-    tt(256, T.RX[:, :, 1, :], T.RX[:, :, 1, :], T.idB[:], A.max, "RX1 idB", "RX1")
-    lin(both(128, 0.5), T.nBO[:], T.BO[:], -1.0, 0.0, "BO", "nBO")
-    lin(both(128, 0.5), T.BOK[:], T.BO[:], 4096.0, 0.0, "BO", "BOK")
-    lin(both(256, 0.5), T.THD[:], T.ta[:, 0:256], 816.0, -1024.0, "ta", "THD")
+    lin(both(128, 0.5), T.nBO[:], T.BO[:], -1.0 / 16, 0.0, "BO", "nBO")
+    fill(32, T.zer[:, 512:576], 255.0, "c255")
+    fill(8, T.zer[:, 576:592], 0.0, "c255")
     ts(128, T.tri[:], T.rowj[:], C(1), -1.0, A.is_le, A.mult, "rowj col", "tri")
     ts(144, T.EE[:], T.row[:], C(7), None, A.is_equal, None, "row col7", "EE")
     tt(256, T.tri[:], T.tri[:], T.BO[:], A.mult, "tri BO", "tri")
     tt(256, T.tri[:], T.tri[:], T.idm[:], A.add, "tri idm", "tri")
-    fill(24, T.L0[:], 0, "L0")
+    fill(25, T.L0[:], 0, "L0")
     fill(1, T.L0[:, 23:24], 96, "L0")
     fill(8, T.L0[:, 32:48], V + 8, "L0")
-    fill(16, T.nbi[:, V:V + 16], 0, "pad0")
-    fill(16, T.pli[:, V:V + 16], 0, "pad1")
-    fill(16, T.cst[:, V:V + 16], 0.0, "pad2")
-    ts(16, T.offc[:], T.offc[:], C(9), None, A.add, None, "offc col9", "offc")
+    for k, x in enumerate((T.nbi, T.pli, T.cst)):
+        fill(16, x[:, V:V + 16], 0, "pad%d" % k)
+    ts(8, T.offc[:], T.offc[:], C(9), None, A.add, None, "offc col9", "offc")
     fill(32, T.FZ[:], 0.0, "FZ")
     fill(96, T.Ms[:], BIG, "Ms")
     fill(96, T.tb[:], 0.0, "tb")
     fill(64, T.BAN[:, 0:96], 0.0, span("BAN_", 0, 6))
-    fill(256, T.zer[:], 0.0, "zer")
-    fill(128, T.on12[:], 2.0 ** -12, "on12")
+    fill(256, T.zer[:, 0:512], 0.0, "zer")
+    fill(64, T.on12[:], 2.0 ** -12, "on12")
     fill(24, T.rrk[:], 1.0, "rrk")
     fill(3, T.rrk[:, 0:48:16], 0.0, "rrk")
     fill(64, T.r4[:], -4096.0, "r4")
-    fill(16, T.r4[:, 0:64:4], -207.0, "r4")
+    fill(16, T.r4[:, 0:64:4], 48.0, "r4")
     fill(32, T.dI[:], 0, "dI0 dI1")
-    fill(32, T.gs[:], 0.0, "gs0 gs1")
-    fill(32, T.gd[:], 0.0, "gd")
+    fill(32, T.gs[:], 0.0, "gs0 gs1 got0 got1")
+    for k, sc in enumerate((576.0, 640.0, 704.0, 192.0, 256.0, 320.0, 255.0)):
+        lin(both(128), T.idk[:, k, :], T.id32[:], sc, 0.0, "id32", "idk%d" % k)
     ts(28, T.rqb[:], T.rq[:], 1.0 / 16, 32 - 15.0 / 32, A.mult, A.add, "rq", "rqb")
     cp(1, C(10), T.thi[:, 0:1], "thi", "col10")
 
     def requests(t):
-        cp(7, T.L0[:, 0:7], T.rq[:, 7 * t:7 * t + 7], "rq L0", "Ls0")
-        cp(7, T.L0[:, 16:23], T.rqb[:, 7 * t:7 * t + 7], "rqb L0", "Lb0")
+        cp(both(7), T.L0[:, 0:7], T.rq[:, 7 * t:7 * t + 7], "rq L0", "Ls0")
+        cp(both(7), T.L0[:, 16:23], T.rqb[:, 7 * t:7 * t + 7], "rqb L0", "Lb0")
     requests(0)
     ts(1, C(13), C(10), 2048.0, 2.0 ** -17, A.is_ge, A.mult, "col10", "col13")
     lin(both(1), C(14), C(1), 2.0 ** -16, C(13), "col col13", "col14")
     lin(both(1), C(11), C(10), 2.0 ** -12, C(14), "col10 col14", "col11")
     lin(both(1), C(12), C(10), -1.0, 2048.0, "col10", "col12")
-    lin(both(128, 1.0, S16), T.thM[:], T.id32[:], C(12), -16.0, "id32 col12", "thM")
-    ts(64, T.tba[:], T.tba[:], C(1), None, A.is_equal, None, "tba col", "tba")
-    ts(64, T.tbb[:], T.tbb[:], C(1), None, A.is_equal, None, "tbb col", "tbb")
-    tt(128, T.tb[:, 32:96], T.tba[:], T.tbb[:], A.add, "tba tbb tb", "tb")
+    lin(both(128), T.thM[:], T.id32[:], C(12), -16.0, "id32 col12", "thM")
+    ts(128, T.tba[:], T.tba[:], C(1), None, A.is_equal, None, "tba tbb col", "tba")
+    tt(128, T.tb[:, 32:96], T.tba[:, 0:64], T.tba[:, 64:128], A.add, "tba tb", "tb")
     for u in range(2):
         a, b = u * GH, u * GH + GH
-        ts(GH, T.cst[:, a:b], T.pti[:, a:b], 1.5 * 2.0 ** 34, 1.5 * 2.0 ** 34, A.add, A.subtract, "pti", "cst%d" % u)
+        lin(both(GH), T.cst[:, a:b], T.pti[:, a:b], 2.0 ** -11, -0.25, "pti", "cst%d" % u)
         ts(GH, T.pli[:, a:b], T.pti[:, a:b], 2047, None, AND, None, "pti", "pli%d" % u)
-    cp(512, T.AF[:, 0:64, :], T.AW[:, 64:128, :], "AW1", "AF0")
-    cp(32, T.bc[:], T.bci[:], "bci0 bci1", "bc")
     lin(both(64), T.mp[:], T.mp[:], 1.0, C(1), "mp col", "mp")
-    ts(4, T.rep[:], T.rowg[:, 0:4], C(1), None, A.add, None, "rowg col", "rep")
-    ts(384, T.tc[:, 0:384], T.tcf[:], C(1), None, A.is_equal, None, "tcf col", "tc")
+    lin(both(4), T.bc[:, 16:20], T.rowg[:, 0:4], 1.0, C(1), "rowg col", "rep")
+    ts(64, T.sel[:], T.sel[:], C(0), None, A.is_equal, None, "sel col", "selb")
+    mm(384, [(T.pY[:, 0:384], T.sel[:], T.tcf[:])], "selb tcf0 tcf1 tcf2 tcf3", "pY.a")
+    ts(384, T.tc[:, 0:384], T.pY[:, 0:384], C(1), None, A.is_equal, None, "pY.a col", "tc")
     ts(192, T.tc[:, 384:768], T.tc[:, 0:384], C(16), None, A.max, None, "tc col16", "tc1")
     ts(256, T.ta[:, V + 16:V + 272], T.taf[:], C(1), None, A.is_equal, None, "taf col", "tao")
+    WALL = "Wa Wb W1 W2 W3"
+
     def keep(d):
         if d == 0:
-            dma("Y", T.S0[:, 0:V], T.W[:, 0:V], "Wa Wb W10 W20 W30", "Sx0")
+            dma("Y", T.S0[:, 0:V], T.W[:, 0:V], WALL, "Sx0")
         else:
-            dma("Y", SR[d][:, 0:GH], T.W[:, V + (d - 1) * GH:V + d * GH], "W%d0 W%d1" % (d, d), "Sx%d" % d)
+            dma("Y", SR[d][:, 0:GH], T.W[:, V + (d - 1) * GH:V + d * GH], "W%d" % d, "Sx%d" % d)
+    for u in range(2):
+        cp(both(512, 0.5), T.AF[:, 32 * u:32 * u + 32, :], T.zer[:, 0:512], "zer", "AF0")
+    for u in range(1, 4):
+        dma("Y", T.AF[:, 64 * u:64 * u + 64, :], T.AF[:, 0:64, :], "AF0", "AF%d" % u, 1.5)
     for d in (1, 2, 3, 0):
         keep(d)
-    for d in range(1, N):
-        fill(256, SR[d][:, GH:V], 0.0, "Sz%d" % d)
-    for u in range(1, 4):
-        dma("Y", T.AF[:, 64 * u:64 * u + 64, :], T.AF[:, 0:64, :], "AF0", "AF%d" % u)
     for d in range(N):
         dma("Y", SR[d][:, V:2 * V], T.plans[:], "", "Sp%d" % d, 2 + 0.5 * d)
+    for d in range(1, N):
+        dma("Y", SR[d][:, GH:V], T.S0[:, V:V + GH], "Sp0", "Sz%d" % d, 3.5)
 
-    WALL = "Wa Wb W10 W11 W20 W21 W30 W31"
     TA = "ta taz "
     ta = T.ta[:, 0:V + 16]
+    rep = T.bc[:, 16:19]
 
-    def to_list(out, bank, src, L, key):
-        mm(16, [(out, T.EE[:, 15 - j:143 - j], src[:, j:L:16]) for j in range(16)], "EE " + key, bank)
-
-    def marks_1(t, NH, sl, bl, b0, sk, bk):
-        AR = T["AR%d" % t]
-        cp(gath(128 * NH), T.FB[:, 0:128 * NH], T.tb[:].indirect(bl[:, b0:b0 + 8 * NH]), "tb " + bk, "FB")
-        cp(gath(128 * NH), AR[:, 0:128 * NH], ta.indirect(sl[:, 0:8 * NH]), TA + sk, each("AR%d%%d" % t, NH))
+    def marks(t, NH, sl, bl, b0, sk, bk):
+        L, n, AR, B = 128 * NH, 8 * NH, T["AR%d" % t], T["B%d" % t]
+        a = 6 if t == 0 and NH == 2 else 0
+        if a:
+            cp(gath(16 * a), T.FB[:, 0:16 * a], T.tb[:].indirect(bl[:, b0:b0 + a]), "tb L0 Lb0", "FBa")
+            cp(gath(16 * a), AR[:, 0:16 * a], ta.indirect(sl[:, 0:a]), TA + "L0 Ls0", "AR00")
+        cp(gath(L - 16 * a), T.FB[:, 16 * a:L], T.tb[:].indirect(bl[:, b0 + a:b0 + n]), "tb " + bk, "FB" if a else "FB FBa")
+        cp(gath(L - 16 * a), AR[:, 16 * a:L], ta.indirect(sl[:, a:n]), TA + sk, span("AR%d" % t, 0, NH))
         for h in range(NH):
-            a, b = 128 * h, 128 * h + 128
-            mm(512, [(T["pB%d" % h][:], T.FB[:, a:b], T.Rc[:])], "FB Rc", "pB%d.a pB%d.b" % (h, h))
-            mm(128, [(T.pA[:, a:b], AR[:, a:b], T.idb[:])], "idb AR%d%d" % (t, h), "pA.a%d" % h)
-            relu(both(512), T["B%d" % t][:, 512 * h:512 * h + 512], T["pB%d" % h][:], -1.0, "pB%d.a pB%d.b" % (h, h), "B%d%d" % (t, h))
-            lin(both(128), T.AW[:, 64 * h:64 * h + 64:8, :], T.pA[:, a:b], T.wcol[:, h:h + 1], 0.0, "pA.a%d wcol" % h, "AW%d" % h)
-
-    def marks_2(t, NH, bl, bk):
-        L, n = 128 * NH, 8 * NH
-        B = T["B%d" % t]
+            mm(512, [(T["pB%d" % h][:], part(T.FB, h), T.Rc[:])], "FB FBa Rc", "pB%d.a" % h)
+            mm(128, [(part(T.pA, h), part(AR, h), (T.idb, T.idw)[h][:])], "idb idw AR%d%d" % (t, h), "pA.a%d" % h)
+            relu(both(512), B[:, 512 * h:512 * h + 512], T["pB%d" % h][:], -1.0, "pB%d.a" % h, "B%d%d" % (t, h))
+        lin(both(L), T.AW[:, 0:64 * NH:8, :], T.pA[:, 0:L], T.wcol[:, 0:1], 0.0, span("pA.a", 0, NH) + " wcol", span("AW", 0, NH))
         mm(64, [(T.pM[:, 0:64], T.idF[:], (T.FZ if t == 0 else T.MK)[:])], "idF " + ("FZ" if t == 0 else "MK"), "pM.w", True, False)
         for h in range(NH):
             mm(64, [(T.pM[:, 0:64], T.AW[:, 64 * h + 7 * k:64 * h + 7 * k + 8, :], B[:, 512 * h + 64 * k:512 * h + 64 * k + 64]) for k in range(8)],
                "AW%d B%d%d" % (h, t, h), "pM.w", False, h == NH - 1)
         cp(both(64), T.Ms[:, 32:96], T.pM[:, 0:64], "pM.w", "Ms")
-        tt(gath(L, "V"), T.LK[:, 0:L], T.Ms[:].indirect(bl), T["AR%d" % t][:, 0:L], A.mult, "Ms " + each("AR%d%%d" % t, NH) + " " + bk, "LK")
+        tt(gath(L, "V"), T.LK[:, 0:L], T.Ms[:].indirect(bl[:, b0:b0 + n]), AR[:, 0:L], A.mult, "Ms " + span("AR%d" % t, 0, NH) + " " + bk, "LK")
         if t == 0:
-            ts(32, T.MK[:], T.Ms[:, 32:96], 0.0, None, A.is_gt, None, "Ms", "MK")
-        to_list(T.pS[:, 0, 0, 0:n], "pS.a", T.LK, L, "LK")
-        tt(16, Z(1 + t, n), T.pS[:, 0, 0, 0:n], T.thr[:, 0:n], A.is_lt, "pS.a thr", "got%d" % t)
+            add(P, both(64, 0.5), lambda q, e: q.tensor_scalar(T.MK[:], T.Ms[:, 32:96], 0.0, None, A.is_gt) if e == "V" else q.activation(T.MK[:], T.Ms[:, 32:96], F.Sign), "Ms", "MK")
+        mm(16, [(T.pS[:, 0, 0, 0:n], T.EE[:, 15 - j:143 - j], T.LK[:, j:L:16]) for j in range(16)], "EE LK", "pS.a")
+        tt(16, T.gs[:, 2 + t, 0:n], T.pS[:, 0, 0, 0:n], T.thr[:, 0:n], A.is_lt, "pS.a thr", "got%d" % t)
 
-    def front(S, sk, cut, a, b):
+    def front(S, sk, cut, a, b, o=0):
         for c0, nb in cut:
             for v in range(2):
                 c = c0 + nb * v
                 lo, hi = max(a, c), min(b, c + nb)
                 if lo < hi:
                     at = slice(16 * c0 + v + 32 * (lo - c), 16 * c0 + 32 * (hi - c), 2)
-                    cp(gath(16 * (hi - lo), S16), T.Q[:, at], T.nbi[:].indirect(S[:, lo:hi]), "nbi pad0 " + sk, span("Q", lo, hi))
-                    lin(gath(16 * (hi - lo)), T.CK[:, at], T.cst[:].indirect(S[:, lo:hi]), 2.0 ** -23, C(11), "cst0 cst1 pad2 col11 " + sk, span("CK", lo, hi))
+                    cp(gath(16 * (hi - lo)), T.Q[:, at], T.nbi[:].indirect(S[:, o + lo:o + hi]), "nbi pad0 " + sk, span("Q", lo, hi))
+                    lin(gath(16 * (hi - lo)), T.CK[:, at], T.cst[:].indirect(S[:, o + lo:o + hi]), 2.0 ** -12, C(11), "cst0 cst1 pad2 col11 " + sk, span("CK", lo, hi))
 
-    def chunk(t, h, c0, nb, on, ban):
+    def chunk(t, h, c0, nb, ban):
         n, m, L = 2 * nb, 16 * nb, 32 * nb
         a, k0 = 16 * c0, c0 // 2
-        pC = T["pC%d" % (h % 2)]
+        pC = T["pC%d" % h]
         pX, kq = pC[:, 0:nb, :, :], pC[:, 8:8 + nb, :, :]
         half = lambda v: pC[:, 0:nb, :, v:16:2]
         K = lambda s: span(s, c0, c0 + n)
-        Kv = lambda s, v: span(s, c0 + nb * v, c0 + nb * v + nb)
-        X, KQ = "pC%d.x" % (h % 2), "pC%d.q" % (h % 2)
-        lin(both(L, 0.5, S16), T.Qf[:, a:a + L], T.Q[:, a:a + L], 1.0, -1024.0, K("Q"), K("Qf"))
+        X, KQ = "pC%d.x" % h, "pC%d.q" % h
+        lin(both(L, 0.5), T.Qf[:, a:a + L], T.Q[:, a:a + L], 1.0, -1024.0, K("Q"), K("Qf"))
         mm(L, [(pX, T.thM[:], T.on12[:, 0:L])], "thM on12", X, True, False)
         for b in range(nb):
             k = k0 + b
-            cp(gath(512, on[k].replace("-", "VS")), T.G[:, 512 * k:512 * k + 512], T.W[:].indirect(T.Q[:, 32 * k:32 * k + 32]),
-               WALL + " Q%d Q%d" % (c0 + b, c0 + nb + b), "G%d" % k)
-            after(LAG)
+            w = WIDE.get(P["at"], (1, 1, 1, 1))[b]
+            if w:
+                cp(gath(512 * w), T.G[:, 512 * k:512 * (k + w)], T.W[:].indirect(T.Q[:, 32 * k:32 * (k + w)]),
+                   WALL + " " + span("Q", c0 + b, c0 + b + w) + " " + span("Q", c0 + nb + b, c0 + nb + b + w), span("G", k, k + w))
+                big.append(len(P["ops"]) - 1)
+                if len(big) > 2:
+                    P["ops"][-1]["dep"].setdefault(big[-3], False)
             if b == nb - 1:
                 mm(4 * L, [(pX, T.id32[:], T.CK[:, a:a + L])], "id32 " + K("CK"), X, False, False)
                 if ban is not None:
                     mm(m, [(half(v), T.id4[:], T[ban][:, a + m * v:a + m * v + m]) for v in range(2)], "id4 " + K(ban + "_"), X, False, False)
             if b % 2 == 1:
                 mm(64, [(pC[:, b - 1:b + 1, :, :], T.id12[:], T.G[:, 512 * (k - 1) + i:512 * (k + 1):16]) for i in range(16)], "id12 G%d G%d" % (k - 1, k), X, False, b == nb - 1)
-            if b % CUTS == CUTS - 1:
-                r, w = 512 * (k + 1 - CUTS), 512 * CUTS
-                turn(w / 2, T.GT[:, r:r + w], T.G[:, r:r + w], span("G", k + 1 - CUTS, k + 1), span("GT", k + 1 - CUTS, k + 1))
+            w = TURN.get(P["at"], (1, 1, 1, 1))[b]
+            if w:
+                turn(256 * w, T.GT[:, 512 * (k + 1 - w):512 * (k + 1)], T.G[:, 512 * (k + 1 - w):512 * (k + 1)], span("G", k + 1 - w, k + 1), span("GT", k + 1 - w, k + 1))
         tt(L, T.ov[:, a:a + L], pX, T.CK[:, a:a + L], A.is_gt, X + " " + K("CK"), K("ov"))
         for v in range(2):
             tt(m, T.kR[:, k0:k0 + nb, v, :], half(v), T.ov[:, a + v:a + L:2], A.add, X + " " + K("ov"), span("kR%d_" % v, k0, k0 + nb))
         mm([L, m, m, m, m], [(kq, T.BOc[:], T.ta[:, 0:L])] + [(pC[:, 8:8 + nb, e, :], T.SWs[:, 2 * e + v, :], T.Qf[:, a + v:a + L:2]) for e in range(2) for v in range(2)],
-           "BOc ta SWs " + K("Qf"), KQ, True, False)
+           "BOc ta SWs " + K("Qf"), KQ)
+        cp(both(L), T.kq[:, a:a + L], kq, KQ, K("kq"))
         turn(L, T.kT[:, a:a + L], T.kR[:, k0:k0 + nb, :, :], span("kR0_", k0, k0 + nb) + " " + span("kR1_", k0, k0 + nb), K("kT"))
-        scan(L, T.km[:, a:a + L], T.rmin[:, 0:L], T.kT[:, a:a + L], A.add, A.min, "rmin " + K("kT"), K("km"))
+        scan(L, T.km[:, a:a + L], T.rmin[:, 0:L], T.kT[:, a:a + L], 0.0, A.add, A.min, "rmin " + K("kT"), K("km"))
         cs = slice(c0, c0 + n)
-        lin(both(n, 1.0, S16), T.ki[:, cs], T.km[:, a + 15:a + L:16], 2.0 ** 17, 0.0, K("km"), K("ki"))
-        ts(n, T.ci[:, cs], T.ki[:, cs], 1, 15, SHR, AND, K("ki"), K("ci"))
-        tt(n, T.off[:, cs], T.ci[:, cs], T.offc[:, 0:n], A.add, "offc " + K("ci"), K("off"))
-        cp(gath(L), T.K1[:, a:a + L], T.GT[:, 16 * a:16 * (a + L)].indirect(T.off[:, cs]), span("GT", k0, k0 + nb) + " " + K("off"), K("K1_"))
-        mm(L, [(kq, T.idb[:], T.K1[:, a:a + L])], "idb " + K("K1_"), KQ, False, True)
-        turn(L, T.K1T[:, a:a + L], kq, KQ, K("K1T"))
-        scan(L, T.bm[:, a:a + L], T.rmax[:, 0:L], T.K1T[:, a:a + L], A.add, A.max, "rmax " + K("K1T"), K("bm"))
-        bi = T["bi%d" % t]
-        for v in range(2):
-            lin(both(nb, 1.0, S16), bi[:, c0 + nb * v:c0 + nb * v + nb], T.bm[:, a + 16 * v + 15:a + L:32], 65536.0, 0.0, K("bm"), Kv("bi%d_" % t, v))
+        lin(both(n), T.ki[:, 0, cs], T.km[:, a + 15:a + L:16], 2.0 ** 17, 0.0, K("km"), K("ki"))
+        ts(n, T.ki[:, 1, cs], T.ki[:, 0, cs], 1, 15, SHR, AND, K("ki"), K("ci"))
+        tt(n, T.off[:, cs], T.ki[:, 1, cs], T.offc[:, 0:n], A.add, "offc " + K("ci"), K("off"))
+        tt(gath(L, "V"), T.K1[:, a:a + L], T.GT[:, 16 * a:16 * (a + L)].indirect(T.off[:, cs]), T.kq[:, a:a + L], A.add, span("GT", k0, k0 + nb) + " " + K("off") + " " + K("kq"), K("K1_"))
+        turn(L, T.K1T[:, a:a + L], T.K1[:, a:a + L], K("K1_"), K("K1T"))
+        scan(L, T.bm[:, a:a + L], T.rmax[:, 0:L], T.K1T[:, a:a + L], 0.0, A.add, A.max, "rmax " + K("K1T"), K("bm"))
         if t == 0:
-            ts(n, T.zi[:, 0, cs], bi[:, cs], 4095, None, AND, None, K("bi0_"), K("b0_"))
+            for v in range(2):
+                lin(both(nb), T.bi[:, c0 + nb * v:c0 + nb * v + nb], T.bm[:, a + 16 * v + 15:a + L:32], 65536.0, 0.0, K("bm"), span("bi", c0 + nb * v, c0 + nb * v + nb))
+            ts(n, T.zi[:, 0, cs], T.bi[:, cs], 4095, None, AND, None, K("bi"), K("b0_"))
             ts(n, T.s1[:, cs], T.zi[:, 0, cs], -512.0, 1024.0, A.add, A.min, K("b0_"), K("s1_"))
 
-    def stuck(t, n, cut):
-        cp(both(n, 1.0, S16), T.CS[:, 0, 0:n], T.ci[:, 0:n], span("ci", 0, n), "CS")
-        ts(n, T.zi[:, 4, 0:n], T.ki[:, 0:n], 1, None, AND, None, span("ki", 0, n), "hh")
-        lin(both(n, 1.0, S16), Z(20, n), T.zi[:, 4, 0:n], 65536.0, 131071.0, "hh", "ht")
-        tt(n, T.CS[:, 1, 0:n], T.ki[:, 0:n], Z(20, n), A.is_gt, span("ki", 0, n) + " ht", "CSs")
-        for c0, nb in cut:
+    def chosen(t, n, S, sk):
+        L, OH = 16 * n, T["OH%d" % t]
+        cp(both(n), T.CS[:, 0, 0:n], T.ki[:, 1, 0:n], span("ci", 0, n), "CS")
+        ts(n, T.zi[:, 4, 0:n], T.ki[:, 0, 0:n], 1, None, AND, None, span("ki", 0, n), "hh")
+        lin(both(n), Z(2, n), T.zi[:, 4, 0:n], 65536.0, 131071.0, "hh", "ht")
+        tt(n, T.CS[:, 1, 0:n], T.ki[:, 0, 0:n], Z(2, n), A.is_gt, span("ki", 0, n) + " ht", "CSs")
+        for c0, nb in CUT[n]:
             for v in range(2):
                 mm(n, [(T.pS[:, 12:14, 0, c0 + nb * v:c0 + nb * v + nb], T.SWb[:, 2 * v + e, :], T.CS[:, :, c0 + e:c0 + 2 * nb:2]) for e in range(2)], "SWs CS CSs", "pS.b")
-        cl = T["c%d" % t]
-        cp(both(n, 1.0, S16), cl[:, 0:n], T.pS[:, 12, 0, 0:n], "pS.b", "cl%d" % t)
-        cp(gath(16 * n), T["OH%d" % t][:, 0:16 * n], ta.indirect(cl[:, 0:n]), TA + "cl%d" % t, span("OH%d_" % t, 0, n))
-        tt(n, T.gs[:, t, 0:n], T.pS[:, 13, 0, 0:n], Z(1 + t, n), A.mult, "pS.b got%d" % t, "gs%d" % t)
+        cp(both(n), T.cl[:, t, 0:n], T.pS[:, 12, 0, 0:n], "pS.b", "cl%d" % t)
+        cp(gath(L), OH[:, 0:L], ta.indirect(T.cl[:, t, 0:n]), TA + "cl%d" % t, span("OH%d_" % t, 0, n))
+        tt(n, T.gs[:, t, 0:n], T.pS[:, 13, 0, 0:n], T.gs[:, 2 + t, 0:n], A.mult, "pS.b got%d" % t, "gs%d" % t)
+        tt(gath(L, "V"), T["PL%d" % t][:, 0:L], T.pli[:].indirect(S[:, 0:n]), OH[:, 0:L], A.mult, "pli0 pli1 pad1 " + span("OH%d_" % t, 0, n) + " " + sk, "PL%d" % t)
 
-    def plan(t, L, S, sk):
-        tt(gath(L, "V"), T["PL%d" % t][:, 0:L], T.pli[:].indirect(S[:, 0:L // 16]), T["OH%d" % t][:, 0:L], A.mult, "pli0 pli1 pad1 " + span("OH%d_" % t, 0, L // 16) + " " + sk, "PL%d" % t)
-
-    def refresh(d, j, a, b):
-        at, m = V + (d - 1) * GH, 12 - 4 * (N - d)
-        cp(gath(256 * (b - a)), T.W[:, at + 256 * a:at + 256 * b], SR[d][:].indirect(T.IN[:, j, m + 16 * a:m + 16 * b]), "Sz%d Sp%d Sx%d IM%d" % (d, d, d, j), span("W%d" % d, a, b))
-
-    front(T.L0, "L0 Ls0", CUT[(8, 0)], 0, 8)
+    front(T.L0, "L0 Ls0", CUT[8], 0, 8)
     for rnd in range(RO):
         n = 8 if rnd == 0 else 16
         L, NH = 16 * n, n // 8
         last = rnd == RO - 1
-        LS, LB = "L0 Ls0 Ls1", "L0 Lb0 Lb1"
+        LS, LB, S1 = "L0 Ls0 Ls1", "L0 Lb0 Lb1", span("s1_", 0, n)
         P["at"], P["sites"] = "r%d m0" % NH, {}
-        marks_1(0, NH, T.L0, T.L0, 16, LS, LB)
-        marks_2(0, NH, T.L0[:, 16:16 + n], LB)
-        for h, (c0, nb) in enumerate(CUT[(n, 0)]):
+        marks(0, NH, T.L0, T.L0, 16, LS, LB)
+        for h, (c0, nb) in enumerate(CUT[n]):
             P["at"] = "r%d s0%d" % (NH, h)
-            chunk(0, h, c0, nb, ON[(n, 0)], "BAN" if rnd > 0 else None)
-            front(T.s1, span("s1_", c0, c0 + 2 * nb), CUT[(n, 1)], c0, c0 + 2 * nb)
-        BI0, BI1, S1 = span("bi0_", 0, n), span("bi1_", 0, n), span("s1_", 0, n)
+            chunk(0, h, c0, nb, "BAN" if rnd > 0 else None)
+            front(T.s1, span("s1_", c0, c0 + 2 * nb), CUT[n], c0, c0 + 2 * nb)
         P["at"] = "r%d m1" % NH
-        stuck(0, n, CUT[(n, 0)])
-        plan(0, L, T.L0, LS)
+        chosen(0, n, T.L0, LS)
         tt(n, T.zi[:, 2, 0:n], T.gs[:, 0, 0:n], T.zi[:, 0, 0:n], A.mult, "gs0 " + span("b0_", 0, n), "bg0")
         lin(both(n), T.b1[:, 0:n], T.zi[:, 2, 0:n], 1.0 / 16, -15.0 / 32, "bg0", "bl1")
-        tt(n, Z(11, n), Z(1, n), T.gs[:, 0, 0:n], A.subtract, "got0 gs0", "gd0")
-        ts(n, T.dI[:, 0, 0:n], T.zi[:, 2, 0:n], 9, None, SHR, None, "bg0", "dI0")
-        tt(gath(48, "V"), T.ff[:, 0, :], T.dI[:, 0, :].indirect(T.rep[:, 0:3]), T.dc[:], A.is_equal, "dI0 rep dc", "ff0")
-        scan(24, T.inc[:, 0, :], T.rrk[:], T.ff[:, 0, :], A.mult, A.add, "rrk ff0", "inc0")
-        if not last:
-            ts(n, Z(15, n), T.zi[:, 2, 0:n], 1536.0, 384.0, A.is_ge, A.mult, "bg0", "ask0")
-        marks_1(1, NH, T.s1, T.b1, 0, S1, "bl1")
-        marks_2(1, NH, T.b1[:, 0:n], "bl1")
-        for h, (c0, nb) in enumerate(CUT[(n, 1)]):
+        lin(both(n), T.dI[:, 0, 0:n], T.zi[:, 2, 0:n], 1.0 / 512, -511.0 / 1024, "bg0", "dI0")
+        tt(gath(48, "V"), T.ff[:, 0, :], T.dI[:, 0, :].indirect(rep), T.dc[:], A.is_equal, "dI0 rep dc", "ff0")
+        scan(24, T.inc[:, 0, :], T.rrk[:], T.ff[:, 0, :], 0.0, A.mult, A.add, "rrk ff0", "inc0")
+        marks(1, NH, T.s1, T.b1, 0, S1, "bl1")
+        for h, (c0, nb) in enumerate(CUT[n]):
             P["at"] = "r%d s1%d" % (NH, h)
-            chunk(1, h, c0, nb, ON[(n, 1)], "OH0")
+            chunk(1, h, c0, nb, "OH0")
         P["at"] = "r%d end" % NH
-        stuck(1, n, CUT[(n, 1)])
-        plan(1, L, T.s1, S1)
-        YB = [T.pY, T.pB0]
-        YK = ("pY.a", "pB0.a")
+        bj = T.bj[:, 0:NH, :, :]
+        for v in range(2):
+            lin(both(n // 2), T.bj[:, 0:NH, v, :], T.bm[:, 16 * v + 15:L:32], 65536.0, 0.0, span("bm", 0, n), "bj%d" % v)
+        chosen(1, n, T.s1, S1)
+        YB, YK = (T.pY, T.pB0), ("pY.a", "pB0.a")
+        for h in range(NH):
+            mm([256, 128, 128], [(YB[h][:, 0:256], T.idb[:], T.zer[:, 0:256])] + [(part(YB[h], t), part(T["AR%d" % t], h), T.idB[:]) for t in range(2)],
+               "idb zer idB AR0%d AR1%d" % (h, h), YK[h], True, False)
+            for t in range(2):
+                mm(128, [(part(YB[h], t), part(T["PL%d" % t], h), T.BO[:])], "BO PL%d" % t, YK[h], False, False)
+        tt(gath(48, "V"), T.DC[:], T.gs[:, 1, :].indirect(rep), T.dc[:], A.mult, "gs1 rep dc", "DC")
+        ts(n, T.dI[:, 1, 0:n], bj, 9, 7, SHR, AND, "bj0 bj1", "dI1")
+        tt(gath(48, "V"), T.ff[:, 1, :], T.dI[:, 1, :].indirect(rep), T.DC[:], A.is_equal, "dI1 rep DC", "ff1")
+        scan(24, T.inc[:, 1, :], T.rrk[:], T.ff[:, 1, :], 0.0, A.mult, A.add, "rrk ff1", "inc1")
+        mm(80, [(T.pM[:, 64:144], T.idb[:], T.zer[:, 512:592])], "idb c255", "pM.r", True, False)
         for t in range(2):
-            mm([L] + [128] * (2 * NH), [(YB[t][:, 0:L], T.idb[:], T.zer[:, 0:L])] +
-               [(YB[t][:, 128 * h:128 * h + 128], x[:, 128 * h:128 * h + 128], y[:]) for h in range(NH) for x, y in ((T["AR%d" % t], T.idB), (T["PL%d" % t], T.BO))],
-               "idb zer idB BO PL%d " % t + each("AR%d%%d" % t, NH), YK[t], True, False)
-        bI, dI = T.zi[:, 3, 0:n], T.zi[:, 5, 0:n]
-        tt(gath(48, "V"), T.DC[:], T.gs[:, 1, :].indirect(T.rep[:, 0:3]), T.dc[:], A.mult, "gs1 rep dc", "DC")
-        ts(n, T.dI[:, 1, 0:n], T.bi1[:, 0:n], 9, 7, SHR, AND, BI1, "dI1")
-        tt(gath(48, "V"), T.ff[:, 1, :], T.dI[:, 1, :].indirect(T.rep[:, 0:3]), T.DC[:], A.is_equal, "dI1 rep DC", "ff1")
-        scan(24, T.inc[:, 1, :], T.rrk[:], T.ff[:, 1, :], A.mult, A.add, "rrk ff1", "inc1")
-        tt(n, Z(12, n), Z(2, n), T.gs[:, 1, 0:n], A.subtract, "got1 gs1", "gd1")
-        tt(n, T.gd[:, 3:4 * n:4], Z(11, n), Z(12, n), A.add, "gd0 gd1", "gd")
-        mm(64, [(T.pM[:, 64:128], T.idm[:], T.gd[:])], "idm gd", "pM.r", True, False)
-        for t in range(2):
+            mm(16, [(T.pM[:, 67:128:4], T.idm[:], T.gs[:, 2 + t, :]), (T.pM[:, 67:128:4], T.idk[:, 6, :], T.gs[:, t, :])], "idm idk6 got%d gs%d" % (t, t), "pM.r", False, False)
+            if not last:
+                mm(16, [(T.pM[:, 128:144], T.idk[:, 3 * t + d, :], T.ff[:, t, 16 * d:16 * d + 16]) for d in range(3)], span("idk", 3 * t, 3 * t + 3) + " ff%d" % t, "pM.r", False, False)
             for x, y, k in ((T.tri, T.ff, "ff"), (T.BO, T.inc, "inc")):
                 mm(16, [(T.pM[:, 64 + d:128:4], x[:], y[:, t, 16 * d:16 * d + 16]) for d in range(3)], "tri BO %s%d" % (k, t), "pM.r", False, t == 1 and k == "inc")
-        add(P, {"V": plain(64)}, lambda q, e: q.tensor_tensor_scan(T.fr[:], T.r4[:], T.pM[:, 64:128], -207.0, A.max, A.min), "r4 pM.r", "fr")
-        tt(gath(L, "V"), T.D[:, 0:L], T.fr[:].indirect(T.bc[:, 16:16 + n]), T.THD[:, 0:L], A.is_le, "fr bc THD", "D")
-        for t in range(2):
-            mm(128, [(YB[t][:, 128 * h:128 * h + 128], T.D[:, 128 * h:128 * h + 128], T.BOK[:]) for h in range(NH)], "BOK D", YK[t], False, True)
+        scan(64, T.fr[:], T.r4[:], T.pM[:, 64:128], 48.0, A.max, A.min, "r4 pM.r", "fr")
+        if last:
+            cp(both(n), T.SL[:, 0:n], T.fr[:, 3:4 * n:4], "fr", "SL")
+        else:
+            tt(n, T.SL[:, 0:n], T.pM[:, 128:128 + n], T.fr[:, 3:4 * n:4], A.add, "pM.r fr", "SL")
+        for h in range(NH):
+            cp(gath(128), part(T.AO, h), T.tc[:].indirect(T.SL[:, 8 * h:8 * h + 8]), "tc tc1 SL", "AO%d" % h)
+            mm(128, [(part(YB[h], t), part(T.AO, h), T.BOK[:]) for t in range(2)], "BOK AO%d" % h, YK[h], False, True)
         if not last:
-            ts(n, T.zi[:, 1, 0:n], T.bi1[:, 0:n], 4095, None, AND, None, BI1, "b1")
-            tt(n, Z(14, n), T.gs[:, 1, 0:n], T.zi[:, 1, 0:n], A.mult, "gs1 b1", "bg1")
-            tt(n, bI, T.zi[:, 2, 0:n], Z(14, n), A.max, "bg0 bg1", "bI")
-            ts(n, dI, bI, 9, None, SHR, None, "bI", "dI")
-            lin(both(n, 1.0, S16), Z(26, n), dI, 64.0, 255.0, "dI", "z26")
-            tt(n, Z(25, n), Z(26, n), Z(15, n), A.add, "z26 ask0", "z25")
-            ts(n, T.XI[:, 0:n], bI, 511, None, AND, None, "bI", "XI")
-            tt(n, T.SL[:, 0:n], Z(25, n), T.fr[:, 3:4 * n:4], A.add, "z25 fr", "SL")
-            cp(gath(L), T.AO[:, 256:256 + L], T.tc[:].indirect(T.SL[:, 0:n]), "tc tc1 SL", "AO1")
-            cp(gath(L), T.AO[:, 0:L], ta.indirect(T.SL[:, 0:n]), TA + "SL", "AO0")
-            tt(gath(L, "V"), T.DX[:, 0:L], T.XI[:, 0:n].indirect(T.bc[:, 0:n]), T.ta[:, 0:L], A.mult, "XI bc ta", "DX")
-            part = lambda x, h: x[:, 128 * h:128 * h + 128]
-            mm([2 * L] + [128] * (2 * NH), [(T.pS[:, 0:8 * NH, :, :], T.idb[:], T.zer[:, 0:2 * L])] +
+            ts(n, T.zi[:, 1, 0:n], bj, 4095, None, AND, None, "bj0 bj1", "b1")
+            tt(n, Z(11, n), T.gs[:, 1, 0:n], T.zi[:, 1, 0:n], A.mult, "gs1 b1", "bg1")
+            tt(n, T.zi[:, 3, 0:n], T.zi[:, 2, 0:n], Z(11, n), A.max, "bg0 bg1", "bI")
+            ts(n, T.XI[:, 0:n], T.zi[:, 3, 0:n], 511, None, AND, None, "bI", "XI")
+            cp(both(n), T.bc[:, 20:20 + n], T.XI[:, 0:n], "XI", "XU")
+            cp(gath(L), T.DX[:, 0:L], T.tx[:].indirect(T.bc[:, 20:20 + n]), "tx XU", "DX")
+            mm([2 * L] + [128] * (2 * NH), [(T.pS[:, 0:n, :, :], T.idb[:], T.zer[:, 0:2 * L])] +
                [(T.pS[:, 8 * h:8 * h + 8, 1, :], part(x, h), y[:]) for h in range(NH) for x, y in ((T.OH0, T.Cm0), (T.OH1, T.Cm1))],
                "idb zer Cm0 Cm1 " + span("OH0_", 0, n) + " " + span("OH1_", 0, n), "pS.a pS.b", True, False)
             mm(128, [(T.pS[:, 8 * h:8 * h + 8, 0, :], part(T.DX, h), T.nBO[:]) for h in range(NH)], "nBO DX", "pS.a pS.b", False, False)
-            mm(256, [(T.pS[:, 8 * h:8 * h + 8, :, :], part(T.AO, 2 + h), T.RX[:]) for h in range(NH)], "RX0 RX1 AO1", "pS.a pS.b", False, True)
+            mm(256, [(T.pS[:, 8 * h:8 * h + 8, :, :], part(T.AO, h), T.RX[:]) for h in range(NH)], "RX " + span("AO", 0, NH), "pS.a pS.b", False, True)
             for h in range(NH):
-                mm(128, [(part(T.pA, h), part(T.AO, h), T.idb[:])], "idb AO0", "pA.a%d" % h)
-            cp(both(L), T.AW[:, 0:64 * NH:8, :], T.pA[:, 0:L], each("pA.a%d", NH), each("AW%d", NH))
-        for t in range(2):
-            relu(both(L, 1.0, S16), T.AF[:, 128 * t:128 * t + 64 * NH:8, :], YB[t][:, 0:L], 1024.0 - 32768.0 - 4096.0, YK[t], "AF%d AF%d" % (2 * t, 2 * t + 1))
-            mm(64, [(T.pM[:, 128:192], T.AF[:, 128 * t + 64 * h + 7 * k:128 * t + 64 * h + 7 * k + 8, :], T["B%d" % t][:, 512 * h + 64 * k:512 * h + 64 * k + 64])
-                    for h in range(NH) for k in range(8)], "AF%d AF%d " % (2 * t, 2 * t + 1) + each("B%d%%d" % t, NH), "pM.m", t == 0, t == 1)
+                mm(128, [(part(T.pA, h), part(T.AO, h), T.RA[:])], "RA AO%d" % h, "pA.a%d" % h)
+            relu(both(L), T.AW[:, 0:64 * NH:8, :], T.pA[:, 0:L], -1.0, span("pA.a", 0, NH), span("AW", 0, NH))
+        for h in range(NH):
+            relu(both(256), T.AF[:, 128 * h:128 * h + 128:8, :], YB[h][:, 0:256], 1024.0 - 32768.0 - 4096.0, YK[h], "AF%d AF%d" % (2 * h, 2 * h + 1))
+            mm(64, [(T.pM[:, 160:224], T.AF[:, 128 * h + 64 * t + 7 * k:128 * h + 64 * t + 7 * k + 8, :], T["B%d" % t][:, 512 * h + 64 * k:512 * h + 64 * k + 64])
+                    for t in range(2) for k in range(8)], "AF%d AF%d B0%d B1%d" % (2 * h, 2 * h + 1, h, h), "pM.m", h == 0, h == NH - 1)
         if not last:
-            relu(both(2 * L, 1.0, S16), T.X[:, 0:2 * L], T.pS[:, 0:8 * NH, :, :], 1024.0 - 32768.0, "pS.a pS.b", "X")
+            relu(both(2 * L), T.X[:, 0:2 * L], T.pS[:, 0:n, :, :], 1024.0 - 65536.0, "pS.a pS.b", "X")
             mm(32, [(T.pA[:, 256:288], T.AW[:, 64 * h + 7 * k:64 * h + 7 * k + 8, :], T.X[:, 256 * h + 32 * k:256 * h + 32 * k + 32])
                     for h in range(NH) for k in range(8)], "AW0 AW1 X", "pA.o")
-        tt(32, T.MSG[:, rnd, 0:32], T.pM[:, 128:160], T.mp[:, 0:32], A.max, "pM.m mp", "MSG0")
-        tt(32, T.mp16[:, 0:32], T.pM[:, 160:192], T.mp[:, 32:64], A.max, "pM.m mp", "mp16")
+        tt(32, T.MSG[:, rnd, 0:32], T.pM[:, 160:192], T.mp[:, 0:32], A.max, "pM.m mp", "MSG0")
+        tt(32, T.mp16[:], T.pM[:, 192:224], T.mp[:, 32:64], A.max, "pM.m mp", "mp16")
         if not last:
-            cp(both(32, 1.0, S16), T.MSG[:, rnd, 32:64], T.pA[:, 256:288], "pA.o", "MSG1")
+            cp(both(32), T.MSG[:, rnd, 32:64], T.pA[:, 256:288], "pA.o", "MSG1")
+            per = len(chip) // len(far)
             for u in range(2):
                 piece = lambda x, k, o: x[:, k, o + 32 * u:o + 32 * u + 32]
-                on = chip if u == 0 else [e for e in chip if e not in out_e]
-                per = len(on) // len(far)
-                over = [(h, on[i * per:(i + 1) * per], "hm%d" % (2 * rnd + u), piece(T.MSG, rnd, 0), piece(T.HM, rnd, 0)) for i, h in enumerate(close)]
-                straight = []
+                ls[0] += remote([(h, chip[i * per:(i + 1) * per], "hm%d" % (2 * rnd + u), piece(T.MSG, rnd, 0), piece(T.HM, rnd, 0)) for i, h in enumerate(close)],
+                                "ls", "MSG%d" % u, "msg%d" % u)
                 for q in near:
                     d = (rank - q) % N
                     j = 3 * rnd + d - 1
-                    straight.append((T.cores[q], out_e, "m%d" % (2 * j + u), piece(T.MSG, rnd, 0), piece(T.IN, j, 12 - 4 * d)))
-                for items in ([over, straight] if u == 0 else [over + straight]):
-                    ls[0] += remote(items, "ls", "MSG%d" % u, "msg%d" % u)
+                    ls[0] += remote([(T.cores[q], out_e, "m%d" % (2 * j + u), piece(T.MSG, rnd, 0), piece(T.IN, j, 12 - 4 * d))], "ls", "MSG%d" % u, "msg%d" % u)
                 for d in range(1, N):
                     j = 3 * rnd + d - 1
-                    lands("m%d" % (2 * j + u), len(out_e), "msg%d" % u, ("IM%d", "IN%d")[u] % j, 1.0 if (rank + d) % N in near else 1.9)
+                    lands("m%d" % (2 * j + u), len(out_e), "msg%d" % u, ("IM%d", "IN%d")[u] % j, NEAR1 if (rank + d) % N in near else FAR1)
         P["at"] = "last" if last else "front"
         cp(gath(GH), T.W[:, 0:GH], T.S0[:].indirect(T.MSG[:, rnd, 0:32]), "Sp0 Sx0 MSG0 sent", "Wa")
-        cp(gath(GH), T.W[:, GH:V], T.S0[:].indirect(T.mp16[:, 0:32]), "Sp0 Sx0 mp16", "Wb")
+        cp(gath(GH), T.W[:, GH:V], T.S0[:].indirect(T.mp16[:]), "Sp0 Sx0 mp16", "Wb")
         if last:
             dma("S", T.y[:, 0:GH], T.W[:, 0:GH], "Wa", "ya")
             dma("Y", T.y[:, GH:V], T.W[:, GH:V], "Wb", "yb")
             break
-        tt(64, T.FZ[:], T.pM[:, 128:192], T.MK[:], A.is_lt, "pM.m MK", "FZ")
+        tt(64, T.FZ[:], T.pM[:, 160:224], T.MK[:], A.is_lt, "pM.m MK", "FZ")
         requests(rnd + 1)
-        front(T.L0, "L0 Ls0", CUT[(16, 0)], 0, 6)
+        front(T.L0, "L0 Ls0", CUT[16], 0, 7)
         j0 = 3 * rnd
-        INS = "IN%d IN%d IN%d" % (j0, j0 + 1, j0 + 2)
+        INS = span("IN", j0, j0 + 3)
         for d in range(1, N):
-            refresh(N - d, j0 + d - 1, 0, 2)
+            at, m, j = V + (N - d - 1) * GH, 12 - 4 * d, j0 + d - 1
+            cp(gath(GH), T.W[:, at:at + GH], SR[N - d][:].indirect(T.IN[:, j, m:m + 32]), "Sz%d Sp%d Sx%d IM%d" % (N - d, N - d, N - d, j), "W%d" % (N - d))
         for d in (2, 1, 3, 0):
             if d == 0 or rnd < RO - 2:
                 keep(d)
-        ts(9, T.L0[:, 7:16], T.IN[:, j0:j0 + 3, 40:43], -1.0, 1024.0, A.mult, A.add, "L0 " + INS, "Ls1")
-        cp(9, T.L0[:, 39:48], T.IN[:, j0:j0 + 3, 56:59], "L0 " + INS, "Lc1")
-        front(T.L0, LS, CUT[(16, 0)], 6, 16)
+        lin(both(9), T.L0[:, 7:16], T.IN[:, j0:j0 + 3, 40:43], -1.0, 1024.0, "L0 " + INS, "Ls1")
+        cp(both(9), T.L0[:, 39:48], T.IN[:, j0:j0 + 3, 56:59], "L0 " + INS, "Lc1")
+        lin(both(1), T.L0[:, 48:49], T.IN[:, j0, 40:41], -1.0, 1024.0, "L0 IN%d" % j0, "Ls2")
+        front(T.L0, "Ls2", CUT[16], 7, 8, 41)
+        front(T.L0, LS, CUT[16], 8, 16)
         cp(gath(160), T.BAN[:, 96:256], T.ta[:].indirect(T.L0[:, 38:48]), TA + "tao L0 Lc1", span("BAN_", 6, 16))
-        ts(9, T.L0[:, 23:32], T.L0[:, 7:16], 1.0 / 16, 32 - 15.0 / 32, A.mult, A.add, LS, "Lb1")
+        lin(both(9), T.L0[:, 23:32], T.L0[:, 7:16], 1.0 / 16, 32 - 15.0 / 32, LS, "Lb1")
 
     issue(P, eng, T)
     g.wait_ge(T.sem.ls, ls[0])

import math
import numpy as np
from concourse.bass import DstId, RemoteDMATransfer
from concourse.mybir import AluOpType as A, ActivationFunctionType as F

V, GH, RO = 1024, 512, 4
BIG = 2.0 ** 94
LNB = math.log(1.75)
LN0 = 90 * math.log(2.0)
WAKE, CROSS, GATHER, PE, FIX, FIXS, LOAD, HOP = 130, 0, 1.56, 0.72, 36, 70, 2400, 2400
FAR0, NEAR0, FAR1, NEAR1, PT0 = 2.5, 1.3, 1.75, 1.0, 2.0
SPARE, TRIES, WARM, SEED = 1.0, (2000, 13000), 300.0, 1
CUT = {8: [(0, 4)], 16: [(0, 4), (8, 4)]}
START = {"r2 s00": "VSVS", "r2 s01": "SSSS", "r2 s10": "SSSS", "r2 s11": "SSSS"}
WIDE = {"r2 s01": (2, 0, 2, 0), "r2 s10": (2, 0, 2, 0), "r2 s11": (2, 0, 1, 1)}
TURN = {"r2 s00": (0, 2, 0, 2), "r2 s01": (0, 2, 0, 2), "r2 s10": (0, 2, 0, 2), "r2 s11": (0, 2, 1, 1)}
LAID, ENDS = {}, []


def _sb(n, d="float32"):
    return ("sbuf", [128] + (n if isinstance(n, list) else [n]), d)


H, I32, U16, F16 = "bfloat16", "int32", "uint16", "float16"
SCRATCH = {
    "W": _sb(2560, H), "S0": _sb(2048, H), "S1": _sb(2048, H), "S2": _sb(2048, H), "S3": _sb(2048, H),
    "nbi": _sb(V + 16, I32), "pti": _sb(V, I32), "pli": _sb(V + 16, I32), "cst": _sb(V + 16, I32),
    "rq": _sb(28, I32), "rqb": _sb(28, I32), "thi": _sb(4, I32), "col": _sb(20), "coli": _sb(4, I32),
    "row": _sb(144), "rowg": _sb(128), "rowj": _sb(128), "Rc": _sb(512, H), "RA": _sb(128, H), "RX": _sb([8, 2, 16], H),
    "idb": _sb(128, H), "id12": _sb(128, H), "id4": _sb(128, H), "idB": _sb(128, H), "idF": _sb(128, H), "idm": _sb(128, H), "idw": _sb(128, H), "id32": _sb(128),
    "thM": _sb(128, F16), "on12": _sb(128, H), "zer": _sb(592, H), "tx": _sb(512),
    "BOc": _sb(128, H), "Cm0": _sb(128, H), "Cm1": _sb(128, F16),
    "BO": _sb(128, H), "nBO": _sb(128, H), "BOK": _sb(128, H), "tri": _sb(128, H), "EE": _sb(144, H), "SWs": _sb([4, 128], H), "SWb": _sb([4, 128], H),
    "ta": _sb(1296, H), "taf": _sb(256), "tb": _sb(192, H), "tba": _sb(128), "tcf": _sb(384, H), "tc": _sb(768, H), "sel": _sb(128, H),
    "bc": _sb(36, U16), "dc": _sb(48), "r4": _sb(64),
    "rmin": _sb(128), "rmax": _sb(128), "rrk": _sb(48, H), "offc": _sb(8, I32), "wi": _sb(32), "wcol": _sb(2), "thr": _sb(16),
    "mp": _sb(64), "mp16": _sb(32, U16), "FZ": _sb(64, H), "MK": _sb(64, H), "Ms": _sb(192, H), "DC": _sb(48),
    "AW": _sb([128, 16], H), "AF": _sb([256, 16], F16),
    "L0": _sb(50, U16), "s1": _sb(16, U16), "b1": _sb(16, U16), "cl": _sb([2, 16], U16),
    "Q": _sb(256, U16), "Qf": _sb(256, F16), "CK": _sb(256), "BAN": _sb(256, H),
    "OH0": _sb(256, H), "OH1": _sb(256, H), "G": _sb(4096, H), "GT": _sb(4096, H),
    "ov": _sb(256), "kR": _sb([8, 2, 16]), "kT": _sb(256), "km": _sb(256), "ki": _sb([2, 16], I32), "off": _sb(16, U16),
    "CS": _sb([2, 16], H), "K1": _sb(256), "kq": _sb(256), "K1T": _sb(256), "bm": _sb(256), "bi": _sb(16, I32), "bj": _sb([2, 2, 4], I32),
    "AR0": _sb(256, H), "AR1": _sb(256, H), "FB": _sb(256, H), "B0": _sb(1024, H), "B1": _sb(1024, H), "LK": _sb(256, H), "PL0": _sb(256, F16), "PL1": _sb(256, F16),
    "z": _sb([12, 16]), "zi": _sb([5, 16], I32), "dI": _sb([2, 16], I32), "gs": _sb([4, 16], H), "idk": _sb([7, 128], H), "ff": _sb([2, 48], H), "inc": _sb([2, 48], H),
    "fr": _sb(64), "XI": _sb(16, I32), "SL": _sb(16, U16), "DX": _sb(256, F16), "AO": _sb(256, H), "X": _sb(512, F16),
    "MSG": _sb([4, 64], U16), "IN": _sb([9, 72], U16), "HB": _sb(128, H), "HM": _sb([3, 64], U16),
}
for _p in ("pA", "pB0", "pB1", "pM", "pY"):
    SCRATCH[_p] = ("psum", [128, 512], "float32")
for _p in ("pC0", "pC1", "pS"):
    SCRATCH[_p] = ("psum", [128, 16, 2, 16], "float32")
SEMAPHORES = (["cV", "cS", "cP", "cG", "l0", "ls", "hx", "xg1", "xg2", "xg3"] + ["hm%d" % k for k in range(6)] + ["m%d" % k for k in range(18)] + ["d%d" % k for k in range(32)])


def bits(es):
    m = 0
    for e in es:
        m |= 1 << e
    return m


def ways(T, topo, r):
    me = T.cores[r]
    n = len(T.cores)
    near = [q for q in range(n) if q != r and topo.may_write(me, T.cores[q])]
    far = [q for q in range(n) if q != r and q not in near]
    hands = [c for c in topo.cores_of(me) if T.rank_of(c) is None and all(topo.may_write(c, T.cores[q]) for q in far)]
    close = sorted(hands, key=lambda c: topo.die(c) != topo.die(me))[:len(far)]
    return near, far, hands, close


def send(g, T, topo, me, items, sem_here):
    trs = []
    for dst, es, sem, src, out in items:
        rid, pid = topo.addr(dst, me)
        trs.append(RemoteDMATransfer(dst_ids=[DstId(rid=rid, pnc=pid)], dma_engine_mask=bits(es), remote_sem=T.sem[sem], srcs=[src], dsts=[out]))
    g.remote_dma_fused(trs, local_sem=T.sem[sem_here])
    return sum(len(it[1]) for it in items)


def helper(g, core, T, topo):
    own = [c for c in topo.cores_of(core) if T.rank_of(c) is not None]
    if not own:
        return
    r = T.rank_of(own[0])
    n = len(T.cores)
    near, far, hands, close = ways(T, topo, r)
    if core not in hands:
        return
    k = hands.index(core)
    wd = GH // len(hands)
    es = topo.engines(core, T.cores[far[0]])
    per = len(es) // len(far)
    g.wait_ge(T.sem.hx, len(topo.engines(own[0], core)) // len(hands))
    items = []
    for i, q in enumerate(far):
        d = (q - r) % n
        a = V + (d - 1) * GH + k * wd
        items.append((T.cores[q], es[i * per:(i + 1) * per], "xg%d" % d, T.HB[:, 0:wd], T.W[:, a:a + wd]))
    ls = send(g, T, topo, core, items, "ls")
    if core in close:
        q = far[close.index(core)]
        d = (r - q) % n
        for t in range(RO - 1):
            j = 3 * t + d - 1
            for u in range(2):
                g.wait_ge(T.sem["hm%d" % (2 * t + u)], len(topo.engines(own[0], core)) // len(far))
                a = 12 - 4 * d + 32 * u
                ls += send(g, T, topo, core, [(T.cores[q], es, "m%d" % (2 * j + u), T.HM[:, t, 32 * u:32 * u + 32], T.IN[:, j, a:a + 32])], "ls")
    g.wait_ge(T.sem.ls, ls)


def add(P, cost, fn, R, Wr, lat=0, tok=None, start=False, stop=False):
    R, Wr = R.split(), Wr.split()
    k = len(P["ops"])
    dep = {}
    for x in R:
        if x in P["lastw"]:
            dep[P["lastw"][x]] = True
    onP = "P" in cost
    for x in Wr:
        if x in P["lastw"]:
            a = P["lastw"][x]
            dep[a] = dep.get(a, False) or not (onP and "P" in P["ops"][a]["cost"])
        for a in P["reads"].get(x, []):
            dep[a] = True
    banks = sorted(set(x.split(".")[0] for x in R + Wr if x[0] == "p" and x[1].isupper()))
    for b in banks:
        if onP and b != "pA":
            if start and b in P["chain"]:
                dep.setdefault(P["chain"][b], False)
            if stop:
                P["chain"][b] = k
    for e in cost:
        if e in "GY":
            if e in P["pin"]:
                dep.setdefault(P["pin"][e], False)
            P["pin"][e] = k
    dep.pop(k, None)
    for x in R:
        P["reads"].setdefault(x, []).append(k)
    for x in Wr:
        P["lastw"][x] = k
        P["reads"][x] = []
    site = P["at"] + " " + Wr[0].rstrip("0123456789_")
    P["sites"][site] = P["sites"].get(site, 0) + 1
    P["ops"].append({"site": "%s %d" % (site, P["sites"][site]), "cost": cost, "fn": fn, "dep": dep, "lat": lat, "tok": tok, "banks": banks})


def lay(P):
    ops = P["ops"]
    n = len(ops)
    before = [[(a, (WAKE + ops[a]["lat"]) if w else 0) for a, w in o["dep"].items()] for o in ops]
    rest = [0.0] * n
    for k in range(n - 1, -1, -1):
        rest[k] += min(ops[k]["cost"].values())
        for a, d in before[k]:
            rest[a] = max(rest[a], rest[k] + d + (CROSS if d == WAKE and not set(ops[a]["cost"]) & set(ops[k]["cost"]) else 0))
    site = [o["site"] for o in ops]
    ways_ = [list(o["cost"].items()) for o in ops]

    def late(line, t, pad):
        i = len(line)
        while i > 0 and line[i - 1][1] + pad > t:
            i -= 1
        return line[i:]

    def enter(line, x):
        i = len(line)
        while i > 0 and line[i - 1][0] > x[0]:
            i -= 1
        line.insert(i, x)

    def place(on, up, a0, a1, start=None):
        if start is None:
            line, bank, at, key, end = {e: [] for e in ("V", "S", "P", "G", "Y", "far")}, {}, [None] * n, [0.0] * n, 0.0
        else:
            end, at, key = start[0], list(start[1]), list(start[4])
            bank, line = {b: x[-40:] for b, x in start[2].items()}, {e: x[-150:] for e, x in start[3].items()}
            if a1 == n:
                bank = {b: list(x) for b, x in start[2].items()}
        for k in range(a0, a1):
            x = -rest[k] - up.get(site[k], 0)
            for a, d in before[k]:
                if key[a] >= x:
                    x = key[a] + 1e-3
            key[k] = x
        for k in sorted(range(a0, a1), key=lambda k: key[k]):
            best = None
            for e, c in ways_[k]:
                if len(ways_[k]) > 1 and on.get(site[k], e) != e:
                    continue
                t0 = 0.0
                for a, d in before[k]:
                    x = at[a][1] + (d + CROSS if d == WAKE and at[a][2] != e else d)
                    if x > t0:
                        t0 = x
                busy = late(line[e], t0, 0) if e != "far" else []
                if ops[k]["banks"]:
                    busy = sorted(busy + [(a - WAKE - CROSS, b + WAKE + CROSS) for bk in ops[k]["banks"] for a, b, e2, j in late(bank.setdefault(bk, []), t0, WAKE + CROSS) if e2 != e])
                t = t0
                for a, b in busy:
                    if t + c <= a:
                        break
                    if b > t:
                        t = b
                by = t + c + (SPARE * c if e == "V" else 0)
                if best is None or by < best[0]:
                    best = (by, t, t + c, e)
            at[k] = best[1:]
            enter(line[best[3]], best[1:3])
            for bk in ops[k]["banks"]:
                enter(bank[bk], best[1:] + (k,))
            end = max(end, best[2] + ops[k]["lat"])
        return end, at, bank, line, key

    def anneal(on, up, names, worth, tries):
        free = [x for x in dict.fromkeys(site[k] for k in range(n) if len(ways_[k]) > 1) if x in names]
        now = worth(on, up)
        best = (now, on, up)
        for it in range(tries):
            on2, up2 = dict(on), dict(up)
            for _ in range((1, 1, 2, 3)[rng.randint(4)]):
                if rng.rand() < 0.35:
                    x, e = free[rng.randint(len(free))], "VS-"[rng.randint(3)]
                    if e == "-":
                        on2.pop(x, None)
                    else:
                        on2[x] = e
                else:
                    x = names[rng.randint(len(names))]
                    up2[x] = (up2.get(x, 0) + (-1500, -600, -300, 300, 600, 1500, 3000)[rng.randint(7)]) if rng.rand() < 0.4 else 0
            end = worth(on2, up2)
            if end <= now + WARM * (1 - it / tries) * rng.rand() ** 3:
                now, on, up = end, on2, up2
                if end < best[0]:
                    best = (end, on, up)
        return best[1:]

    head = min(k for k in range(n) if site[k].startswith("front"))
    mark = min(k for k in range(n) if site[k] == "r2 s01 ov 1")
    upto = min(k for k in range(mark, n) if site[k].startswith("r2 m1"))
    shape = tuple(o["lat"] for o in ops)
    rng = np.random.RandomState(SEED)
    if shape not in LAID:
        on, up = {"%s G %d" % (s, i + 1): e for s, es in START.items() for i, e in enumerate(es)}, {}
        on.update({"last Wa 1": "S", "last Wb 1": "V"})
        on, up = anneal(on, up, list(dict.fromkeys(site[:head])), lambda on, up: place(on, up, head, upto, place(on, up, 0, head))[1][mark][1], TRIES[0])
        start = place(on, up, 0, head)
        LAID[shape] = anneal(on, up, list(dict.fromkeys(site[head:])), lambda on, up: place(on, up, head, n, start)[0], TRIES[1])
    end, at, bank = place(*LAID[shape], head, n, place(*LAID[shape], 0, head))[:3]
    ENDS.append(end)
    for k in range(n):
        ops[k]["e"] = at[k][2]
    for uses in bank.values():
        last = {}
        for a, b, e, k in uses:
            for e2, k2 in last.items():
                if e2 != e:
                    ops[k]["dep"][k2] = True
            last[e] = k
    return sorted(range(n), key=lambda k: (at[k][0], at[k][1], k))


def issue(P, eng, T):
    ops = P["ops"]
    cnt, seen = {}, {}
    for k in lay(P):
        o = ops[k]
        e = o["e"]
        if e == "far":
            cnt[o["tok"][0]] = o["tok"][1]
            continue
        need = {}
        for a, w in o["dep"].items():
            if w and ops[a]["tok"]:
                s, v = ops[a]["tok"]
                need[s] = max(need.get(s, 0), v)
        for s, v in need.items():
            if seen.get((e, s), 0) < v:
                eng[e].wait_ge(T.sem[s], v)
                seen[(e, s)] = v
        out = o["fn"](eng[e], e)
        if o["tok"]:
            out.then_inc(T.sem[o["tok"][0]], o["tok"][1])
            cnt[o["tok"][0]] = o["tok"][1]
        elif out is not None:
            s = "c" + e
            for ins in (out if isinstance(out, list) else [out]):
                ins.then_inc(T.sem[s], 1)
                cnt[s] = cnt.get(s, 0) + 1
            o["tok"] = (s, cnt[s])
    for s in sorted(cnt):
        if seen.get(("G", s), 0) < cnt[s]:
            eng["G"].wait_ge(T.sem[s], cnt[s])


def rank_program(g, core, T, topo):
    rank = T.rank_of(core)
    if rank is None:
        helper(g, core, T, topo)
        return
    N = len(T.cores)
    near, far, hands, close = ways(T, topo, rank)
    eng = {"V": g.vector, "S": g.scalar, "P": g.tensor, "G": g, "Y": g.sync}
    P = {"ops": [], "lastw": {}, "reads": {}, "chain": {}, "pin": {}, "at": "set", "sites": {}}
    nd, ls, big = [0], [0], []
    plain = lambda n: max(64.0, n) + FIX
    gath = lambda n, es="VS": {e: (60 if e == "V" else 78) + GATHER * n for e in es}
    both = lambda n, r=1.0: {"V": plain(n * r), "S": plain(n) + FIXS}
    vec = lambda n: n if isinstance(n, dict) else {"V": plain(n)}

    def dma(e, out, in_, R, Wr, lat=1.0):
        s = "d%d" % nd[0]
        nd[0] += 1
        add(P, {e: 50}, lambda q, _e: q.dma_start(out, in_), R, Wr, lat * LOAD, (s, 16))

    def lands(s, n, R, key, lat):
        add(P, {"far": 1}, None, R, key, lat * HOP, (s, n))

    def ts(n, out, in0, s1, s2, o0, o1, R, Wr):
        if o1 is None:
            add(P, vec(n), lambda q, e: q.tensor_scalar(out, in0, s1, None, o0), R, Wr)
        else:
            add(P, vec(n), lambda q, e: q.tensor_scalar(out, in0, s1, s2, o0, o1), R, Wr)

    def tt(n, out, a, b, o, R, Wr):
        add(P, vec(n), lambda q, e: q.tensor_tensor(out, a, b, o), R, Wr)

    def cp(c, out, a, R, Wr):
        add(P, vec(c), lambda q, e: q.tensor_copy(out, a) if e == "V" else q.activation(out, a, F.Copy), R, Wr)

    def lin(c, out, a, scale, bias, R, Wr):
        add(P, c, lambda q, e: q.tensor_scalar(out, a, scale, bias, A.mult, A.add) if e == "V" else q.activation(out, a, F.Identity, bias=bias, scale=scale), R, Wr)

    def relu(c, out, a, bias, R, Wr):
        add(P, c, lambda q, e: q.tensor_scalar(out, a, bias, 0.0, A.add, A.max) if e == "V" else q.activation(out, a, F.Relu, bias=bias), R, Wr)

    def act(c, out, a, f, R, Wr):
        add(P, {"S": c}, lambda q, e: q.activation(out, a, f), R, Wr)

    def mm(n, items, R, Wr, start=True, stop=True, least=64):
        m = len(items)
        c = PE * (sum(max(least, x) for x in n) if isinstance(n, list) else m * max(least, n))
        add(P, {"P": c}, lambda q, e: [q.matmul(o, l, r, start and i == 0, stop and i == m - 1) for i, (o, l, r) in enumerate(items)], R, Wr, 0, None, start, stop)

    def scan(n, out, a, b, first, o0, o1, R, Wr):
        add(P, vec(n), lambda q, e: q.tensor_tensor_scan(out, a, b, first, o0, o1), R, Wr)

    def turn(n, out, a, R, Wr):
        add(P, vec(n), lambda q, e: q.transpose(out, a), R, Wr)

    def fill(n, ap, c, Wr):
        add(P, vec(n), lambda q, e: q.memset(ap, c), "", Wr)

    def iota(n, ap, pat, base, cm, Wr, flt=True):
        if flt:
            add(P, {"G": 160 + 2 * n}, lambda q, e: q.iota(ap, pat, base, cm, allow_small_or_imprecise_dtypes=True), "", Wr)
        else:
            add(P, {"G": 160 + 2 * n}, lambda q, e: q.iota(ap, pat, base, cm), "", Wr)

    def put(n, ap, pat, val, base, key):
        add(P, {"G": 200 + 2 * n}, lambda q, e: q.affine_select(ap, ap, pat, A.not_equal, val, base, -1), key, key)

    def remote(items, sem, R, Wr, c=350):
        def fn(q, e):
            send(g, T, topo, core, items, sem)
        add(P, {"G": c}, fn, R, Wr)
        return sum(len(it[1]) for it in items)

    C = lambda k: T.col[:, k:k + 1]
    Z = lambda k, n: T.z[:, k, 0:n]
    SR = [T.S0, T.S1, T.S2, T.S3]
    SHR, AND = A.logical_shift_right, A.bitwise_and
    span = lambda s, a, b: " ".join("%s%d" % (s, k) for k in range(a, b))
    part = lambda x, h: x[:, 128 * h:128 * h + 128]

    dma("Y", T.W[:, 0:GH], T.x[:, 0:GH], "", "Wa")
    dma("S", T.rq[:], T.req[:], "", "rq")
    dma("S", T.thi[:, 0:1], T.th[:], "", "thi")
    dma("Y", T.nbi[:, 0:V], T.nb[:], "", "nbi", 2)
    iota(1, T.coli[:, 0:1], [[0, 1]], 0, 1, "coli", False)
    iota(144, T.row[:], [[1, 144]], 0, 0, "row")
    iota(128, T.rowj[:], [[0, 8], [1, 16]], 0, 0, "rowj")
    iota(128, T.rowg[:], [[1, 8], [0, 16]], 0, 0, "rowg")
    iota(2, T.wi[:, 0:2], [[128, 2]], 0, 1, "wi0")
    iota(16, T.wi[:, 16:32], [[16, 16]], 0, 0, "wi1")
    iota(64, T.tba[:, 0:64], [[1, 8], [0, 8]], 0, 0, "tba")
    iota(64, T.tba[:, 64:128], [[0, 8], [1, 8]], 8, 0, "tbb")
    chip = topo.engines(core, hands[0])
    per = len(chip) // len(hands)
    wd = GH // len(hands)
    out_e = topo.engines(core, T.cores[near[0]])
    l0 = remote([(h, chip[i * per:(i + 1) * per], "hx", T.W[:, i * wd:(i + 1) * wd], T.HB[:, 0:wd]) for i, h in enumerate(hands)], "l0", "Wa", "out0", 1300)
    for q in near:
        d = (q - rank) % N
        a = V + (d - 1) * GH
        l0 += remote([(T.cores[q], out_e, "xg%d" % d, T.W[:, 0:GH], T.W[:, a:a + GH])], "l0", "Wa", "out1")
    iota(8, T.offc[:], [[512, 4], [16, 2]], 0, 0, "offc issued", False)
    dma("Y", T.pti[:], T.pt[:], "issued", "pti", PT0)
    dma("Y", T.W[:, GH:V], T.x[:, GH:V], "", "Wb", PT0 + 0.3)
    for d in range(1, N):
        q = (rank - d) % N
        nq, fq, hq, _c = ways(T, topo, q)
        lands("xg%d" % d, len(out_e) if rank in nq else len(hq) * (len(topo.engines(hq[0], core)) // len(fq)), "out0 out1", "W%d" % d, NEAR0 if rank in nq else FAR0)
    lands("l0", l0, "out0 out1", "sent", 1)
    fill(256, T.Rc[:], 0.0, "Rc")
    put(512, T.Rc[:], [[16, 8], [1, 8], [0, 8]], 1.0, 0, "Rc")
    put(512, T.Rc[:], [[16, 8], [0, 8], [1, 8]], 1.0, 8, "Rc")
    iota(64, T.mp[:], [[16, 64]], 0, 0, "mp")
    iota(48, T.dc[:], [[1, 3], [0, 16]], 3, 0, "dc")
    iota(128, T.sel[:], [[0, 8], [32, 4], [0, 4]], 0, 0, "sel")
    iota(256, T.taf[:], [[1, 16], [0, 16]], 0, 0, "taf")
    for k, (pat, base) in enumerate((([[0, 96], [1, 4]], 0), ([[0, 24], [1, 4], [0, 4]], 4), ([[1, 6], [0, 64]], 5), ([[0, 6], [1, 4], [0, 16]], 12))):
        add(P, {"G": 930}, lambda q, e, k=k, pat=pat, base=base: q.iota(T.tcf[32 * k:32 * k + 32, :], pat, base, 0, allow_small_or_imprecise_dtypes=True),
            "tcf%d" % (k - 1) if k else "taf", "tcf%d" % k)
    add(P, {"G": 420}, lambda q, e: q.iota(T.BOK[:], [[0, 128]], 0, 0, allow_small_or_imprecise_dtypes=True), "tcf3", "BOK")
    fill(64, T.RA[:], 0.0, "RA")
    fill(128, T.RX[:], 0.0, "RX")
    low, high, flat = [[16, 8], [0, 4], [1, 4]], [[16, 8], [1, 4], [0, 4]], [[16, 8], [0, 16]]
    for out, key, val, pat, base in ([(T.BOK[:], "BOK", 4096.0, flat, r) for r in (12, 13, 14)] + [(T.RA[:], "RA", 1.0, low, 0), (T.RA[:], "RA", 1.0, high, 4)] +
                                     [(T.RX[:, :, f, :], "RX", 32768.0, pat, base) for f in range(2) for pat, base in ((high, 8), (low, 12))] +
                                     [(T.RX[:, :, 1, :], "RX", 1040.0, flat, 11)]):
        put(128, out, pat, val, base, key)
    iota(512, T.tx[:], [[1, 512]], 0, 0, "tx")
    iota(1024, T.AW[:, 64:128, :], [[0, 1024]], 0, 0, "AW1")
    fill(512, T.AW[:, 0:64, :], 0.0, "AW0")

    ts(1, T.coli[:, 1:2], T.coli[:, 0:1], 15, None, AND, None, "coli", "coli1")
    ts(1, T.coli[:, 2:3], T.coli[:, 0:1], 4, None, SHR, None, "coli", "coli2")
    ts(1, T.coli[:, 3:4], T.coli[:, 0:1], 4, 1, SHR, AND, "coli", "coli3")
    cp(4, T.col[:, 0:4], T.coli[:, 0:4], "coli coli1 coli2 coli3", "col")
    ts(128, T.id32[:], T.row[:, 0:128], C(0), None, A.is_equal, None, "row col", "id32")
    ts(128, T.ta[:, 0:128], T.rowj[:], C(1), None, A.is_equal, None, "rowj col", "ta")
    for nm, sc in (("id12", 2.0 ** -12), ("idb", 1.0), ("id4", 4.0), ("idB", 32768.0), ("idm", -255.0), ("idF", BIG), ("idw", 1.75 ** -128)):
        lin(both(128), T[nm][:], T.id32[:], sc, 0.0, "id32", nm)
    for w in (128, 256, 512):
        cp(both(w, 0.5), T.ta[:, w:2 * w], T.ta[:, 0:w], "ta", "ta")
    for k, a, sc, off in ((4, 3, -1.0, 1.0), (5, 0, 1.0, 16.0), (6, 0, 1.0, -16.0), (7, 2, 16.0, 15.0), (8, 1, 16.0, 0.0), (9, 1, 32.0, 0.0), (15, 1, 1.0, -1024.0)):
        lin(both(1), C(k), C(a), sc, off, "col", "col%d" % k)
    ts(1, C(16), C(1), 11.0, None, A.is_equal, None, "col", "col16")
    lin(both(128), T.BOc[:], T.rowj[:], -1.0 / 16, 15.0 / 16 + 1536.0 / 65536, "rowj", "BOc")
    ts(16, T.wi[:, 16:32], T.wi[:, 16:32], C(1), -LNB, A.add, A.mult, "wi1 col", "wi1")
    ts(2, T.wi[:, 0:2], T.wi[:, 0:2], -LNB, LN0, A.mult, A.add, "wi0", "wi0")
    ts(16, T.wi[:, 16:32], T.wi[:, 16:32], LN0 + math.log(2.53), None, A.add, None, "wi1", "wi1")
    for k, (a, b) in enumerate(((0, 4), (5, 4), (6, 3), (0, 3))):
        ts(128, T.SWb[:, k, :], T.row[:, 0:128], C(a), C(b), A.is_equal, A.mult, "row col col4 col5 col6", "SW%d" % k)
    act(1600, T.wcol[:], T.wi[:, 0:2], F.Exp, "wi0", "wcol")
    act(100, T.thr[:], T.wi[:, 16:32], F.Exp, "wi1 wcol", "thr")
    lin(both(512, 0.5), T.SWs[:], T.SWb[:], 2.0 ** -16, 0.0, "SW0 SW1 SW2 SW3", "SWs")
    for x, c in (("rmin", 1024.0), ("rmax", -1024.0)):
        fill(128, T[x][:], 0.0, x)
        fill(8, T[x][:, 0:128:16], c, x)
    fill(16, T.ta[:, V:V + 16], 0.0, "taz")
    fill(1, T.ta[:, V:V + 1], 1.0, "taz")
    ts(128, T.BO[:], T.rowg[:], C(2), None, A.is_equal, None, "rowg col", "BO")
    tt(256, T.BOc[:], T.BOc[:], T.BO[:], A.mult, "BOc BO", "BOc")
    lin(both(128, 0.5), T.Cm1[:], T.BO[:], C(15), 0.0, "BO col15", "Cm1")
    lin(both(128, 0.5), T.Cm0[:], T.BO[:], C(8), 0.0, "BO col8", "Cm0")
    lin(both(128, 0.5), T.nBO[:], T.BO[:], -1.0 / 16, 0.0, "BO", "nBO")
    fill(32, T.zer[:, 512:576], 255.0, "c255")
    fill(8, T.zer[:, 576:592], 0.0, "c255")
    ts(128, T.tri[:], T.rowj[:], C(1), -1.0, A.is_le, A.mult, "rowj col", "tri")
    ts(144, T.EE[:], T.row[:], C(7), None, A.is_equal, None, "row col7", "EE")
    tt(256, T.tri[:], T.tri[:], T.BO[:], A.mult, "tri BO", "tri")
    tt(256, T.tri[:], T.tri[:], T.idm[:], A.add, "tri idm", "tri")
    fill(25, T.L0[:], 0, "L0")
    fill(1, T.L0[:, 23:24], 96, "L0")
    fill(8, T.L0[:, 32:48], V + 8, "L0")
    for k, x in enumerate((T.nbi, T.pli, T.cst)):
        fill(16, x[:, V:V + 16], 0, "pad%d" % k)
    ts(8, T.offc[:], T.offc[:], C(9), None, A.add, None, "offc col9", "offc")
    fill(32, T.FZ[:], 0.0, "FZ")
    fill(96, T.Ms[:], BIG, "Ms")
    fill(96, T.tb[:], 0.0, "tb")
    fill(64, T.BAN[:, 0:96], 0.0, span("BAN_", 0, 6))
    fill(256, T.zer[:, 0:512], 0.0, "zer")
    fill(64, T.on12[:], 2.0 ** -12, "on12")
    fill(24, T.rrk[:], 1.0, "rrk")
    fill(3, T.rrk[:, 0:48:16], 0.0, "rrk")
    fill(64, T.r4[:], -4096.0, "r4")
    fill(16, T.r4[:, 0:64:4], 48.0, "r4")
    fill(32, T.dI[:], 0, "dI0 dI1")
    fill(32, T.gs[:], 0.0, "gs0 gs1 got0 got1")
    for k, sc in enumerate((576.0, 640.0, 704.0, 192.0, 256.0, 320.0, 255.0)):
        lin(both(128), T.idk[:, k, :], T.id32[:], sc, 0.0, "id32", "idk%d" % k)
    ts(28, T.rqb[:], T.rq[:], 1.0 / 16, 32 - 15.0 / 32, A.mult, A.add, "rq", "rqb")
    cp(1, C(10), T.thi[:, 0:1], "thi", "col10")

    def requests(t):
        cp(both(7), T.L0[:, 0:7], T.rq[:, 7 * t:7 * t + 7], "rq L0", "Ls0")
        cp(both(7), T.L0[:, 16:23], T.rqb[:, 7 * t:7 * t + 7], "rqb L0", "Lb0")
    requests(0)
    ts(1, C(13), C(10), 2048.0, 2.0 ** -17, A.is_ge, A.mult, "col10", "col13")
    lin(both(1), C(14), C(1), 2.0 ** -16, C(13), "col col13", "col14")
    lin(both(1), C(11), C(10), 2.0 ** -12, C(14), "col10 col14", "col11")
    lin(both(1), C(12), C(10), -1.0, 2048.0, "col10", "col12")
    lin(both(128), T.thM[:], T.id32[:], C(12), -16.0, "id32 col12", "thM")
    ts(128, T.tba[:], T.tba[:], C(1), None, A.is_equal, None, "tba tbb col", "tba")
    tt(128, T.tb[:, 32:96], T.tba[:, 0:64], T.tba[:, 64:128], A.add, "tba tb", "tb")
    for u in range(2):
        a, b = u * GH, u * GH + GH
        lin(both(GH), T.cst[:, a:b], T.pti[:, a:b], 2.0 ** -11, -0.25, "pti", "cst%d" % u)
        ts(GH, T.pli[:, a:b], T.pti[:, a:b], 2047, None, AND, None, "pti", "pli%d" % u)
    lin(both(64), T.mp[:], T.mp[:], 1.0, C(1), "mp col", "mp")
    lin(both(4), T.bc[:, 16:20], T.rowg[:, 0:4], 1.0, C(1), "rowg col", "rep")
    ts(64, T.sel[:], T.sel[:], C(0), None, A.is_equal, None, "sel col", "selb")
    mm(384, [(T.pY[:, 0:384], T.sel[:], T.tcf[:])], "selb tcf0 tcf1 tcf2 tcf3", "pY.a")
    ts(384, T.tc[:, 0:384], T.pY[:, 0:384], C(1), None, A.is_equal, None, "pY.a col", "tc")
    ts(192, T.tc[:, 384:768], T.tc[:, 0:384], C(16), None, A.max, None, "tc col16", "tc1")
    ts(256, T.ta[:, V + 16:V + 272], T.taf[:], C(1), None, A.is_equal, None, "taf col", "tao")
    WALL = "Wa Wb W1 W2 W3"

    def keep(d):
        if d == 0:
            dma("Y", T.S0[:, 0:V], T.W[:, 0:V], WALL, "Sx0")
        else:
            dma("Y", SR[d][:, 0:GH], T.W[:, V + (d - 1) * GH:V + d * GH], "W%d" % d, "Sx%d" % d)
    for u in range(2):
        cp(both(512, 0.5), T.AF[:, 32 * u:32 * u + 32, :], T.zer[:, 0:512], "zer", "AF0")
    for u in range(1, 4):
        dma("Y", T.AF[:, 64 * u:64 * u + 64, :], T.AF[:, 0:64, :], "AF0", "AF%d" % u, 1.5)
    for d in (1, 2, 3, 0):
        keep(d)
    for d in range(N):
        dma("Y", SR[d][:, V:2 * V], T.plans[:], "", "Sp%d" % d, 2 + 0.5 * d)
    for d in range(1, N):
        dma("Y", SR[d][:, GH:V], T.S0[:, V:V + GH], "Sp0", "Sz%d" % d, 3.5)

    TA = "ta taz "
    ta = T.ta[:, 0:V + 16]
    rep = T.bc[:, 16:19]

    def marks(t, NH, sl, bl, b0, sk, bk):
        L, n, AR, B = 128 * NH, 8 * NH, T["AR%d" % t], T["B%d" % t]
        a = 6 if t == 0 and NH == 2 else 0
        if a:
            cp(gath(16 * a), T.FB[:, 0:16 * a], T.tb[:].indirect(bl[:, b0:b0 + a]), "tb L0 Lb0", "FBa")
            cp(gath(16 * a), AR[:, 0:16 * a], ta.indirect(sl[:, 0:a]), TA + "L0 Ls0", "AR00")
        cp(gath(L - 16 * a), T.FB[:, 16 * a:L], T.tb[:].indirect(bl[:, b0 + a:b0 + n]), "tb " + bk, "FB" if a else "FB FBa")
        cp(gath(L - 16 * a), AR[:, 16 * a:L], ta.indirect(sl[:, a:n]), TA + sk, span("AR%d" % t, 0, NH))
        for h in range(NH):
            mm(512, [(T["pB%d" % h][:], part(T.FB, h), T.Rc[:])], "FB FBa Rc", "pB%d.a" % h)
            mm(128, [(part(T.pA, h), part(AR, h), (T.idb, T.idw)[h][:])], "idb idw AR%d%d" % (t, h), "pA.a%d" % h)
            relu(both(512), B[:, 512 * h:512 * h + 512], T["pB%d" % h][:], -1.0, "pB%d.a" % h, "B%d%d" % (t, h))
        lin(both(L), T.AW[:, 0:64 * NH:8, :], T.pA[:, 0:L], T.wcol[:, 0:1], 0.0, span("pA.a", 0, NH) + " wcol", span("AW", 0, NH))
        mm(64, [(T.pM[:, 0:64], T.idF[:], (T.FZ if t == 0 else T.MK)[:])], "idF " + ("FZ" if t == 0 else "MK"), "pM.w", True, False)
        for h in range(NH):
            mm(64, [(T.pM[:, 0:64], T.AW[:, 64 * h + 7 * k:64 * h + 7 * k + 8, :], B[:, 512 * h + 64 * k:512 * h + 64 * k + 64]) for k in range(8)],
               "AW%d B%d%d" % (h, t, h), "pM.w", False, h == NH - 1)
        cp(both(64), T.Ms[:, 32:96], T.pM[:, 0:64], "pM.w", "Ms")
        tt(gath(L, "V"), T.LK[:, 0:L], T.Ms[:].indirect(bl[:, b0:b0 + n]), AR[:, 0:L], A.mult, "Ms " + span("AR%d" % t, 0, NH) + " " + bk, "LK")
        if t == 0:
            add(P, both(64, 0.5), lambda q, e: q.tensor_scalar(T.MK[:], T.Ms[:, 32:96], 0.0, None, A.is_gt) if e == "V" else q.activation(T.MK[:], T.Ms[:, 32:96], F.Sign), "Ms", "MK")
        mm(16, [(T.pS[:, 0, 0, 0:n], T.EE[:, 15 - j:143 - j], T.LK[:, j:L:16]) for j in range(16)], "EE LK", "pS.a")
        tt(16, T.gs[:, 2 + t, 0:n], T.pS[:, 0, 0, 0:n], T.thr[:, 0:n], A.is_lt, "pS.a thr", "got%d" % t)

    def front(S, sk, cut, a, b, o=0):
        for c0, nb in cut:
            for v in range(2):
                c = c0 + nb * v
                lo, hi = max(a, c), min(b, c + nb)
                if lo < hi:
                    at = slice(16 * c0 + v + 32 * (lo - c), 16 * c0 + 32 * (hi - c), 2)
                    cp(gath(16 * (hi - lo)), T.Q[:, at], T.nbi[:].indirect(S[:, o + lo:o + hi]), "nbi pad0 " + sk, span("Q", lo, hi))
                    lin(gath(16 * (hi - lo)), T.CK[:, at], T.cst[:].indirect(S[:, o + lo:o + hi]), 2.0 ** -12, C(11), "cst0 cst1 pad2 col11 " + sk, span("CK", lo, hi))

    def chunk(t, h, c0, nb, ban):
        n, m, L = 2 * nb, 16 * nb, 32 * nb
        a, k0 = 16 * c0, c0 // 2
        pC = T["pC%d" % h]
        pX, kq = pC[:, 0:nb, :, :], pC[:, 8:8 + nb, :, :]
        half = lambda v: pC[:, 0:nb, :, v:16:2]
        K = lambda s: span(s, c0, c0 + n)
        X, KQ = "pC%d.x" % h, "pC%d.q" % h
        lin(both(L, 0.5), T.Qf[:, a:a + L], T.Q[:, a:a + L], 1.0, -1024.0, K("Q"), K("Qf"))
        mm(L, [(pX, T.thM[:], T.on12[:, 0:L])], "thM on12", X, True, False)
        for b in range(nb):
            k = k0 + b
            w = WIDE.get(P["at"], (1, 1, 1, 1))[b]
            if w:
                cp(gath(512 * w), T.G[:, 512 * k:512 * (k + w)], T.W[:].indirect(T.Q[:, 32 * k:32 * (k + w)]),
                   WALL + " " + span("Q", c0 + b, c0 + b + w) + " " + span("Q", c0 + nb + b, c0 + nb + b + w), span("G", k, k + w))
                big.append(len(P["ops"]) - 1)
                if len(big) > 2:
                    P["ops"][-1]["dep"].setdefault(big[-3], False)
            if b == nb - 1:
                mm(4 * L, [(pX, T.id32[:], T.CK[:, a:a + L])], "id32 " + K("CK"), X, False, False)
                if ban is not None:
                    mm(m, [(half(v), T.id4[:], T[ban][:, a + m * v:a + m * v + m]) for v in range(2)], "id4 " + K(ban + "_"), X, False, False)
            if b % 2 == 1:
                mm(64, [(pC[:, b - 1:b + 1, :, :], T.id12[:], T.G[:, 512 * (k - 1) + i:512 * (k + 1):16]) for i in range(16)], "id12 G%d G%d" % (k - 1, k), X, False, b == nb - 1)
            w = TURN.get(P["at"], (1, 1, 1, 1))[b]
            if w:
                turn(256 * w, T.GT[:, 512 * (k + 1 - w):512 * (k + 1)], T.G[:, 512 * (k + 1 - w):512 * (k + 1)], span("G", k + 1 - w, k + 1), span("GT", k + 1 - w, k + 1))
        tt(L, T.ov[:, a:a + L], pX, T.CK[:, a:a + L], A.is_gt, X + " " + K("CK"), K("ov"))
        for v in range(2):
            tt(m, T.kR[:, k0:k0 + nb, v, :], half(v), T.ov[:, a + v:a + L:2], A.add, X + " " + K("ov"), span("kR%d_" % v, k0, k0 + nb))
        mm([L, m, m, m, m], [(kq, T.BOc[:], T.ta[:, 0:L])] + [(pC[:, 8:8 + nb, e, :], T.SWs[:, 2 * e + v, :], T.Qf[:, a + v:a + L:2]) for e in range(2) for v in range(2)],
           "BOc ta SWs " + K("Qf"), KQ)
        cp(both(L), T.kq[:, a:a + L], kq, KQ, K("kq"))
        turn(L, T.kT[:, a:a + L], T.kR[:, k0:k0 + nb, :, :], span("kR0_", k0, k0 + nb) + " " + span("kR1_", k0, k0 + nb), K("kT"))
        scan(L, T.km[:, a:a + L], T.rmin[:, 0:L], T.kT[:, a:a + L], 0.0, A.add, A.min, "rmin " + K("kT"), K("km"))
        cs = slice(c0, c0 + n)
        lin(both(n), T.ki[:, 0, cs], T.km[:, a + 15:a + L:16], 2.0 ** 17, 0.0, K("km"), K("ki"))
        ts(n, T.ki[:, 1, cs], T.ki[:, 0, cs], 1, 15, SHR, AND, K("ki"), K("ci"))
        tt(n, T.off[:, cs], T.ki[:, 1, cs], T.offc[:, 0:n], A.add, "offc " + K("ci"), K("off"))
        tt(gath(L, "V"), T.K1[:, a:a + L], T.GT[:, 16 * a:16 * (a + L)].indirect(T.off[:, cs]), T.kq[:, a:a + L], A.add, span("GT", k0, k0 + nb) + " " + K("off") + " " + K("kq"), K("K1_"))
        turn(L, T.K1T[:, a:a + L], T.K1[:, a:a + L], K("K1_"), K("K1T"))
        scan(L, T.bm[:, a:a + L], T.rmax[:, 0:L], T.K1T[:, a:a + L], 0.0, A.add, A.max, "rmax " + K("K1T"), K("bm"))
        if t == 0:
            for v in range(2):
                lin(both(nb), T.bi[:, c0 + nb * v:c0 + nb * v + nb], T.bm[:, a + 16 * v + 15:a + L:32], 65536.0, 0.0, K("bm"), span("bi", c0 + nb * v, c0 + nb * v + nb))
            ts(n, T.zi[:, 0, cs], T.bi[:, cs], 4095, None, AND, None, K("bi"), K("b0_"))
            ts(n, T.s1[:, cs], T.zi[:, 0, cs], -512.0, 1024.0, A.add, A.min, K("b0_"), K("s1_"))

    def chosen(t, n, S, sk):
        L, OH = 16 * n, T["OH%d" % t]
        cp(both(n), T.CS[:, 0, 0:n], T.ki[:, 1, 0:n], span("ci", 0, n), "CS")
        ts(n, T.zi[:, 4, 0:n], T.ki[:, 0, 0:n], 1, None, AND, None, span("ki", 0, n), "hh")
        lin(both(n), Z(2, n), T.zi[:, 4, 0:n], 65536.0, 131071.0, "hh", "ht")
        tt(n, T.CS[:, 1, 0:n], T.ki[:, 0, 0:n], Z(2, n), A.is_gt, span("ki", 0, n) + " ht", "CSs")
        for c0, nb in CUT[n]:
            for v in range(2):
                mm(n, [(T.pS[:, 12:14, 0, c0 + nb * v:c0 + nb * v + nb], T.SWb[:, 2 * v + e, :], T.CS[:, :, c0 + e:c0 + 2 * nb:2]) for e in range(2)], "SWs CS CSs", "pS.b")
        cp(both(n), T.cl[:, t, 0:n], T.pS[:, 12, 0, 0:n], "pS.b", "cl%d" % t)
        cp(gath(L), OH[:, 0:L], ta.indirect(T.cl[:, t, 0:n]), TA + "cl%d" % t, span("OH%d_" % t, 0, n))
        tt(n, T.gs[:, t, 0:n], T.pS[:, 13, 0, 0:n], T.gs[:, 2 + t, 0:n], A.mult, "pS.b got%d" % t, "gs%d" % t)
        tt(gath(L, "V"), T["PL%d" % t][:, 0:L], T.pli[:].indirect(S[:, 0:n]), OH[:, 0:L], A.mult, "pli0 pli1 pad1 " + span("OH%d_" % t, 0, n) + " " + sk, "PL%d" % t)

    front(T.L0, "L0 Ls0", CUT[8], 0, 8)
    for rnd in range(RO):
        n = 8 if rnd == 0 else 16
        L, NH = 16 * n, n // 8
        last = rnd == RO - 1
        LS, LB, S1 = "L0 Ls0 Ls1", "L0 Lb0 Lb1", span("s1_", 0, n)
        P["at"], P["sites"] = "r%d m0" % NH, {}
        marks(0, NH, T.L0, T.L0, 16, LS, LB)
        for h, (c0, nb) in enumerate(CUT[n]):
            P["at"] = "r%d s0%d" % (NH, h)
            chunk(0, h, c0, nb, "BAN" if rnd > 0 else None)
            front(T.s1, span("s1_", c0, c0 + 2 * nb), CUT[n], c0, c0 + 2 * nb)
        P["at"] = "r%d m1" % NH
        chosen(0, n, T.L0, LS)
        tt(n, T.zi[:, 2, 0:n], T.gs[:, 0, 0:n], T.zi[:, 0, 0:n], A.mult, "gs0 " + span("b0_", 0, n), "bg0")
        lin(both(n), T.b1[:, 0:n], T.zi[:, 2, 0:n], 1.0 / 16, -15.0 / 32, "bg0", "bl1")
        lin(both(n), T.dI[:, 0, 0:n], T.zi[:, 2, 0:n], 1.0 / 512, -511.0 / 1024, "bg0", "dI0")
        tt(gath(48, "V"), T.ff[:, 0, :], T.dI[:, 0, :].indirect(rep), T.dc[:], A.is_equal, "dI0 rep dc", "ff0")
        scan(24, T.inc[:, 0, :], T.rrk[:], T.ff[:, 0, :], 0.0, A.mult, A.add, "rrk ff0", "inc0")
        marks(1, NH, T.s1, T.b1, 0, S1, "bl1")
        for h, (c0, nb) in enumerate(CUT[n]):
            P["at"] = "r%d s1%d" % (NH, h)
            chunk(1, h, c0, nb, "OH0")
        P["at"] = "r%d end" % NH
        bj = T.bj[:, 0:NH, :, :]
        for v in range(2):
            lin(both(n // 2), T.bj[:, 0:NH, v, :], T.bm[:, 16 * v + 15:L:32], 65536.0, 0.0, span("bm", 0, n), "bj%d" % v)
        chosen(1, n, T.s1, S1)
        YB, YK = (T.pY, T.pB0), ("pY.a", "pB0.a")
        for h in range(NH):
            mm([256, 128, 128], [(YB[h][:, 0:256], T.idb[:], T.zer[:, 0:256])] + [(part(YB[h], t), part(T["AR%d" % t], h), T.idB[:]) for t in range(2)],
               "idb zer idB AR0%d AR1%d" % (h, h), YK[h], True, False)
            for t in range(2):
                mm(128, [(part(YB[h], t), part(T["PL%d" % t], h), T.BO[:])], "BO PL%d" % t, YK[h], False, False)
        tt(gath(48, "V"), T.DC[:], T.gs[:, 1, :].indirect(rep), T.dc[:], A.mult, "gs1 rep dc", "DC")
        ts(n, T.dI[:, 1, 0:n], bj, 9, 7, SHR, AND, "bj0 bj1", "dI1")
        tt(gath(48, "V"), T.ff[:, 1, :], T.dI[:, 1, :].indirect(rep), T.DC[:], A.is_equal, "dI1 rep DC", "ff1")
        scan(24, T.inc[:, 1, :], T.rrk[:], T.ff[:, 1, :], 0.0, A.mult, A.add, "rrk ff1", "inc1")
        mm(80, [(T.pM[:, 64:144], T.idb[:], T.zer[:, 512:592])], "idb c255", "pM.r", True, False)
        for t in range(2):
            mm(16, [(T.pM[:, 67:128:4], T.idm[:], T.gs[:, 2 + t, :]), (T.pM[:, 67:128:4], T.idk[:, 6, :], T.gs[:, t, :])], "idm idk6 got%d gs%d" % (t, t), "pM.r", False, False)
            if not last:
                mm(16, [(T.pM[:, 128:144], T.idk[:, 3 * t + d, :], T.ff[:, t, 16 * d:16 * d + 16]) for d in range(3)], span("idk", 3 * t, 3 * t + 3) + " ff%d" % t, "pM.r", False, False)
            for x, y, k in ((T.tri, T.ff, "ff"), (T.BO, T.inc, "inc")):
                mm(16, [(T.pM[:, 64 + d:128:4], x[:], y[:, t, 16 * d:16 * d + 16]) for d in range(3)], "tri BO %s%d" % (k, t), "pM.r", False, t == 1 and k == "inc")
        scan(64, T.fr[:], T.r4[:], T.pM[:, 64:128], 48.0, A.max, A.min, "r4 pM.r", "fr")
        if last:
            cp(both(n), T.SL[:, 0:n], T.fr[:, 3:4 * n:4], "fr", "SL")
        else:
            tt(n, T.SL[:, 0:n], T.pM[:, 128:128 + n], T.fr[:, 3:4 * n:4], A.add, "pM.r fr", "SL")
        for h in range(NH):
            cp(gath(128), part(T.AO, h), T.tc[:].indirect(T.SL[:, 8 * h:8 * h + 8]), "tc tc1 SL", "AO%d" % h)
            mm(128, [(part(YB[h], t), part(T.AO, h), T.BOK[:]) for t in range(2)], "BOK AO%d" % h, YK[h], False, True)
        if not last:
            ts(n, T.zi[:, 1, 0:n], bj, 4095, None, AND, None, "bj0 bj1", "b1")
            tt(n, Z(11, n), T.gs[:, 1, 0:n], T.zi[:, 1, 0:n], A.mult, "gs1 b1", "bg1")
            tt(n, T.zi[:, 3, 0:n], T.zi[:, 2, 0:n], Z(11, n), A.max, "bg0 bg1", "bI")
            ts(n, T.XI[:, 0:n], T.zi[:, 3, 0:n], 511, None, AND, None, "bI", "XI")
            cp(both(n), T.bc[:, 20:20 + n], T.XI[:, 0:n], "XI", "XU")
            cp(gath(L), T.DX[:, 0:L], T.tx[:].indirect(T.bc[:, 20:20 + n]), "tx XU", "DX")
            mm([2 * L] + [128] * (2 * NH), [(T.pS[:, 0:n, :, :], T.idb[:], T.zer[:, 0:2 * L])] +
               [(T.pS[:, 8 * h:8 * h + 8, 1, :], part(x, h), y[:]) for h in range(NH) for x, y in ((T.OH0, T.Cm0), (T.OH1, T.Cm1))],
               "idb zer Cm0 Cm1 " + span("OH0_", 0, n) + " " + span("OH1_", 0, n), "pS.a pS.b", True, False)
            mm(128, [(T.pS[:, 8 * h:8 * h + 8, 0, :], part(T.DX, h), T.nBO[:]) for h in range(NH)], "nBO DX", "pS.a pS.b", False, False)
            mm(256, [(T.pS[:, 8 * h:8 * h + 8, :, :], part(T.AO, h), T.RX[:]) for h in range(NH)], "RX " + span("AO", 0, NH), "pS.a pS.b", False, True)
            for h in range(NH):
                mm(128, [(part(T.pA, h), part(T.AO, h), T.RA[:])], "RA AO%d" % h, "pA.a%d" % h)
            relu(both(L), T.AW[:, 0:64 * NH:8, :], T.pA[:, 0:L], -1.0, span("pA.a", 0, NH), span("AW", 0, NH))
        for h in range(NH):
            relu(both(256), T.AF[:, 128 * h:128 * h + 128:8, :], YB[h][:, 0:256], 1024.0 - 32768.0 - 4096.0, YK[h], "AF%d AF%d" % (2 * h, 2 * h + 1))
            mm(64, [(T.pM[:, 160:224], T.AF[:, 128 * h + 64 * t + 7 * k:128 * h + 64 * t + 7 * k + 8, :], T["B%d" % t][:, 512 * h + 64 * k:512 * h + 64 * k + 64])
                    for t in range(2) for k in range(8)], "AF%d AF%d B0%d B1%d" % (2 * h, 2 * h + 1, h, h), "pM.m", h == 0, h == NH - 1)
        if not last:
            relu(both(2 * L), T.X[:, 0:2 * L], T.pS[:, 0:n, :, :], 1024.0 - 65536.0, "pS.a pS.b", "X")
            mm(32, [(T.pA[:, 256:288], T.AW[:, 64 * h + 7 * k:64 * h + 7 * k + 8, :], T.X[:, 256 * h + 32 * k:256 * h + 32 * k + 32])
                    for h in range(NH) for k in range(8)], "AW0 AW1 X", "pA.o")
        tt(32, T.MSG[:, rnd, 0:32], T.pM[:, 160:192], T.mp[:, 0:32], A.max, "pM.m mp", "MSG0")
        tt(32, T.mp16[:], T.pM[:, 192:224], T.mp[:, 32:64], A.max, "pM.m mp", "mp16")
        if not last:
            cp(both(32), T.MSG[:, rnd, 32:64], T.pA[:, 256:288], "pA.o", "MSG1")
            per = len(chip) // len(far)
            for u in range(2):
                piece = lambda x, k, o: x[:, k, o + 32 * u:o + 32 * u + 32]
                ls[0] += remote([(h, chip[i * per:(i + 1) * per], "hm%d" % (2 * rnd + u), piece(T.MSG, rnd, 0), piece(T.HM, rnd, 0)) for i, h in enumerate(close)],
                                "ls", "MSG%d" % u, "msg%d" % u)
                for q in near:
                    d = (rank - q) % N
                    j = 3 * rnd + d - 1
                    ls[0] += remote([(T.cores[q], out_e, "m%d" % (2 * j + u), piece(T.MSG, rnd, 0), piece(T.IN, j, 12 - 4 * d))], "ls", "MSG%d" % u, "msg%d" % u)
                for d in range(1, N):
                    j = 3 * rnd + d - 1
                    lands("m%d" % (2 * j + u), len(out_e), "msg%d" % u, ("IM%d", "IN%d")[u] % j, NEAR1 if (rank + d) % N in near else FAR1)
        P["at"] = "last" if last else "front"
        cp(gath(GH), T.W[:, 0:GH], T.S0[:].indirect(T.MSG[:, rnd, 0:32]), "Sp0 Sx0 MSG0 sent", "Wa")
        cp(gath(GH), T.W[:, GH:V], T.S0[:].indirect(T.mp16[:]), "Sp0 Sx0 mp16", "Wb")
        if last:
            dma("S", T.y[:, 0:GH], T.W[:, 0:GH], "Wa", "ya")
            dma("Y", T.y[:, GH:V], T.W[:, GH:V], "Wb", "yb")
            break
        tt(64, T.FZ[:], T.pM[:, 160:224], T.MK[:], A.is_lt, "pM.m MK", "FZ")
        requests(rnd + 1)
        front(T.L0, "L0 Ls0", CUT[16], 0, 7)
        j0 = 3 * rnd
        INS = span("IN", j0, j0 + 3)
        for d in range(1, N):
            at, m, j = V + (N - d - 1) * GH, 12 - 4 * d, j0 + d - 1
            cp(gath(GH), T.W[:, at:at + GH], SR[N - d][:].indirect(T.IN[:, j, m:m + 32]), "Sz%d Sp%d Sx%d IM%d" % (N - d, N - d, N - d, j), "W%d" % (N - d))
        for d in (2, 1, 3, 0):
            if d == 0 or rnd < RO - 2:
                keep(d)
        lin(both(9), T.L0[:, 7:16], T.IN[:, j0:j0 + 3, 40:43], -1.0, 1024.0, "L0 " + INS, "Ls1")
        cp(both(9), T.L0[:, 39:48], T.IN[:, j0:j0 + 3, 56:59], "L0 " + INS, "Lc1")
        lin(both(1), T.L0[:, 48:49], T.IN[:, j0, 40:41], -1.0, 1024.0, "L0 IN%d" % j0, "Ls2")
        front(T.L0, "Ls2", CUT[16], 7, 8, 41)
        front(T.L0, LS, CUT[16], 8, 16)
        cp(gath(160), T.BAN[:, 96:256], T.ta[:].indirect(T.L0[:, 38:48]), TA + "tao L0 Lc1", span("BAN_", 6, 16))
        lin(both(9), T.L0[:, 23:32], T.L0[:, 7:16], 1.0 / 16, 32 - 15.0 / 32, LS, "Lb1")

    issue(P, eng, T)
    g.wait_ge(T.sem.ls, ls[0])
